import numpy as np, ml_dtypes
CORES = [24,25,26,27,28,29,30,31]
N = 8
import mx_ref
BF = ml_dtypes.bfloat16
def cols(t, e):
    v = np.concatenate([t.reshape(128, -1, 4), np.zeros((128, 1, 4), BF)], axis=1)
    return np.ascontiguousarray(v[:, e]).reshape(128, -1)
def pick(q, e):
    c = np.concatenate([q[0].reshape(128, -1, 4), np.zeros((128, 1, 4), np.uint8)], axis=1); s = np.concatenate([q[1], np.ones((16, 1), np.uint8)], axis=1)
    return (np.ascontiguousarray(c[:, e].reshape(128, -1)), np.ascontiguousarray(s[:, e]))
def join(*qs):
    return (np.concatenate([q[0] for q in qs], axis=1), np.concatenate([q[1] for q in qs], axis=1))
def put(q, e, v):
    c, s = q[0].reshape(128, -1, 4).copy(), q[1].copy(); c[:, e] = v[0].reshape(128, -1, 4); s[:, e] = v[1]
    return (c.reshape(128, -1), s)
def pk(c, s):
    return (np.ascontiguousarray(c), mx_ref.live(s))
def emit(q):
    return q[0], q[1]
def decode(q):
    o = []
    for b in range(4):
        e = np.zeros((128, 128, 4), np.float32); e[np.arange(128), np.arange(128), b] = 1
        o.append(mx_ref.matmul(mx_ref.quantize(e.reshape(128, 512).astype(BF)), q))
    return np.stack(o, axis=2).reshape(128, -1)
def f(rng, *shape):
    return mx_ref.flush((rng.standard_normal(shape, dtype=np.float32) * np.exp2(rng.integers(-2, 3, shape[:-1] + (1,)))).astype(BF))
def wide(rng, *shape, cols=0):
    v = rng.standard_normal(shape, dtype=np.float32) * np.exp2(rng.integers(-12, 13, shape)).astype(np.float32)
    if cols: v *= np.repeat(np.exp2(rng.integers(-cols, cols + 1, shape[:-2] + (1, shape[-1] // 4))) * (rng.random(shape[:-2] + (1, shape[-1] // 4)) > 0.0625), 4, axis=-1).astype(np.float32)
    return mx_ref.flush(v.astype(BF))
P, K, O = 256, 64, 1
def big(v):
    v = np.array(v.astype(np.float32))
    v[np.abs(v) < np.float32(2.0 ** -16)] = 0
    return v.astype(BF)
def sized(t, a):
    return big(t.astype(np.float32) * np.repeat(np.asarray(a, np.float32), 4, axis=-1))
def query(rng):
    v = np.zeros((N, 128, 512), BF)
    v[:, :, :4] = f(rng, 1, 128, 4)
    return v
def plain(rng):
    return {"lv": big(f(rng, N, 128, 4 * P)), "dm": big(f(rng, N, 128, 4 * P)), "nz": big(f(rng, N, 128, 4 * P)), "u": query(rng), "z": query(rng), "w": f(rng, N, 128, 512 * O)}
def positive(d):
    return {k: v if k == "w" else np.abs(v.astype(np.float32)).astype(BF) for k, v in d.items()}
def onto(t, e, rng):
    at, far = np.arange(N * P), e[e >= P]
    free = rng.permutation(np.setdiff1d(np.arange(P), e))[:far.size]
    at[free], at[far] = far, free
    return np.stack(np.split(cols(np.concatenate(t, axis=1), at), N, axis=1))
def setup_inputs(rng):
    return plain(rng)
def setup_inputs_ties(rng):
    d = plain(rng)
    for k in ("lv", "dm", "nz"):
        v = big((1 + rng.random((128, 48))) * 2.0 ** 27)
        d[k] = np.stack([big(cols(v, rng.permutation(np.arange(P) % 12)).astype(np.float32) * np.repeat(1 - 2 * rng.integers(0, 2, P), 4)) for r in range(N)])
    for k in ("u", "z"): d[k][:, :, :4] = big((1 + rng.random((1, 128, 4))) * 2.0 ** 29)
    return d
def setup_inputs_one(rng):
    d = positive(plain(rng))
    a, b = rng.permutation(N)[:2]
    g, h = np.ones((N, P)), np.ones((N, P))
    g[a, rng.permutation(P)[:K]] = 2.0 ** -8
    g[b, rng.permutation(P)[:K]] = 2.0 ** -4
    h[b, rng.permutation(P)[:K]] = 2.0 ** 8
    h[a, rng.permutation(P)[:K]] = 2.0 ** 4
    d["lv"], d["dm"] = sized(d["lv"], g[:, None]), sized(d["dm"], h[:, None])
    return d
def setup_inputs_again(rng):
    d = positive(plain(rng))
    n, top = K // N, (np.arange(128) < 64)[None, :, None]
    lt, lb, dt, db, nt = np.ones((5, N, P))
    for r in range(N):
        at, to = rng.permutation(P), rng.permutation(P)
        lt[r, at[:n]], lt[r, at[n:2 * n]] = 2.0 ** -6, 2.0 ** -3
        lb[r, at[:n:2]] = 2.0 ** 8
        nt[r, at[:n // 2]], nt[r, at[n // 2:n]] = 2.0 ** -8, 2.0 ** 4
        dt[r, to[:n]] = 2.0 ** -8
        db[r, to[:n]], db[r, to[n:2 * n]] = 2.0 ** 6, 2.0 ** 3
    d["lv"] = sized(d["lv"], np.where(top, lt[:, None], lb[:, None]))
    d["dm"] = sized(d["dm"], np.where(top, dt[:, None], db[:, None]))
    d["nz"] = sized(d["nz"], np.where(top, nt[:, None], 1.0))
    d["u"], d["z"] = big(d["u"].astype(np.float32) * top), big(d["z"].astype(np.float32) * ~top)
    return d
def setup_inputs_zero(rng):
    d = plain(rng)
    g, h, e = np.ones((3, N, P))
    for r in range(N):
        g[r, rng.permutation(P)[:3 * K // (2 * N)]] = 0
        h[r, rng.permutation(P)[K // (2 * N):]] = 0
        e[r, rng.permutation(P)[:P // 2]] = 0
    d["lv"], d["dm"], d["nz"] = sized(d["lv"], g[:, None]), sized(d["dm"], h[:, None]), sized(d["nz"], e[:, None])
    return d
def setup_inputs_spread(rng):
    d = plain(rng)
    d["lv"] = sized(wide(rng, N, 128, 4 * P), 32 * np.exp2(rng.integers(-6, 7, (N, 1, P))))
    for k in ("dm", "nz"): d[k] = sized(wide(rng, N, 128, 4 * P, cols=6), np.full((1, 1, P), 32.0))
    for k in ("u", "z"): d[k] = sized(d[k], np.full((1, 1, 128), 2.0 ** 24))
    low = np.concatenate([score(d["u"][r], mx_ref.quantize(np.ascontiguousarray(d["lv"][r]))) for r in range(N)])
    high = np.concatenate([score(d["z"][r], mx_ref.quantize(np.ascontiguousarray(d["dm"][r]))) for r in range(N)])
    d["lv"] = onto(d["lv"], np.argsort(low, kind="stable")[:K], rng)
    d["dm"] = onto(d["dm"], np.argsort(-high, kind="stable")[:K], rng)
    return d
def check_inputs(d):
    b = []
    for k, lo, hi in (("lv", -16, 28), ("dm", -16, 28), ("nz", -16, 28), ("u", -30, 30), ("z", -30, 30), ("w", -30, 30)):
        v = np.abs(d[k].astype(np.float32))
        if not (np.isfinite(v).all() and ((v == 0) | (v >= 2.0 ** lo) & (v <= 2.0 ** hi)).all()): b.append("a value of " + k)
    for k in ("u", "z"):
        v = d[k].astype(np.float32)
        if (v[:, :, 4:] != 0).any(): b.append(k + " has numbers behind its column 0")
        if (v != v[:1]).any(): b.append(k + " isn't the same on all ranks")
    return b
def score(t, q):
    return np.abs(mx_ref.matmul(mx_ref.quantize(np.ascontiguousarray(t)), q)[0]) + np.float32(0)
def reference(lv, dm, nz, u, z, w):
    L = [mx_ref.quantize(np.ascontiguousarray(lv[r])) for r in range(N)]
    X = [mx_ref.quantize(np.ascontiguousarray(dm[r])) for r in range(N)]
    noise = join(*[mx_ref.quantize(np.ascontiguousarray(nz[r])) for r in range(N)])
    oc, osc = np.zeros((N, 128, 8 * P), np.uint8), np.zeros((N, 16, 2 * P), np.uint8)
    sw, lw, y = np.zeros((N, 2, K), np.float32), np.zeros((N, 2, K), np.float32), np.zeros((N, 128, O * P), np.float32)
    for t in range(2):
        low = np.argsort(np.concatenate([score(u[r], L[r]) for r in range(N)]), kind="stable")[:K]
        high = np.argsort(-np.concatenate([score(z[r], X[r]) for r in range(N)]), kind="stable")[:K]
        lw[:, t], sw[:, t] = low, high
        gone, come = pick(join(*L), low), pick(join(*X), high)
        v = decode(come) * np.float32(0.5) + decode(pick(noise, low)) * np.float32(0.5)
        new = mx_ref.quantize(np.ascontiguousarray(v.astype(BF)))
        for r in range(N):
            a, b = np.flatnonzero(low // P == r), np.flatnonzero(high // P == r)
            L[r] = put(L[r], low[a] - P * r, pick(new, a))
            X[r] = put(X[r], high[b] - P * r, pick(gone, b))
    for r in range(N):
        oc[r], osc[r] = emit(join(L[r], X[r]))
        for o in range(O):
            y[r, :, P * o:P * o + P] = mx_ref.matmul(mx_ref.quantize(np.ascontiguousarray(w[r][:, 512 * o:512 * o + 512])), L[r])
    return {"oc": oc, "osc": osc, "sw": sw, "lw": lw, "y": y}

@@ -1,0 +1,618 @@
+from concourse.bass import DstId, RemoteDMATransfer
+from concourse.mybir import dt, AluOpType, AxisListType, ActivationFunctionType as AF
+
+N, P, K = 8, 256, 64
+PEERS = N - 1
+HS = K // N
+
+SCRATCH, VIEW = {}, {}
+SEMAPHORES = ["qv", "qs", "qt", "qg", "ls", "ak1", "ak2", "ai1", "ai2", "azc", "azs", "ahc", "ahs", "awc", "aws", "anum"] + ["d%d" % i for i in range(48)]
+
+
+def _sb(name, w, d):
+    SCRATCH[name] = ("sbuf", [128, w], d)
+    VIEW[name] = (name, 0, w)
+
+
+def _codes(name, w):
+    _sb(name, w, "float8_e4m3fn_x4")
+    _sb(name + "s", w, "uint8")
+
+
+def _pool(name, d, parts):
+    at = 0
+    for n, w in parts:
+        VIEW[n] = (name, at, w)
+        at += (w + 15) // 16 * 16
+    SCRATCH[name] = ("sbuf", [128, at], d)
+
+
+for _n, _w in (("TL", 1024), ("TX", 1024), ("TN", 1024), ("TW", 512), ("U4", 4), ("Z4", 4), ("UT", 1280), ("ONE", 128),
+               ("ZB", 128), ("CO", 512), ("WT", 2816), ("ET", 2048), ("EYE", 128), ("CT", 1024), ("OT", 768), ("HT", 512),
+               ("MSK", 256), ("DS", 512)):
+    _sb(_n, _w, "bfloat16")
+_pool("BB", "bfloat16", (("EQK", 256), ("MM", 448), ("EQ", 256), ("EQN", 64)))
+_pool("FC", "float32", (("CC", 16), ("IROW", 64), ("N16", 64), ("M16", 64), ("RB", 256), ("BDN", 1), ("BDP", 1), ("CROW", 4), ("KC", 4), ("CW8", 8),
+                        ("HALF", 1), ("WA", 1), ("WC", 1), ("VX", 1), ("IC", 2), ("SGN", 32), ("DCOL", 1), ("BROW", 1)))
+_pool("FD", "float32", (("AC", 4), ("RLA", 256), ("RXA", 256)))
+_pool("FB", "float32", (("PRD", 256), ("JK", 768), ("PM", 64), ("P8", 4), ("K1S", 1), ("OKC", 2), ("D0", 64),
+                        ("KR", 224), ("KW", 224), ("XC", 2), ("XR", 64), ("Y", 64), ("TY", 64), ("GS", 64), ("MU", 256), ("FS", 4),
+                        ("SW", 4), ("FLD", 8), ("FM", 4), ("FO", 8), ("FP", 8), ("VT", 64), ("VM", 64), ("VU", 64), ("VV", 64), ("PN", 64),
+                        ("NA", 2), ("NB", 2), ("V28", 28), ("W5", 4), ("W6", 4), ("AB", 8), ("V8", 8), ("VS", 1), ("HL8", 8)))
+for _n, _w in (("NUM", 2), ("NL", 14), ("RES", 4), ("YO", 256)):
+    _sb(_n, _w, "float32")
+for _t in "12":
+    for _n, _w in (("K1_", 1), ("KL", 7), ("ROW", 256), ("LST", 32)):
+        _sb(_n + _t, _w, "float32")
+    for _n, _w in (("INFO", 4), ("IL", 28)):
+        _sb(_n + _t, _w, "uint16")
+    _pool("UB" + _t, "uint16", tuple((_n + _t, _w) for _n, _w in (("PIU", 4), ("ZU", 4), ("NU", 4), ("LAB", 8), ("PLU", 32), ("HLU", 8))))
+    _codes("Z" + _t, K)
+    _codes("LXV" + _t, 2 * P + K + 128)
+    _codes("B" + _t, 128)
+    _codes("N" + _t, 128)
+_sb("PI", 1, "int32")
+_sb("II", 5, "int32")
+for _n, _w in (("UQ", 320), ("LX1", 512), ("LX2", 512), ("LX3", 512), ("NQ", 256), ("WQ", 128), ("COQ", 128), ("WTQ", 704), ("EC", 512),
+               ("CQ", 256), ("OQ", 192), ("WIN1", N * K + 2 * P), ("WIN2", K + 128 + 2 * P), ("HW", 32 + K)):
+    _codes(_n, _w)
+PSUM = {"pA": 1, "pB": 1, "pC": 1, "pD": 4, "pE": 1}
+for _n in PSUM:
+    SCRATCH[_n] = ("psum", [128, 512 * PSUM[_n]], "float32")
+    VIEW[_n] = (_n, 0, 512 * PSUM[_n])
+
+ADD, SUB, MUL, MAX, MIN = AluOpType.add, AluOpType.subtract, AluOpType.mult, AluOpType.max, AluOpType.min
+GT, GE, LT, LE, EQL = AluOpType.is_gt, AluOpType.is_ge, AluOpType.is_lt, AluOpType.is_le, AluOpType.is_equal
+
+
+def R(name, c0=0, c1=None, p0=0, p1=128, step=1):
+    buf, at, width = VIEW[name]
+    return (buf, at + c0, at + (width if c1 is None else c1), p0, p1, step)
+
+
+def overlap(a, b):
+    if a[4] <= b[3] or b[4] <= a[3] or a[2] <= b[1] or b[2] <= a[1]:
+        return False
+    return not (a[5] == b[5] and a[5] > 1 and (a[1] - b[1]) % a[5])
+
+
+def covers(a, b):
+    return a[5] == 1 and a[1] <= b[1] and a[2] >= b[2] and a[3] <= b[3] and a[4] >= b[4]
+
+
+def bank(r):
+    return (r[0], r[1] // 512 * 512, (r[2] + 511) // 512 * 512, 0, 128, 1) if r[0] in PSUM else r
+
+
+def rank_program(g, core, T, topo):
+    rank = T.rank_of(core)
+    if rank is None:
+        return
+    peers = [r for r in range(N) if r != rank]
+    queues = {"v": g.vector, "s": g.scalar, "t": g.tensor, "g": g, "y": g.sync}
+    hist, known, count, total = {}, {q: {} for q in queues}, {q: 0 for q in queues}, {}
+    seq, ndma = [0], [0]
+
+    def waits(q, reads, writes, adds=False):
+        need = []
+        for r in reads:
+            b, ps = bank(r), r[0] in PSUM
+            for kind, box, tok in hist.get(r[0], []):
+                if overlap(b, box) and (kind == "w" or ps and tok[2] != q):
+                    need.append(tok)
+        for w in writes:
+            b = bank(w)
+            for kind, box, tok in hist.get(w[0], []):
+                if overlap(b, box) and not (adds and tok[2] == q):
+                    need.append(tok)
+        for tok in sorted(need, key=lambda k: -k[3]):
+            if known[q].get(tok[0], 0) < tok[1]:
+                queues[q].wait_ge(T.sem[tok[0]], tok[1])
+                known[q][tok[0]] = tok[1]
+                for s, n in tok[4].items():
+                    known[q][s] = max(known[q].get(s, 0), n)
+
+    def note(q, reads, writes, sem, val):
+        seq[0] += 1
+        tok = (sem, val, q, seq[0], dict(known[q]) if q in known else {})
+        for w in writes:
+            b = bank(w)
+            hist[w[0]] = [h for h in hist.get(w[0], []) if not covers(b, h[1])] + [("w", b, tok)]
+        for r in reads:
+            hist.setdefault(r[0], []).append(("r", bank(r), tok))
+
+    def run(q, make, reads, writes, adds=False):
+        waits(q, reads, writes, adds)
+        count[q] += 1
+        make().then_inc(T.sem["q" + q], 1)
+        total["q" + q] = count[q]
+        note(q, reads, writes, "q" + q, count[q])
+
+    def A(r):
+        t = T[r[0]]
+        rows = slice(None) if (r[3], r[4]) == (0, 128) else slice(r[3], r[4])
+        return t[rows, r[1]:r[2]] if r[5] == 1 else t[rows, r[1]:r[2]:r[5]]
+
+    def S8(r):
+        return A(r).bitcast(dt.uint8) if SCRATCH[r[0]][2] == "float8_e4m3fn_x4" else A(r)
+
+    def dma(q, out, in_, outap=None, inap=None):
+        reads, writes = [in_] if in_ else [], [out] if out else []
+        waits(q, reads, writes)
+        sem = "d%d" % ndma[0]
+        ndma[0] += 1
+        queues[q].dma_start(outap if outap is not None else S8(out), inap if inap is not None else S8(in_)).then_inc(T.sem[sem], 16)
+        total[sem] = 16
+        note(q, reads, writes, sem, 16)
+
+    def dmaq(q, out, c, in_, d, n):
+        dma(q, R(out, c, c + n), R(in_, d, d + n))
+        dma(q, R(out + "s", c, c + n), R(in_ + "s", d, d + n))
+
+    def memset(r, v):
+        run("v", lambda: g.vector.memset(A(r), v), [], [r])
+
+    def copy(q, out, in_):
+        if q == "v":
+            run("v", lambda: g.vector.tensor_copy(A(out), A(in_)), [in_], [out])
+        else:
+            run("s", lambda: g.scalar.activation(A(out), A(in_), AF.Copy), [in_], [out])
+
+    def tt(out, a, b, op):
+        run("v", lambda: g.vector.tensor_tensor(A(out), A(a), A(b), op), [a, b], [out])
+
+    def ts(out, a, s1, op0, s2=None, op1=None):
+        reads = [a] + [s for s in (s1, s2) if isinstance(s, tuple)]
+        v1 = A(s1) if isinstance(s1, tuple) else s1
+        v2 = A(s2) if isinstance(s2, tuple) else s2
+        if op1 is None:
+            run("v", lambda: g.vector.tensor_scalar(A(out), A(a), v1, None, op0), reads, [out])
+        else:
+            run("v", lambda: g.vector.tensor_scalar(A(out), A(a), v1, v2, op0, op1), reads, [out])
+
+    def act(out, in_, f, bias=None, scale=None, acc=None):
+        kw = {}
+        if bias is not None:
+            kw["bias"] = A(bias) if isinstance(bias, tuple) else bias
+        if scale is not None:
+            kw["scale"] = A(scale) if isinstance(scale, tuple) else scale
+        if acc is not None:
+            kw["accum_out"] = A(acc)
+        run("s", lambda: g.scalar.activation(A(out), A(in_), f, **kw), [in_] + [x for x in (bias, scale) if isinstance(x, tuple)],
+            [out] + ([acc] if acc is not None else []))
+
+    def fills(r, v):
+        act(r, R("ZB", 0, r[2] - r[1], r[3], r[4]), AF.Identity, bias=float(v))
+
+    def turn(out, in_):
+        run("v", lambda: g.vector.transpose(A(out), A(in_)), [in_], [out])
+
+    def total_of(out, in_, sizes=False):
+        kw = {"apply_absolute_value": True} if sizes else {}
+        run("v", lambda: g.vector.tensor_reduce(A(out), A(in_), AxisListType.X, ADD, **kw), [in_], [out])
+
+    def quant(out, c, n, tile, e):
+        o, s, i = R(out, c, c + n), R(out + "s", c, c + n), R(tile, 4 * e, 4 * e + 4 * n)
+        run("v", lambda: g.vector.quantize_mx(A(o), A(s), A(i)), [i], [o, s])
+
+    def mm(ps, b, w, c, x, d, n, start=True, stop=True):
+        o = R(ps, 512 * b, 512 * b + n)
+        l, ls, r, rs = R(w, c, c + 128), R(w + "s", c, c + 128), R(x, d, d + n), R(x + "s", d, d + n)
+        run("t", lambda: g.tensor.matmul_mx(A(o), A(l), A(ls), A(r), A(rs), start, stop), [l, ls, r, rs], [o], not start)
+
+    def pick_codes(out, c, win, width, lst, e, f):
+        o, i, l = R(out, c, c + 16 * (f - e)), R(win, 0, width), R(lst, e, f)
+        run("v", lambda: g.vector.tensor_copy(A(o).bitcast(dt.uint32), A(i).bitcast(dt.uint32).indirect(A(l))), [i, l], [o])
+
+    def pick_scales(out, c, win, width, lst, e, f):
+        o, i, l = R(out + "s", c, c + 16 * (f - e)), R(win + "s", 0, width), R(lst, e, f)
+        run("s", lambda: g.scalar.activation(A(o), A(i).indirect(A(l)), AF.Copy), [i, l], [o])
+
+    def pick(*a):
+        pick_codes(*a)
+        pick_scales(*a)
+
+    def iota(out, pattern, base, cm):
+        if SCRATCH[out[0]][2] == "int32":
+            run("g", lambda: g.iota(A(out), pattern, base, cm), [], [out])
+        else:
+            run("g", lambda: g.iota(A(out), pattern, base, cm, allow_small_or_imprecise_dtypes=True), [], [out])
+
+    def choose(r, pattern, op, fill, cm):
+        run("g", lambda: g.affine_select(A(r), A(r), pattern, op, fill, 0, cm), [r], [r])
+
+    def bits(es):
+        return sum(1 << e for e in es)
+
+    def dst(r):
+        a = topo.addr(T.cores[r])
+        return DstId(rid=a[0], pnc=a[1])
+
+    shared = [e for e in topo.engines(core, T.cores[peers[0]]) if all(e in topo.engines(core, T.cores[r]) for r in peers)]
+    whole = 1
+    while 2 * whole <= len(shared):
+        whole *= 2
+    part = 1
+    while 2 * part * PEERS <= len(shared):
+        part *= 2
+
+    def slot_at(r):
+        return rank if rank < r else rank - 1
+
+    def to_all(src, place, sem):
+        waits("g", [src], [])
+        t = RemoteDMATransfer(dst_ids=[dst(r) for r in peers], dma_engine_mask=bits(shared[:whole]), remote_sem=T.sem[sem],
+                              srcs=[S8(src)], dsts=[S8(place(r)) for r in peers], alu_op=0)
+        g.remote_dma_fused([t], local_sem=T.sem.ls)
+        total["ls"] = total.get("ls", 0) + whole
+
+    def to_each(src, place, sem):
+        waits("g", [src(r) for r in peers], [])
+        calls = []
+        for i, r in enumerate(peers):
+            calls.append(RemoteDMATransfer(dst_ids=[dst(r)], dma_engine_mask=bits(shared[part * i:part * i + part]), remote_sem=T.sem[sem],
+                                           srcs=[S8(src(r))], dsts=[S8(place(r))], alu_op=0))
+        g.remote_dma_fused(calls, local_sem=T.sem.ls)
+        total["ls"] = total.get("ls", 0) + part * PEERS
+
+    def arrives(regions, sem, per):
+        total[sem] = PEERS * per
+        note("remote", [], regions, sem, PEERS * per)
+
+    ch = rank // 2
+    dma("y", R("U4"), None, inap=T.u[:, 0:4])
+    dma("s", R("Z4"), None, inap=T.z[:, 0:4])
+    dma("y", R("TX"), None, inap=T.dm[:, :])
+    dma("y", R("TL"), None, inap=T.lv[:, :])
+    iota(R("PI"), [[0, 1]], 0, 1)
+    iota(R("WT", 4 * 448, 4 * 704), [[0, 4 * 256]], 1, 0)
+    memset(R("ZB"), 0.0)
+    for p in (0, 64):
+        fills(R("SGN", p0=p, p1=p + 64), -1.0 if p else 1.0)
+        fills(R("BROW", p0=p, p1=p + 64), 2 * P + 1 if p else 2 * P + K + 1)
+        fills(R("BDN", p0=p, p1=p + 64), -P if p else 0)
+        fills(R("BDP", p0=p, p1=p + 64), P if p else 0)
+        fills(R("DCOL", p0=p, p1=p + 64), P * rank - 1 - P if p else P * rank - 1)
+        fills(R("IC", 0, 2, p + 32, p + 64), 0.0)
+    memset(R("MSK", 0, 128), 0.5)
+    memset(R("MSK", 128, 256), -0.5)
+    choose(R("MSK", 128, 256), [[1, 128]], GT, 0.5, -1)
+    choose(R("MSK", 0, 128), [[1, 128]], GT, -0.5, -1)
+    memset(R("ONE"), 1.0)
+    memset(R("UT", 512, 768), 0.0)
+    for i, (op, v) in enumerate(((AluOpType.bitwise_and, 15), (AluOpType.arith_shift_right, 4), (AluOpType.bitwise_and, 63),
+                                 (AluOpType.bitwise_and, 31), (AluOpType.bitwise_and, 7))):
+        ts(R("II", i, i + 1), R("PI"), v, op)
+    memset(R("CO"), 0.0)
+    for c in (0, 1, 258, 259):
+        memset(R("CO", c, c // 256 * 256 + 256, step=4), 1.0)
+    copy("v", R("CC", 0, 5), R("II"))
+    Q16, TGT = R("CC", 0, 1), R("CC", 2, 3)
+    iota(R("CROW"), [[16, 4]], 0, 0)
+    iota(R("N16"), [[0, 4], [1, 16]], 0, 0)
+    for a in (64, 256):
+        iota(R("WT", 4 * a, 4 * a + 512), [[0, 512]], 1, 0)
+    iota(R("IROW"), [[1, 64]], 0, 0)
+    iota(R("ET", 0, 512), [[0, 512]], 0, 0)
+    for t in range(4):
+        if t < 2:
+            act(R("UT", 768 + t, 1280, step=4), R("ZB"), AF.Identity, bias=R("Z4", t, t + 1))
+        else:
+            ts(R("UT", 768 + t, 1280, step=4), R("ONE"), R("Z4", t, t + 1), MUL)
+        ts(R("UT", t, 512, step=4), R("ONE"), R("U4", t, t + 1), MUL)
+    quant("UQ", 0, 320, "UT", 0)
+    quant("LX1", P, P, "TX", 0)
+    for o, i, m, a in ((8, 0, 16.0, 0.0), (9, 1, 1.0, 8.0), (5, 0, 1.0, 1.0), (6, 1, 16.0, 0.0), (7, 1, 16.0, 128.0)):
+        act(R("CC", o, o + 1), R("CC", i, i + 1), AF.Identity, bias=a, scale=m)
+    quant("COQ", 0, 128, "CO", 0)
+    quant("LX1", 0, P, "TL", 0)
+    for a in (0, 192, 384):
+        memset(R("WT", 4 * a, 4 * a + 256), 0.0)
+    memset(R("EYE"), 0.5)
+    dmaq("y", "WIN1", N * K, "LX1", 0, 2 * P)
+    dma("y", R("TN"), None, inap=T.nz[:, :])
+
+    def compare(typ):
+        bk, d0, m0 = (2, 256, 128) if typ == "X" else (0, 0, 0)
+        lo, le, on = (LT, LE, GT) if typ == "X" else (GT, GE, LT)
+        row = "R%sA" % typ
+        ts(R("CT", 512 + bk, 1024, step=4), R(row, 128, 256), R("AC", bk, bk + 1), le)
+        ts(R("CT", bk + 1, 512, step=4), R(row, 0, 128), R("AC", bk + 1, bk + 2), lo)
+        for h in range(2):
+            tt(R("CT", 513 * h + bk, 512 * h + 512, step=4), R("DS", d0 + 128 * h, d0 + 128 * h + 128), R("MSK", m0, m0 + 128), on)
+
+    def local(t):
+        lx, k1 = "LX%d" % t, "K1_%d" % t
+        for typ in "XL":
+            c0, bk, row, d0 = (P, 2, "pB", 256) if typ == "X" else (0, 0, "pA", 0)
+            q, qc = "UQ", 192 if typ == "X" else 0
+            at = (("pE", 0), ("pC", 0)) if typ == "X" else (("pD", 0), ("pD", 1))
+            mm(row, 0, q, qc, lx, c0, P)
+            for h in range(2):
+                mm(at[h][0], at[h][1], lx, c0 + 128 * h, q, qc, 128)
+            act(R("R%sA" % typ), R(row, 0, P), AF.Abs)
+            if t == 2 and typ == "X":
+                pick_scales("LX2", 0, "LXV1", 2 * P + K + 128, "PLU1", 0, 16)
+            for h in range(2):
+                total_of(R("AC", bk + h, bk + h + 1), R(at[h][0], 512 * at[h][1], 512 * at[h][1] + 1), True)
+            for h in range(2):
+                act(R("DS", d0 + 128 * h, d0 + 128 * h + 128), R("R%sA" % typ, 128 * h, 128 * h + 128), AF.Sign,
+                    bias=R("AC", bk + h, bk + h + 1), scale=-1.0)
+            compare(typ)
+        mm("pC", 0, "UQ", 64, lx, 0, P, True, False)
+        mm("pC", 0, "UQ", 128, lx, P, P, False, True)
+        quant("CQ", 0, P, "CT", 0)
+        for h in range(2):
+            mm(("pE", "pA")[h], 0, "COQ", 0, "CQ", 128 * h, 128)
+        if t == 1:
+            memset(R("OT"), 0.0)
+            memset(R("OT", 258, 512, step=4), 1.0)
+            for m, b, c in ((448, 0, 8), (448, 1, 8), (576, 0, 1), (576, 1, 9), (64, 0, 5), (64, 1, 5), (256, 0, 6), (256, 1, 7)):
+                act(R("WT", 4 * m + b, 4 * m + 512, step=4), R("ZB", 0, 128), AF.Identity, bias=R("CC", c, c + 1))
+        for h in range(2):
+            ts(R("EQK", 128 * h, 128 * h + 128), R(("pE", "pA")[h], 0, 128), TGT, EQL)
+        for h in range(2):
+            tt(R("PRD", 128 * h, 128 * h + 128), R("EQK", 128 * h, 128 * h + 128), R("pC", 128 * h, 128 * h + 128), MUL)
+        total_of(R(k1), R("PRD"), True)
+        to_all(R(k1), lambda r: R("KL%d" % t, slot_at(r), slot_at(r) + 1), "ak%d" % t)
+
+    def early_constants():
+        act(R("KC"), R("CROW"), AF.Identity, bias=Q16)
+        act(R("WA"), Q16, AF.Identity, bias=float(K * rank))
+        ts(R("M16"), R("N16"), Q16, EQL)
+        for p in (0, 64):
+            for m in range(2):
+                act(R("IC", m, m + 1, p, p + 32), R("CC", 3, 4, p, p + 32), AF.Identity, bias=32.0 * m)
+
+    def late_constants():
+        ts(R("HALF"), Q16, 8.0, GE if rank % 2 else LT, float(64 + 16 * rank - 16 * ch), MUL)
+        act(R("WC"), R("CC", 4, 5), AF.Identity, bias=float(HS * rank + 1))
+        act(R("VX"), Q16, AF.Identity, bias=float(16 * (ch % 2) - 31))
+        for c in (0, 4):
+            copy("s", R("CW8", c, c + 4), R("KC"))
+        for c in (0, 4):
+            act(R("CW8", c + ch, c + ch + 1), R("KC", ch, ch + 1), AF.Identity, bias=R("HALF"))
+
+    def post(t):
+        for h in range(2):
+            mm("pD", h, "CQ", 128 * h, "COQ", 0, 128)
+        if t == 1:
+            iota(R("RB"), [[1, 16], [16, 16]], 1, 0)
+            choose(R("EYE"), [[-1, 128]], EQL, 0.0, 1)
+            iota(R("ET", 512, 1024), [[0, 512]], 0, 0)
+            for b in range(4):
+                fills(R("HT", 256 + 64 * b, 320 + 64 * b), 0.0)
+        for c in (256, 0):
+            for h in range(2):
+                ts(R("OT", c + h, c + 256, step=4), R("IROW"), R("pD", 512 * h + c // 4, 512 * h + c // 4 + 1), EQL)
+        tt(R("K1S"), R("K1_%d" % t), R("SGN", 0, 1), MUL)
+        quant("OQ", 0, 192, "OT", 0)
+        for c, s, d in ((0, 0, 0), (0, 0, 32), (0, 64, 64), (0, 64, 96), (1, 32, 0), (1, 32, 32), (1, 96, 64), (1, 96, 96)):
+            copy("s", R("OKC", c, c + 1, d, d + 32), R("K1S", 0, 1, s, s + 32))
+        if t == 1:
+            quant("WTQ", 448, 256, "WT", 448)
+            quant("WTQ", 0, 448, "WT", 0)
+        mm("pB", 0, "WTQ", 448, "OQ", 0, 128, True, False)
+        mm("pB", 0, "WTQ", 576, "OQ", 0, 128, False, True)
+        for i, (c, d) in enumerate(((128, 0), (320, 0), (0, 64), (192, 64))):
+            mm("pC", 0, "WTQ", c, "OQ", d, 128, i == 0, i == 3)
+        if t == 1:
+            early_constants()
+        for p in (0, 64):
+            tt(R("PM", p0=p, p1=p + 64), R("M16", p0=p, p1=p + 64), R("pB", p, p + 64, p, p + 64), MUL)
+        if t == 1:
+            late_constants()
+            for b in (2, 3):
+                memset(R("ET", 512 * b, 512 * b + 512), 0.0)
+            quant("NQ", 0, P, "TN", 0)
+        else:
+            list_numbers(1)
+
+    def merge(t):
+        kl = "KL%d" % t
+        arrives([R(kl)], "ak%d" % t, whole)
+        if t == 1:
+            waits("y", [R(kl)], [])
+            dmaq("y", "LXV1", 0, "LX1", 0, 2 * P)
+            for w in ("N1", "B1", "N2", "B2"):
+                dmaq("y", w, K, "LX1", 0, K)
+            dmaq("y", "HW", 32 + HS * rank, "LX1", 0, HS)
+            dmaq("y", "WIN1", K * rank, "LX1", 0, K)
+            dma("y", R("TW"), None, inap=T.w[:, :])
+        rest = [lambda c=c: total_of(R("P8", c, c + 1), R("PM", 16 * c, 16 * c + 16)) for c in range(4)]
+        rest.append(lambda: ts(R("D0"), R("pC", 0, 64), -1.0, MUL, R("BROW"), ADD))
+        rest.append(lambda: ts(R("PIU%d" % t), R("P8"), R("BDN"), ADD))
+
+        def fill(n=1):
+            for _ in range(n):
+                if rest:
+                    rest.pop(0)()
+        for s in range(PEERS):
+            o, kc = R("KR", 32 * s, 32 * s + 32), R(kl, s, s + 1)
+            if s in (1, 3, 5):
+                act(o, R("SGN"), AF.Copy, scale=kc)
+            else:
+                ts(o, R("SGN"), kc, MUL)
+        fill()
+        turn(R("KW"), R("KR"))
+        fill()
+        for m in range(2):
+            own = R("OKC", m, m + 1)
+            if rank:
+                ts(R("MM", 224 * m, 224 * m + 32 * rank), R("KW", 0, 32 * rank), own, LE)
+            if rank < PEERS:
+                ts(R("MM", 224 * m + 32 * rank, 224 * m + 224), R("KW", 32 * rank, 224), own, LT)
+            if m == 0:
+                act(R("JK", 256, 480), R("MM", 0, 224), AF.Copy, acc=R("XC", 0, 1))
+            else:
+                fill()
+                total_of(R("XC", 1, 2), R("MM", 224, 448))
+                fill()
+        if t == 1:
+            for n in "12":
+                act(R("ROW" + n), R("RB"), AF.Identity, bias=R("BDP"))
+        for m in (1, 0):
+            ts(R("XR", 32 * m, 32 * m + 32), R("ONE", 0, 32), R("XC", m, m + 1), MUL, R("IC", m, m + 1), ADD)
+        fill()
+        turn(R("Y"), R("XR"))
+        fill()
+        for p in (32, 0, 96, 64):
+            o = p - 32 if p % 64 else p + 32
+            copy("v", R("TY", p0=p, p1=p + 32), R("Y", p0=o, p1=o + 32))
+        fill()
+        tt(R("GS"), R("Y"), R("TY"), ADD)
+        for step in "e0 e1 m0 m1 e2 e3 m2 m3".split():
+            c = int(step[1])
+            e, u = R("EQ", 64 * c, 64 * c + 64), R("MU", 64 * c, 64 * c + 64)
+            if step[0] == "e":
+                ts(e, R("GS"), R("KC", c, c + 1), EQL)
+                continue
+            tt(u, e, R("pC", 0, 64), MUL)
+            if c >= 2:
+                total_of(R("FS", c, c + 1), u)
+            else:
+                act(R("JK", 512 + 64 * c, 576 + 64 * c), u, AF.Copy, acc=R("FS", c, c + 1))
+        fill()
+        copy("v", R("SW", p0=64), R("FS", p1=64))
+        copy("v", R("SW", p1=64), R("FS", p0=64))
+        fill()
+        tt(R("FM"), R("FS"), R("SW"), MAX)
+        ts(R("ZU%d" % t), R("FM"), -1.0, ADD)
+        if t == 1:
+            ts(R("INFO1"), R("FM"), 0.0, GT, R("WA"), MUL)
+        else:
+            ts(R("INFO2"), R("FM"), 0.0, GT, R("WC"), MUL)
+        pick("Z%d" % t, 0, "LX%d" % t, 2 * P, "ZU%d" % t, 0, 4)
+        fill(9)
+        to_all(R("INFO%d" % t), lambda r: R("IL%d" % t, 4 * slot_at(r), 4 * slot_at(r) + 4), "ai%d" % t)
+
+    def list_places(t):
+        row, off = R("ROW%d" % t), R("PIU%d" % t)
+        ts(R("VM"), R("GS"), float(K), LT)
+        tt(R("VT"), R("GS"), R("D0"), ADD)
+        tt(R("VU"), R("VT"), R("VM"), MUL)
+        tt(R("VV"), R("VU"), R("pC", 0, 64), ADD)
+        run("v", lambda: g.vector.tensor_copy(A(row).indirect(A(off)), A(R("VV"))), [R("VV"), off], [row])
+        for k in range(2):
+            dma("y", R("LST%d" % t, 16 * k, 16 * k + 16), R("ROW%d" % t, 0, 256, 64 * k, 64 * k + 8))
+
+    def list_slots(t, base):
+        for c, p in ((0, 0), (0, 64), (4, 64), (4, 0)):
+            copy("s", R("FLD", c, c + 4, p, p + 64), R("FS", p0=16 * c, p1=16 * c + 64))
+        ts(R("NU%d" % t), R("FLD", 0, 4), -1.0, ADD)
+        ts(R("FP"), R("FLD"), 0.0, GT, float(base - 1), MUL)
+        pick("N%d" % t, 0, "NQ", P, "NU%d" % t, 0, 4)
+        tt(R("FO"), R("FP"), R("FLD"), ADD)
+        if t == 1:
+            quant("EC", 0, 512, "ET", 0)
+        for k in range(4):
+            mm("pD", k, "EC", 128 * k, "N%d" % t, 0, 128, True, False)
+
+    def list_own(t):
+        ts(R("EQN"), R("GS"), TGT, EQL)
+        tt(R("PN"), R("EQN"), R("pC", 0, 64), MUL)
+
+    def list_numbers(t):
+        a, b = t - 1, t
+        total_of(R("NA", a, b), R("PN"))
+        ts(R("NB", a, b), R("NA", a, b), 0.0, GT, R("DCOL"), MUL)
+        tt(R("NUM", a, b), R("NB", a, b), R("NA", a, b), ADD)
+        if t == 2:
+            to_all(R("NUM"), lambda r: R("NL", 2 * slot_at(r), 2 * slot_at(r) + 2), "anum")
+
+    def renew(t, width):
+        win, lxv, nxt, lab = "WIN%d" % t, "LXV%d" % t, "LX%d" % (t + 1), "LAB%d" % t
+        pick("B%d" % t, 0, win, width, lab, 4, 8)
+        for b in range(4):
+            mm("pD", b, "EC", 128 * b, "B%d" % t, 0, 128, False, True)
+        pick(lxv, 2 * P, win, width, lab, 0, 4)
+        ts(R("PLU%d" % t), R("LST%d" % t), -1.0, ADD)
+        pick(nxt, P, lxv, 2 * P + K, "PLU%d" % t, 16, 32)
+        for b in range(4):
+            copy("sv"[b % 2], R("HT", b, 256, step=4), R("pD", 512 * b, 512 * b + 64))
+        quant(lxv, 2 * P + K, 128, "HT", 0)
+        if t == 1:
+            pick_codes(nxt, 0, lxv, 2 * P + K + 128, "PLU1", 0, 16)
+        else:
+            for h in range(2):
+                pick(nxt, 128 * h, lxv, 2 * P + K + 128, "PLU2", 8 * h, 8 * h + 8)
+
+    local(1)
+    post(1)
+    merge(1)
+    to_all(R("Z1"), lambda r: R("WIN1", K * rank, K * rank + K), "azc")
+    to_all(R("Z1s"), lambda r: R("WIN1s", K * rank, K * rank + K), "azs")
+    for b in range(4):
+        copy("s", R("ET", 512 * b + b, 512 * b + 512, step=4), R("EYE"))
+    list_places(1)
+    list_slots(1, N * K)
+    arrives([R("IL1")], "ai1", whole)
+    ts(R("V28"), R("IL1"), 0.0, ADD)
+    for c in range(4):
+        total_of(R("W5", c, c + 1), R("V28", c, 28, step=4))
+    tt(R("W6"), R("W5"), R("CROW"), ADD)
+    for k in (1, 0):
+        tt(R("AB", 4 * k, 4 * k + 4), R("FO", 4 * k, 4 * k + 4), R("W6"), MAX)
+    ts(R("LAB1"), R("AB"), 0.0, ADD)
+    list_own(1)
+    for s, sem in (("", "azc"), ("s", "azs")):
+        arrives([R("WIN1" + s, K * r, K * r + K) for r in peers], sem, whole)
+    renew(1, N * K + 2 * P)
+
+    local(2)
+    dmaq("y", "WIN2", K + 128, "LX2", 0, 2 * P)
+    dmaq("y", "LXV2", 0, "LX2", 0, 2 * P)
+    post(2)
+    merge(2)
+    for s, sem in (("", "ahc"), ("s", "ahs")):
+        to_each(lambda r: R("Z2" + s, HS * r, HS * r + HS), lambda r: R("HW" + s, 32 + HS * rank, 32 + HS * rank + HS), sem)
+    pick("HW", 0, "LX2", 2 * P, "ZU2", ch // 2 * 2, ch // 2 * 2 + 2)
+    ts(R("V8", rank, rank + 1), R("FM", ch, ch + 1), 0.0, GT, R("VX"), MUL)
+    list_places(2)
+    arrives([R("IL2")], "ai2", whole)
+    if rank:
+        ts(R("V8", 0, rank), R("IL2", ch, 4 * rank, step=4), 0.0, ADD)
+    if rank < PEERS:
+        ts(R("V8", rank + 1, N), R("IL2", 4 * rank + ch, 4 * PEERS, step=4), 0.0, ADD)
+    total_of(R("VS"), R("V8"))
+    ts(R("HL8"), R("V8"), -1.0, MUL, R("VS"), ADD)
+    ts(R("HLU2"), R("HL8"), float(K), MIN, 31.0, ADD)
+    others = [(a, b) for a, b in ((0, HS * rank), (HS * rank + HS, K)) if a < b]
+    for s, sem in (("", "ahc"), ("s", "ahs")):
+        arrives([R("HW" + s, 32 + a, 32 + b) for a, b in others], sem, part)
+    pick("WIN2", K, "HW", 32 + K, "HLU2", 0, 8)
+    hc = K + HS * (rank % 2)
+    for s, sem in (("", "awc"), ("s", "aws")):
+        to_each(lambda r: R("WIN2" + s, hc + 16 * r, hc + 16 * r + HS), lambda r: R("WIN2" + s, HS * rank, HS * rank + HS), sem)
+    list_slots(2, K + 128)
+    tt(R("AB"), R("FO"), R("CW8"), MAX)
+    ts(R("LAB2"), R("AB"), 0.0, ADD)
+    list_own(2)
+    list_numbers(2)
+    quant("WQ", 0, 128, "TW", 0)
+    for s, sem in (("", "awc"), ("s", "aws")):
+        arrives([R("WIN2" + s, a, b) for a, b in others], sem, part)
+    renew(2, K + 128 + 2 * P)
+
+    for h in range(2):
+        mm("pD", h, "WQ", 0, "LX3", 128 * h, 128)
+    dma("y", None, R("LX3", P, 2 * P), outap=T.oc[:, 4 * P:8 * P])
+    for k in range(4):
+        dma("y", None, R("LX3s", P, 2 * P, 32 * k, 32 * k + 4), outap=T.osc[4 * k:4 * k + 4, P:2 * P])
+    arrives([R("NL")], "anum", whole)
+    for t in range(2):
+        total_of(R("RES", t, t + 1), R("NL", t, 14, step=2))
+    tt(R("RES", 2, 4), R("RES", 0, 2), R("NUM"), ADD)
+    dma("y", None, R("LX3", 0, P), outap=T.oc[:, 0:4 * P])
+    for h in range(2):
+        copy("sv"[h], R("YO", 128 * h, 128 * h + 128), R("pD", 512 * h, 512 * h + 128))
+    for k in range(4):
+        dma("y", None, R("LX3s", 0, P, 32 * k, 32 * k + 4), outap=T.osc[4 * k:4 * k + 4, 0:P])
+    dma("s", None, R("YO", 0, 128), outap=T.y[:, 0:128])
+    for t in range(2):
+        dma("s", None, R("RES", 2 + t, 3 + t, 0, 64), outap=T.lw[t:t + 1, :])
+        dma("s", None, R("RES", 2 + t, 3 + t, 64, 128), outap=T.sw[t:t + 1, :])
+    dma("y", None, R("YO", 128, 256), outap=T.y[:, 128:256])
+    for sem in total:
+        if known["g"].get(sem, 0) < total[sem]:
+            g.wait_ge(T.sem[sem], total[sem])

@@ -3,10 +3,10 @@ from concourse.mybir import dt, AluOpType, AxisListType, ActivationFunctionType 
 
 N, P, K = 8, 256, 64
 PEERS = N - 1
-HS = K // N
+HS = 4 * K // N
 
 SCRATCH, VIEW = {}, {}
-SEMAPHORES = ["qv", "qs", "qt", "qg", "ls", "ak1", "ak2", "ai1", "ai2", "azc", "azs", "ahc", "ahs", "awc", "aws", "anum"] + ["d%d" % i for i in range(48)]
+SEMAPHORES = ["qv", "qs", "qt", "qg", "ls", "aka", "akb", "ai", "azc", "azs", "ag", "awc", "aws", "asc", "anc", "ans", "ahc", "ahs"] + ["d%d" % i for i in range(48)]
 
 
 def _sb(name, w, d):
@@ -28,33 +28,30 @@ def _pool(name, d, parts):
 
 
 for _n, _w in (("TL", 1024), ("TX", 1024), ("TN", 1024), ("TW", 512), ("U4", 4), ("Z4", 4), ("UT", 1280), ("ONE", 128),
-               ("ZB", 128), ("CO", 512), ("WT", 2816), ("ET", 2048), ("EYE", 128), ("CT", 1024), ("OT", 768), ("HT", 512),
-               ("MSK", 256), ("DS", 512)):
+               ("ZB", 128), ("CO", 512), ("WT", 1024), ("ET", 2048), ("EYE", 128), ("CT", 1024), ("OT", 512), ("HT", 768),
+               ("MSK", 256), ("DS", 512), ("SEL", 192), ("IRB", 128), ("FR", 128)):
     _sb(_n, _w, "bfloat16")
-_pool("BB", "bfloat16", (("EQK", 256), ("MM", 448), ("EQ", 256), ("EQN", 64)))
-_pool("FC", "float32", (("CC", 16), ("IROW", 64), ("N16", 64), ("M16", 64), ("RB", 256), ("BDN", 1), ("BDP", 1), ("CROW", 4), ("KC", 4), ("CW8", 8),
-                        ("HALF", 1), ("WA", 1), ("WC", 1), ("VX", 1), ("IC", 2), ("SGN", 32), ("DCOL", 1), ("BROW", 1)))
+_pool("BB", "bfloat16", (("EQK", 256), ("EQL", 256), ("MM", 6 * 224), ("JB", 448), ("MD", 128), ("ML", 128), ("D2", 128), ("B2T", 128),
+                         ("FM", 128), ("FS16", 128), ("JS", 224), ("XOB", 2)))
+_pool("BC", "bfloat16", (("M16", 128), ("RST", 128), ("V192", 64)))
+_pool("FC", "float32", (("CC", 16), ("N16", 128), ("SGN", 32), ("ICT", 128), ("NK", 128), ("KC", 8), ("NKC", 8), ("D16", 16),
+                        ("N32", 64), ("M32", 64), ("M4", 8), ("M8", 8), ("M8B", 8), ("MH", 4), ("VR", 128), ("V384", 64), ("PF", 2),
+                        ("SM", 32), ("R32", 128)))
 _pool("FD", "float32", (("AC", 4), ("RLA", 256), ("RXA", 256)))
-_pool("FB", "float32", (("PRD", 256), ("JK", 768), ("PM", 64), ("P8", 4), ("K1S", 1), ("OKC", 2), ("D0", 64),
-                        ("KR", 224), ("KW", 224), ("XC", 2), ("XR", 64), ("Y", 64), ("TY", 64), ("GS", 64), ("MU", 256), ("FS", 4),
-                        ("SW", 4), ("FLD", 8), ("FM", 4), ("FO", 8), ("FP", 8), ("VT", 64), ("VM", 64), ("VU", 64), ("VV", 64), ("PN", 64),
-                        ("NA", 2), ("NB", 2), ("V28", 28), ("W5", 4), ("W6", 4), ("AB", 8), ("V8", 8), ("VS", 1), ("HL8", 8)))
-for _n, _w in (("NUM", 2), ("NL", 14), ("RES", 4), ("YO", 256)):
+_pool("FB", "float32", (("PRD", 256), ("PRE", 256), ("OKC", 4), ("KR", 448), ("KW", 448), ("XC", 2), ("XO", 4), ("XR", 128), ("Y", 128), ("VV", 128),
+                        ("AB", 1024), ("FS", 8), ("XS", 16), ("G2", 2), ("GG", 2), ("GM", 2), ("A16", 16), ("H16", 16), ("PI16", 16), ("OFF", 16),
+                        ("GB", 256), ("GR", 256), ("GT8", 8), ("GC", 2), ("OF8", 8), ("OFC", 1), ("WD", 1), ("RD", 128), ("RL", 128), ("OWN", 2),
+                        ("CNT", 1), ("XB", 128), ("YB", 128), ("PA", 4), ("PB", 4), ("PC", 4), ("PD", 4), ("RES", 4), ("O4", 4), ("O5", 4),
+                        ("O32", 2), ("MO", 64), ("SM64", 64), ("S2", 2), ("SB", 64), ("G8", 8), ("G1", 1), ("NUM", 128)))
+for _n, _w in (("K1a", 1), ("K1b", 1), ("KLa", 7), ("KLb", 7), ("IL", 32), ("GA", 32), ("SC", 32), ("ROW", 384), ("LST", 32), ("YO", 256)):
     _sb(_n, _w, "float32")
-for _t in "12":
-    for _n, _w in (("K1_", 1), ("KL", 7), ("ROW", 256), ("LST", 32)):
-        _sb(_n + _t, _w, "float32")
-    for _n, _w in (("INFO", 4), ("IL", 28)):
-        _sb(_n + _t, _w, "uint16")
-    _pool("UB" + _t, "uint16", tuple((_n + _t, _w) for _n, _w in (("PIU", 4), ("ZU", 4), ("NU", 4), ("LAB", 8), ("PLU", 32), ("HLU", 8))))
-    _codes("Z" + _t, K)
-    _codes("LXV" + _t, 2 * P + K + 128)
-    _codes("B" + _t, 128)
-    _codes("N" + _t, 128)
+_pool("UB", "uint16", (("ZU", 16), ("HU", 2), ("NU", 8), ("OU", 8), ("BU", 4), ("O2", 4), ("LU", 4), ("FU", 8), ("H2U", 2), ("PLU", 32)))
 _sb("PI", 1, "int32")
-_sb("II", 5, "int32")
-for _n, _w in (("UQ", 320), ("LX1", 512), ("LX2", 512), ("LX3", 512), ("NQ", 256), ("WQ", 128), ("COQ", 128), ("WTQ", 704), ("EC", 512),
-               ("CQ", 256), ("OQ", 192), ("WIN1", N * K + 2 * P), ("WIN2", K + 128 + 2 * P), ("HW", 32 + K)):
+_sb("II", 8, "int32")
+_pool("IB", "int32", (("GI", 2), ("GJ", 2), ("AI", 16), ("HI", 16), ("RI", 4), ("RJ", 4), ("RK", 4), ("G1I", 1), ("G1J", 1)))
+for _n, _w in (("UQ", 320), ("LX1", 512), ("LX3", 512), ("NQ", 256), ("WQ", 128), ("COQ", 128), ("WTQ", 256), ("EC", 512), ("CQ", 256),
+               ("OQ", 128), ("Z", 256), ("HW", 256), ("WIN", 256), ("NE", 128), ("B2", 128), ("N2", 128), ("FW", 320), ("HW2", 64),
+               ("H2O", 16), ("AW", 128), ("LW", 384), ("XW", 448)):
     _codes(_n, _w)
 PSUM = {"pA": 1, "pB": 1, "pC": 1, "pD": 4, "pE": 1}
 for _n in PSUM:
@@ -63,6 +60,7 @@ for _n in PSUM:
 
 ADD, SUB, MUL, MAX, MIN = AluOpType.add, AluOpType.subtract, AluOpType.mult, AluOpType.max, AluOpType.min
 GT, GE, LT, LE, EQL = AluOpType.is_gt, AluOpType.is_ge, AluOpType.is_lt, AluOpType.is_le, AluOpType.is_equal
+AND, SHR = AluOpType.bitwise_and, AluOpType.arith_shift_right
 
 
 def R(name, c0=0, c1=None, p0=0, p1=128, step=1):
@@ -170,6 +168,9 @@ def rank_program(g, core, T, topo):
         else:
             run("v", lambda: g.vector.tensor_scalar(A(out), A(a), v1, v2, op0, op1), reads, [out])
 
+    def scan(out, a, b, op0):
+        run("v", lambda: g.vector.tensor_tensor_scan(A(out), A(a), A(b), 0.0, op0, ADD), [a, b], [out])
+
     def act(out, in_, f, bias=None, scale=None, acc=None):
         kw = {}
         if bias is not None:
@@ -184,12 +185,18 @@ def rank_program(g, core, T, topo):
     def fills(r, v):
         act(r, R("ZB", 0, r[2] - r[1], r[3], r[4]), AF.Identity, bias=float(v))
 
+    def plus(q, out, in_, v):
+        if q == "v":
+            ts(out, in_, float(v), ADD)
+        else:
+            act(out, in_, AF.Identity, bias=float(v))
+
     def turn(out, in_):
         run("v", lambda: g.vector.transpose(A(out), A(in_)), [in_], [out])
 
-    def total_of(out, in_, sizes=False):
+    def total_of(out, in_, sizes=False, op=ADD):
         kw = {"apply_absolute_value": True} if sizes else {}
-        run("v", lambda: g.vector.tensor_reduce(A(out), A(in_), AxisListType.X, ADD, **kw), [in_], [out])
+        run("v", lambda: g.vector.tensor_reduce(A(out), A(in_), AxisListType.X, op, **kw), [in_], [out])
 
     def quant(out, c, n, tile, e):
         o, s, i = R(out, c, c + n), R(out + "s", c, c + n), R(tile, 4 * e, 4 * e + 4 * n)
@@ -200,17 +207,23 @@ def rank_program(g, core, T, topo):
         l, ls, r, rs = R(w, c, c + 128), R(w + "s", c, c + 128), R(x, d, d + n), R(x + "s", d, d + n)
         run("t", lambda: g.tensor.matmul_mx(A(o), A(l), A(ls), A(r), A(rs), start, stop), [l, ls, r, rs], [o], not start)
 
-    def pick_codes(out, c, win, width, lst, e, f):
-        o, i, l = R(out, c, c + 16 * (f - e)), R(win, 0, width), R(lst, e, f)
+    def pick_codes(out, c, win, a, width, lst, e, f):
+        o, i, l = R(out, c, c + 16 * (f - e)), R(win, a, a + width), R(lst, e, f)
         run("v", lambda: g.vector.tensor_copy(A(o).bitcast(dt.uint32), A(i).bitcast(dt.uint32).indirect(A(l))), [i, l], [o])
 
-    def pick_scales(out, c, win, width, lst, e, f):
-        o, i, l = R(out + "s", c, c + 16 * (f - e)), R(win + "s", 0, width), R(lst, e, f)
+    def pick_scales(out, c, win, a, width, lst, e, f):
+        o, i, l = R(out + "s", c, c + 16 * (f - e)), R(win + "s", a, a + width), R(lst, e, f)
         run("s", lambda: g.scalar.activation(A(o), A(i).indirect(A(l)), AF.Copy), [i, l], [o])
 
     def pick(*a):
         pick_codes(*a)
         pick_scales(*a)
+
+    def scatter(win, off, vals):
+        run("v", lambda: g.vector.tensor_copy(A(win).indirect(A(off)), A(vals)), [vals, off], [win])
+
+    def gather(out, win, off):
+        run("s", lambda: g.scalar.activation(A(out), A(win).indirect(A(off)), AF.Copy), [win, off], [out])
 
     def iota(out, pattern, base, cm):
         if SCRATCH[out[0]][2] == "int32":
@@ -259,41 +272,31 @@ def rank_program(g, core, T, topo):
         total[sem] = PEERS * per
         note("remote", [], regions, sem, PEERS * per)
 
-    ch = rank // 2
+    base = P * rank
     dma("y", R("U4"), None, inap=T.u[:, 0:4])
     dma("s", R("Z4"), None, inap=T.z[:, 0:4])
     dma("y", R("TX"), None, inap=T.dm[:, :])
     dma("y", R("TL"), None, inap=T.lv[:, :])
     iota(R("PI"), [[0, 1]], 0, 1)
-    iota(R("WT", 4 * 448, 4 * 704), [[0, 4 * 256]], 1, 0)
     memset(R("ZB"), 0.0)
-    for p in (0, 64):
-        fills(R("SGN", p0=p, p1=p + 64), -1.0 if p else 1.0)
-        fills(R("BROW", p0=p, p1=p + 64), 2 * P + 1 if p else 2 * P + K + 1)
-        fills(R("BDN", p0=p, p1=p + 64), -P if p else 0)
-        fills(R("BDP", p0=p, p1=p + 64), P if p else 0)
-        fills(R("DCOL", p0=p, p1=p + 64), P * rank - 1 - P if p else P * rank - 1)
-        fills(R("IC", 0, 2, p + 32, p + 64), 0.0)
     memset(R("MSK", 0, 128), 0.5)
     memset(R("MSK", 128, 256), -0.5)
     choose(R("MSK", 128, 256), [[1, 128]], GT, 0.5, -1)
     choose(R("MSK", 0, 128), [[1, 128]], GT, -0.5, -1)
+    iota(R("IRB"), [[1, 128]], 0, 0)
+    for p in (0, 64):
+        fills(R("SGN", p0=p, p1=p + 64), -1.0 if p else 1.0)
+    for i, v in enumerate((1.0, 0.0, 1.0)):
+        fills(R("SEL", 64 * i, 64 * i + 64), v)
     memset(R("ONE"), 1.0)
     memset(R("UT", 512, 768), 0.0)
-    for i, (op, v) in enumerate(((AluOpType.bitwise_and, 15), (AluOpType.arith_shift_right, 4), (AluOpType.bitwise_and, 63),
-                                 (AluOpType.bitwise_and, 31), (AluOpType.bitwise_and, 7))):
+    for i, (op, v) in enumerate(((AND, 15), (SHR, 4), (AND, 63), (AND, 31), (AND, 7), (SHR, 5), (AND, 16))):
         ts(R("II", i, i + 1), R("PI"), v, op)
     memset(R("CO"), 0.0)
     for c in (0, 1, 258, 259):
         memset(R("CO", c, c // 256 * 256 + 256, step=4), 1.0)
-    copy("v", R("CC", 0, 5), R("II"))
+    copy("v", R("CC", 0, 7), R("II", 0, 7))
     Q16, TGT = R("CC", 0, 1), R("CC", 2, 3)
-    iota(R("CROW"), [[16, 4]], 0, 0)
-    iota(R("N16"), [[0, 4], [1, 16]], 0, 0)
-    for a in (64, 256):
-        iota(R("WT", 4 * a, 4 * a + 512), [[0, 512]], 1, 0)
-    iota(R("IROW"), [[1, 64]], 0, 0)
-    iota(R("ET", 0, 512), [[0, 512]], 0, 0)
     for t in range(4):
         if t < 2:
             act(R("UT", 768 + t, 1280, step=4), R("ZB"), AF.Identity, bias=R("Z4", t, t + 1))
@@ -302,14 +305,15 @@ def rank_program(g, core, T, topo):
         ts(R("UT", t, 512, step=4), R("ONE"), R("U4", t, t + 1), MUL)
     quant("UQ", 0, 320, "UT", 0)
     quant("LX1", P, P, "TX", 0)
-    for o, i, m, a in ((8, 0, 16.0, 0.0), (9, 1, 1.0, 8.0), (5, 0, 1.0, 1.0), (6, 1, 16.0, 0.0), (7, 1, 16.0, 128.0)):
-        act(R("CC", o, o + 1), R("CC", i, i + 1), AF.Identity, bias=a, scale=m)
+    for o, i, m, a in ((8, 0, 1.0, 1.0), (9, 1, 16.0, 0.0), (10, 1, 16.0, 128.0)):
+        act(R("CC", o, o + 1), R("CC", i, i + 1), AF.Identity, bias=a / 4096, scale=m / 4096)
+    act(R("CC", 11, 12), TGT, AF.Identity, bias=64.0)
     quant("COQ", 0, 128, "CO", 0)
     quant("LX1", 0, P, "TL", 0)
-    for a in (0, 192, 384):
-        memset(R("WT", 4 * a, 4 * a + 256), 0.0)
     memset(R("EYE"), 0.5)
-    dmaq("y", "WIN1", N * K, "LX1", 0, 2 * P)
+    choose(R("EYE"), [[-1, 128]], EQL, 0.0, 1)
+    iota(R("ET", 0, 1024), [[0, 1024]], 0, 0)
+    waits("y", [R("TL")], [])
     dma("y", R("TN"), None, inap=T.nz[:, :])
 
     def compare(typ):
@@ -321,298 +325,333 @@ def rank_program(g, core, T, topo):
         for h in range(2):
             tt(R("CT", 513 * h + bk, 512 * h + 512, step=4), R("DS", d0 + 128 * h, d0 + 128 * h + 128), R("MSK", m0, m0 + 128), on)
 
-    def local(t):
-        lx, k1 = "LX%d" % t, "K1_%d" % t
-        for typ in "XL":
-            c0, bk, row, d0 = (P, 2, "pB", 256) if typ == "X" else (0, 0, "pA", 0)
-            q, qc = "UQ", 192 if typ == "X" else 0
-            at = (("pE", 0), ("pC", 0)) if typ == "X" else (("pD", 0), ("pD", 1))
-            mm(row, 0, q, qc, lx, c0, P)
-            for h in range(2):
-                mm(at[h][0], at[h][1], lx, c0 + 128 * h, q, qc, 128)
-            act(R("R%sA" % typ), R(row, 0, P), AF.Abs)
-            if t == 2 and typ == "X":
-                pick_scales("LX2", 0, "LXV1", 2 * P + K + 128, "PLU1", 0, 16)
-            for h in range(2):
-                total_of(R("AC", bk + h, bk + h + 1), R(at[h][0], 512 * at[h][1], 512 * at[h][1] + 1), True)
-            for h in range(2):
-                act(R("DS", d0 + 128 * h, d0 + 128 * h + 128), R("R%sA" % typ, 128 * h, 128 * h + 128), AF.Sign,
-                    bias=R("AC", bk + h, bk + h + 1), scale=-1.0)
-            compare(typ)
-        mm("pC", 0, "UQ", 64, lx, 0, P, True, False)
-        mm("pC", 0, "UQ", 128, lx, P, P, False, True)
-        quant("CQ", 0, P, "CT", 0)
+    for typ in "XL":
+        c0, bk, row, d0 = (P, 2, "pB", 256) if typ == "X" else (0, 0, "pA", 0)
+        qc = 192 if typ == "X" else 0
+        at = (("pE", 0), ("pC", 0)) if typ == "X" else (("pD", 0), ("pD", 1))
+        mm(row, 0, "UQ", qc, "LX1", c0, P)
         for h in range(2):
-            mm(("pE", "pA")[h], 0, "COQ", 0, "CQ", 128 * h, 128)
-        if t == 1:
-            memset(R("OT"), 0.0)
-            memset(R("OT", 258, 512, step=4), 1.0)
-            for m, b, c in ((448, 0, 8), (448, 1, 8), (576, 0, 1), (576, 1, 9), (64, 0, 5), (64, 1, 5), (256, 0, 6), (256, 1, 7)):
-                act(R("WT", 4 * m + b, 4 * m + 512, step=4), R("ZB", 0, 128), AF.Identity, bias=R("CC", c, c + 1))
+            mm(at[h][0], at[h][1], "LX1", c0 + 128 * h, "UQ", qc, 128)
+        act(R("R%sA" % typ), R(row, 0, P), AF.Abs)
         for h in range(2):
-            ts(R("EQK", 128 * h, 128 * h + 128), R(("pE", "pA")[h], 0, 128), TGT, EQL)
+            total_of(R("AC", bk + h, bk + h + 1), R(at[h][0], 512 * at[h][1], 512 * at[h][1] + 1), True)
         for h in range(2):
-            tt(R("PRD", 128 * h, 128 * h + 128), R("EQK", 128 * h, 128 * h + 128), R("pC", 128 * h, 128 * h + 128), MUL)
-        total_of(R(k1), R("PRD"), True)
-        to_all(R(k1), lambda r: R("KL%d" % t, slot_at(r), slot_at(r) + 1), "ak%d" % t)
-
-    def early_constants():
-        act(R("KC"), R("CROW"), AF.Identity, bias=Q16)
-        act(R("WA"), Q16, AF.Identity, bias=float(K * rank))
-        ts(R("M16"), R("N16"), Q16, EQL)
-        for p in (0, 64):
-            for m in range(2):
-                act(R("IC", m, m + 1, p, p + 32), R("CC", 3, 4, p, p + 32), AF.Identity, bias=32.0 * m)
-
-    def late_constants():
-        ts(R("HALF"), Q16, 8.0, GE if rank % 2 else LT, float(64 + 16 * rank - 16 * ch), MUL)
-        act(R("WC"), R("CC", 4, 5), AF.Identity, bias=float(HS * rank + 1))
-        act(R("VX"), Q16, AF.Identity, bias=float(16 * (ch % 2) - 31))
-        for c in (0, 4):
-            copy("s", R("CW8", c, c + 4), R("KC"))
-        for c in (0, 4):
-            act(R("CW8", c + ch, c + ch + 1), R("KC", ch, ch + 1), AF.Identity, bias=R("HALF"))
-
-    def post(t):
+            act(R("DS", d0 + 128 * h, d0 + 128 * h + 128), R("R%sA" % typ, 128 * h, 128 * h + 128), AF.Sign,
+                bias=R("AC", bk + h, bk + h + 1), scale=-1.0)
+        compare(typ)
+    mm("pC", 0, "UQ", 64, "LX1", 0, P, True, False)
+    mm("pC", 0, "UQ", 128, "LX1", P, P, False, True)
+    quant("CQ", 0, P, "CT", 0)
+    for h in range(2):
+        mm(("pE", "pA")[h], 0, "COQ", 0, "CQ", 128 * h, 128)
+    for h in range(2):
+        mm("pD", h, "CQ", 128 * h, "COQ", 0, 128)
+    for m in range(2):
+        for b in range(4):
+            s0, dc = 0 if b < 2 else 64, 8 + m * (1 + b % 2)
+            act(R("WT", 512 * m + b, 512 * m + 512, step=4), R("SEL", s0, s0 + 128), AF.Copy, scale=R("CC", dc, dc + 1))
+    for n, e, pr, tg in (("a", "EQK", "PRD", TGT), ("b", "EQL", "PRE", R("CC", 11, 12))):
         for h in range(2):
-            mm("pD", h, "CQ", 128 * h, "COQ", 0, 128)
-        if t == 1:
-            iota(R("RB"), [[1, 16], [16, 16]], 1, 0)
-            choose(R("EYE"), [[-1, 128]], EQL, 0.0, 1)
-            iota(R("ET", 512, 1024), [[0, 512]], 0, 0)
-            for b in range(4):
-                fills(R("HT", 256 + 64 * b, 320 + 64 * b), 0.0)
-        for c in (256, 0):
-            for h in range(2):
-                ts(R("OT", c + h, c + 256, step=4), R("IROW"), R("pD", 512 * h + c // 4, 512 * h + c // 4 + 1), EQL)
-        tt(R("K1S"), R("K1_%d" % t), R("SGN", 0, 1), MUL)
-        quant("OQ", 0, 192, "OT", 0)
-        for c, s, d in ((0, 0, 0), (0, 0, 32), (0, 64, 64), (0, 64, 96), (1, 32, 0), (1, 32, 32), (1, 96, 64), (1, 96, 96)):
-            copy("s", R("OKC", c, c + 1, d, d + 32), R("K1S", 0, 1, s, s + 32))
-        if t == 1:
-            quant("WTQ", 448, 256, "WT", 448)
-            quant("WTQ", 0, 448, "WT", 0)
-        mm("pB", 0, "WTQ", 448, "OQ", 0, 128, True, False)
-        mm("pB", 0, "WTQ", 576, "OQ", 0, 128, False, True)
-        for i, (c, d) in enumerate(((128, 0), (320, 0), (0, 64), (192, 64))):
-            mm("pC", 0, "WTQ", c, "OQ", d, 128, i == 0, i == 3)
-        if t == 1:
-            early_constants()
-        for p in (0, 64):
-            tt(R("PM", p0=p, p1=p + 64), R("M16", p0=p, p1=p + 64), R("pB", p, p + 64, p, p + 64), MUL)
-        if t == 1:
-            late_constants()
-            for b in (2, 3):
-                memset(R("ET", 512 * b, 512 * b + 512), 0.0)
-            quant("NQ", 0, P, "TN", 0)
-        else:
-            list_numbers(1)
+            ts(R(e, 128 * h, 128 * h + 128), R(("pE", "pA")[h], 0, 128), tg, EQL)
+        for h in range(2):
+            tt(R(pr, 128 * h, 128 * h + 128), R(e, 128 * h, 128 * h + 128), R("pC", 128 * h, 128 * h + 128), MUL)
+        total_of(R("K1" + n), R(pr), True)
+        to_all(R("K1" + n), lambda r: R("KL" + n, slot_at(r), slot_at(r) + 1), "ak" + n)
 
-    def merge(t):
-        kl = "KL%d" % t
-        arrives([R(kl)], "ak%d" % t, whole)
-        if t == 1:
-            waits("y", [R(kl)], [])
-            dmaq("y", "LXV1", 0, "LX1", 0, 2 * P)
-            for w in ("N1", "B1", "N2", "B2"):
-                dmaq("y", w, K, "LX1", 0, K)
-            dmaq("y", "HW", 32 + HS * rank, "LX1", 0, HS)
-            dmaq("y", "WIN1", K * rank, "LX1", 0, K)
-            dma("y", R("TW"), None, inap=T.w[:, :])
-        rest = [lambda c=c: total_of(R("P8", c, c + 1), R("PM", 16 * c, 16 * c + 16)) for c in range(4)]
-        rest.append(lambda: ts(R("D0"), R("pC", 0, 64), -1.0, MUL, R("BROW"), ADD))
-        rest.append(lambda: ts(R("PIU%d" % t), R("P8"), R("BDN"), ADD))
+    iota(R("R32"), [[32, 4], [0, 32]], 0, 0)
+    iota(R("SM", 0, 8), [[16, 8]], 0, 0)
+    iota(R("N16"), [[0, 8], [1, 16]], 0, 0)
+    iota(R("ROW", 0, 256), [[1, 16], [16, 16]], 0, 0)
+    iota(R("NK"), [[-16, 4], [0, 2], [-1, 16]], 0, 0)
+    iota(R("SM", 8, 16), [[0, 2], [1, 4]], 0, 0)
+    iota(R("SM", 16, 24), [[-4, 2], [1, 4]], 4, 0)
+    iota(R("N32"), [[0, 2], [1, 32]], 0, 0)
+    iota(R("PF", 0, 1), [[0, 1]], 0, 1)
+    iota(R("SM", 24, 28), [[0, 2], [16, 2]], 0, 0)
+    for b in range(4):
+        c = 512 * (b % 2) + 64 * (b // 2)
+        ts(R("OT", b, 512, step=4), R("IRB"), R("pD", c, c + 1), EQL)
+    quant("OQ", 0, 128, "OT", 0)
+    quant("WTQ", 0, 256, "WT", 0)
+    for m in range(4):
+        for q in range(4):
+            s = 64 * (q // 2) + 32 * (m % 2)
+            act(R("OKC", m, m + 1, 32 * q, 32 * q + 32), R("K1" + "aabb"[m], 0, 1, s, s + 32), AF.Copy, scale=-1.0 if q > 1 else 1.0)
+    for m in range(2):
+        mm("pB", 0, "WTQ", 128 * m, "OQ", 0, 128, m == 0, m == 1)
+    quant("NQ", 0, P, "TN", 0)
+    for b in (2, 3):
+        memset(R("ET", 512 * b, 512 * b + 512), 0.0)
+    act(R("ICT"), R("R32"), AF.Identity, bias=R("CC", 3, 4))
+    act(R("KC"), R("SM", 0, 8), AF.Identity, bias=Q16)
+    act(R("NKC"), R("KC"), AF.Copy, scale=-4096.0)
+    for b in range(4):
+        copy("s", R("ET", 512 * b + b, 512 * b + 512, step=4), R("EYE"))
+    memset(R("HT", 0, 256), 0.0)
+    memset(R("HT", 512, 768), 0.0)
+    quant("EC", 0, 512, "ET", 0)
+    for c in (0, 8):
+        act(R("D16", c, c + 8), R("KC"), AF.Identity, bias=float(P))
+    for c in (256, 320):
+        fills(R("ROW", c, c + 64), 0.0)
 
-        def fill(n=1):
-            for _ in range(n):
-                if rest:
-                    rest.pop(0)()
+    arrives([R("KLa")], "aka", whole)
+    arrives([R("KLb")], "akb", whole)
+    waits("y", [R("KLb")], [])
+    dmaq("y", "LW", 0, "LX1", 0, P)
+    dmaq("y", "XW", 0, "LX1", P, P)
+    for w in ("B2", "N2"):
+        dmaq("y", w, K, "LX1", 0, K)
+    dma("y", R("TW"), None, inap=T.w[:, :])
+
+    def spread(t, on_s):
         for s in range(PEERS):
-            o, kc = R("KR", 32 * s, 32 * s + 32), R(kl, s, s + 1)
-            if s in (1, 3, 5):
+            o, kc = R("KR", 224 * t + 32 * s, 224 * t + 32 * s + 32), R("KL" + "ab"[t], s, s + 1)
+            if s in on_s:
                 act(o, R("SGN"), AF.Copy, scale=kc)
             else:
                 ts(o, R("SGN"), kc, MUL)
-        fill()
-        turn(R("KW"), R("KR"))
-        fill()
-        for m in range(2):
-            own = R("OKC", m, m + 1)
-            if rank:
-                ts(R("MM", 224 * m, 224 * m + 32 * rank), R("KW", 0, 32 * rank), own, LE)
-            if rank < PEERS:
-                ts(R("MM", 224 * m + 32 * rank, 224 * m + 224), R("KW", 32 * rank, 224), own, LT)
-            if m == 0:
-                act(R("JK", 256, 480), R("MM", 0, 224), AF.Copy, acc=R("XC", 0, 1))
-            else:
-                fill()
-                total_of(R("XC", 1, 2), R("MM", 224, 448))
-                fill()
-        if t == 1:
-            for n in "12":
-                act(R("ROW" + n), R("RB"), AF.Identity, bias=R("BDP"))
-        for m in (1, 0):
-            ts(R("XR", 32 * m, 32 * m + 32), R("ONE", 0, 32), R("XC", m, m + 1), MUL, R("IC", m, m + 1), ADD)
-        fill()
-        turn(R("Y"), R("XR"))
-        fill()
-        for p in (32, 0, 96, 64):
-            o = p - 32 if p % 64 else p + 32
-            copy("v", R("TY", p0=p, p1=p + 32), R("Y", p0=o, p1=o + 32))
-        fill()
-        tt(R("GS"), R("Y"), R("TY"), ADD)
-        for step in "e0 e1 m0 m1 e2 e3 m2 m3".split():
-            c = int(step[1])
-            e, u = R("EQ", 64 * c, 64 * c + 64), R("MU", 64 * c, 64 * c + 64)
-            if step[0] == "e":
-                ts(e, R("GS"), R("KC", c, c + 1), EQL)
-                continue
-            tt(u, e, R("pC", 0, 64), MUL)
-            if c >= 2:
-                total_of(R("FS", c, c + 1), u)
-            else:
-                act(R("JK", 512 + 64 * c, 576 + 64 * c), u, AF.Copy, acc=R("FS", c, c + 1))
-        fill()
-        copy("v", R("SW", p0=64), R("FS", p1=64))
-        copy("v", R("SW", p1=64), R("FS", p0=64))
-        fill()
-        tt(R("FM"), R("FS"), R("SW"), MAX)
-        ts(R("ZU%d" % t), R("FM"), -1.0, ADD)
-        if t == 1:
-            ts(R("INFO1"), R("FM"), 0.0, GT, R("WA"), MUL)
-        else:
-            ts(R("INFO2"), R("FM"), 0.0, GT, R("WC"), MUL)
-        pick("Z%d" % t, 0, "LX%d" % t, 2 * P, "ZU%d" % t, 0, 4)
-        fill(9)
-        to_all(R("INFO%d" % t), lambda r: R("IL%d" % t, 4 * slot_at(r), 4 * slot_at(r) + 4), "ai%d" % t)
 
-    def list_places(t):
-        row, off = R("ROW%d" % t), R("PIU%d" % t)
-        ts(R("VM"), R("GS"), float(K), LT)
-        tt(R("VT"), R("GS"), R("D0"), ADD)
-        tt(R("VU"), R("VT"), R("VM"), MUL)
-        tt(R("VV"), R("VU"), R("pC", 0, 64), ADD)
-        run("v", lambda: g.vector.tensor_copy(A(row).indirect(A(off)), A(R("VV"))), [R("VV"), off], [row])
-        for k in range(2):
-            dma("y", R("LST%d" % t, 16 * k, 16 * k + 16), R("ROW%d" % t, 0, 256, 64 * k, 64 * k + 8))
+    def against(u, t, m):
+        own, a = R("OKC", m, m + 1), 224 * t
+        if rank:
+            ts(R("MM", 224 * u, 224 * u + 32 * rank), R("KW", a, a + 32 * rank), own, LE)
+        if rank < PEERS:
+            ts(R("MM", 224 * u + 32 * rank, 224 * u + 224), R("KW", a + 32 * rank, a + 224), own, LT)
 
-    def list_slots(t, base):
-        for c, p in ((0, 0), (0, 64), (4, 64), (4, 0)):
-            copy("s", R("FLD", c, c + 4, p, p + 64), R("FS", p0=16 * c, p1=16 * c + 64))
-        ts(R("NU%d" % t), R("FLD", 0, 4), -1.0, ADD)
-        ts(R("FP"), R("FLD"), 0.0, GT, float(base - 1), MUL)
-        pick("N%d" % t, 0, "NQ", P, "NU%d" % t, 0, 4)
-        tt(R("FO"), R("FP"), R("FLD"), ADD)
-        if t == 1:
-            quant("EC", 0, 512, "ET", 0)
-        for k in range(4):
-            mm("pD", k, "EC", 128 * k, "N%d" % t, 0, 128, True, False)
+    def other(q):
+        return 32 * (q ^ 1)
 
-    def list_own(t):
-        ts(R("EQN"), R("GS"), TGT, EQL)
-        tt(R("PN"), R("EQN"), R("pC", 0, 64), MUL)
-
-    def list_numbers(t):
-        a, b = t - 1, t
-        total_of(R("NA", a, b), R("PN"))
-        ts(R("NB", a, b), R("NA", a, b), 0.0, GT, R("DCOL"), MUL)
-        tt(R("NUM", a, b), R("NB", a, b), R("NA", a, b), ADD)
-        if t == 2:
-            to_all(R("NUM"), lambda r: R("NL", 2 * slot_at(r), 2 * slot_at(r) + 2), "anum")
-
-    def renew(t, width):
-        win, lxv, nxt, lab = "WIN%d" % t, "LXV%d" % t, "LX%d" % (t + 1), "LAB%d" % t
-        pick("B%d" % t, 0, win, width, lab, 4, 8)
-        for b in range(4):
-            mm("pD", b, "EC", 128 * b, "B%d" % t, 0, 128, False, True)
-        pick(lxv, 2 * P, win, width, lab, 0, 4)
-        ts(R("PLU%d" % t), R("LST%d" % t), -1.0, ADD)
-        pick(nxt, P, lxv, 2 * P + K, "PLU%d" % t, 16, 32)
-        for b in range(4):
-            copy("sv"[b % 2], R("HT", b, 256, step=4), R("pD", 512 * b, 512 * b + 64))
-        quant(lxv, 2 * P + K, 128, "HT", 0)
-        if t == 1:
-            pick_codes(nxt, 0, lxv, 2 * P + K + 128, "PLU1", 0, 16)
-        else:
-            for h in range(2):
-                pick(nxt, 128 * h, lxv, 2 * P + K + 128, "PLU2", 8 * h, 8 * h + 8)
-
-    local(1)
-    post(1)
-    merge(1)
-    to_all(R("Z1"), lambda r: R("WIN1", K * rank, K * rank + K), "azc")
-    to_all(R("Z1s"), lambda r: R("WIN1s", K * rank, K * rank + K), "azs")
-    for b in range(4):
-        copy("s", R("ET", 512 * b + b, 512 * b + 512, step=4), R("EYE"))
-    list_places(1)
-    list_slots(1, N * K)
-    arrives([R("IL1")], "ai1", whole)
-    ts(R("V28"), R("IL1"), 0.0, ADD)
-    for c in range(4):
-        total_of(R("W5", c, c + 1), R("V28", c, 28, step=4))
-    tt(R("W6"), R("W5"), R("CROW"), ADD)
-    for k in (1, 0):
-        tt(R("AB", 4 * k, 4 * k + 4), R("FO", 4 * k, 4 * k + 4), R("W6"), MAX)
-    ts(R("LAB1"), R("AB"), 0.0, ADD)
-    list_own(1)
+    spread(0, (1, 3, 5))
+    turn(R("KW", 0, 224), R("KR", 0, 224))
+    spread(1, range(PEERS))
+    for m in (2, 3):
+        against(m, 0, m)
+        act(R("JS"), R("MM", 224 * m, 224 * m + 224), AF.Copy, acc=R("XC", m - 2, m - 1))
+    for m in (0, 1):
+        against(m, 0, m)
+    for q in range(4):
+        copy("s", R("XO", 2, 4, 32 * q, 32 * q + 32), R("XC", 0, 2, other(q), other(q) + 32))
+    turn(R("KW", 224, 448), R("KR", 224, 448))
+    for m in (0, 1):
+        against(4 + m, 1, m)
+    for m in (0, 1):
+        scan(R("JB", 224 * m, 224 * m + 224), R("MM", 224 * m, 224 * m + 224), R("MM", 224 * (4 + m), 224 * (5 + m)), ADD)
+    for q in range(4):
+        copy("vs"[q % 2], R("XOB", 0, 2, 32 * q, 32 * q + 32), R("JB", 223, 448, other(q), other(q) + 32, 224))
+        if q % 2:
+            m = 2 + q // 2
+            ts(R("XR", 32 * m, 32 * m + 32), R("ICT", 32 * m, 32 * m + 32), R("XC", m - 2, m - 1), ADD, R("XO", m, m + 1), ADD)
+    for m in (0, 1):
+        ts(R("XR", 32 * m, 32 * m + 32), R("ICT", 32 * m, 32 * m + 32), R("JB", 224 * m + 223, 224 * m + 224), ADD, R("XOB", m, m + 1), ADD)
+    turn(R("Y"), R("XR"))
+    tt(R("VV"), R("Y"), R("pB", 0, 128), ADD)
+    for c in range(7, -1, -1):
+        a = R("AB", 128 * c, 128 * c + 16 * c + 16)
+        act(a, R("VV", 0, 16 * c + 16), AF.Abs, bias=R("NKC", c, c + 1), scale=4096.0)
+        total_of(R("FS", c, c + 1), a, op=MIN)
+    for q, d, s in (("v", 0, 64), ("s", 0, 0), ("v", 64, 0), ("s", 64, 64)):
+        plus(q, R("XS", 8 - s // 8, 16 - s // 8, d, d + 64), R("FS", 0, 8, s, s + 64), base - 1 + 4 * s)
+    to_each(lambda r: R("XS", 2 * r, 2 * r + 2), lambda r: R("IL", 4 * rank, 4 * rank + 2), "ai")
+    ts(R("ZU"), R("XS"), float(base + 2 * P - 1), MIN, float(-base), ADD)
+    pick("Z", 0, "LX1", 0, 2 * P, "ZU", 0, 16)
     for s, sem in (("", "azc"), ("s", "azs")):
-        arrives([R("WIN1" + s, K * r, K * r + K) for r in peers], sem, whole)
-    renew(1, N * K + 2 * P)
+        to_each(lambda r: R("Z" + s, HS * r, HS * r + HS), lambda r: R("HW" + s, HS * rank, HS * rank + HS), sem)
+    copy("s", R("IL", 4 * rank, 4 * rank + 2), R("XS", 2 * rank, 2 * rank + 2))
+    pick("HW", HS * rank, "LX1", 0, 2 * P, "ZU", 2 * rank, 2 * rank + 2)
 
-    local(2)
-    dmaq("y", "WIN2", K + 128, "LX2", 0, 2 * P)
-    dmaq("y", "LXV2", 0, "LX2", 0, 2 * P)
-    post(2)
-    merge(2)
-    for s, sem in (("", "ahc"), ("s", "ahs")):
-        to_each(lambda r: R("Z2" + s, HS * r, HS * r + HS), lambda r: R("HW" + s, 32 + HS * rank, 32 + HS * rank + HS), sem)
-    pick("HW", 0, "LX2", 2 * P, "ZU2", ch // 2 * 2, ch // 2 * 2 + 2)
-    ts(R("V8", rank, rank + 1), R("FM", ch, ch + 1), 0.0, GT, R("VX"), MUL)
-    list_places(2)
-    arrives([R("IL2")], "ai2", whole)
-    if rank:
-        ts(R("V8", 0, rank), R("IL2", ch, 4 * rank, step=4), 0.0, ADD)
-    if rank < PEERS:
-        ts(R("V8", rank + 1, N), R("IL2", 4 * rank + ch, 4 * PEERS, step=4), 0.0, ADD)
-    total_of(R("VS"), R("V8"))
-    ts(R("HL8"), R("V8"), -1.0, MUL, R("VS"), ADD)
-    ts(R("HLU2"), R("HL8"), float(K), MIN, 31.0, ADD)
-    others = [(a, b) for a, b in ((0, HS * rank), (HS * rank + HS, K)) if a < b]
-    for s, sem in (("", "ahc"), ("s", "ahs")):
-        arrives([R("HW" + s, 32 + a, 32 + b) for a, b in others], sem, part)
-    pick("WIN2", K, "HW", 32 + K, "HLU2", 0, 8)
-    hc = K + HS * (rank % 2)
+    ts(R("NU"), R("XS", 8, 16), float(base + P - 1), MIN, float(-base), ADD)
+    for c, a in ((0, base + P), (8, base)):
+        ts(R("AI", c, c + 8), R("XS", c, c + 8), float(-a), ADD, 3839.0, MIN)
+    pick("NE", 0, "NQ", 0, P, "NU", 0, 8)
+    for b in range(4):
+        mm("pD", b, "EC", 128 * b, "NE", 0, 128, True, False)
+    ts(R("HI"), R("AI"), 4, SHR)
+    ts(R("A16"), R("AI"), 16.0, MUL)
+    ts(R("H16"), R("HI"), -255.0, MUL)
+    ts(R("MH"), R("SM", 24, 28), R("CC", 6, 7), EQL)
+    tt(R("PI16"), R("A16"), R("H16"), ADD)
+    ts(R("O4"), R("XS", 8, 12), float(base + P), LT)
+    tt(R("OFF"), R("PI16"), R("D16"), MIN)
+    tt(R("O5"), R("O4"), R("MH"), MUL)
+    for p in (0, 64):
+        ts(R("OU", p0=p, p1=p + 64), R("OFF", 8 - p // 8, 16 - p // 8, p, p + 64), 0.0, ADD)
+    tt(R("O32"), R("O5", 0, 4, step=2), R("O5", 1, 4, step=2), ADD)
+    for n, src, c in (("M32", R("N32"), 3), ("M8", R("SM", 16, 24), 1), ("M4", R("SM", 8, 16), 5), ("M8B", R("N16", 0, 8), 4)):
+        ts(R(n), src, R("CC", c, c + 1), EQL)
+    for a in range(2):
+        act(R("MO", 32 * a, 32 * a + 32), R("M32", 32 * a, 32 * a + 32), AF.Copy, scale=R("O32", a, a + 1))
+    plus("s", R("VR", p1=64), R("IRB", p1=64), 256)
+    for a in (0, 64):
+        plus("s", R("VR", a, a + 64, 64), R("IRB", 64 - a, 128 - a, 64), 256)
+
+    arrives([R("IL", 4 * r, 4 * r + 2) for r in peers], "ai", part)
+    for c in range(2):
+        total_of(R("G2", c, c + 1), R("IL", c, 32, step=4), op=MIN)
+    plus("s", R("GG"), R("G2"), -P if rank < N // 2 else 0)
+    ts(R("GI"), R("G2"), float(-P if rank < N // 2 else 0), ADD)
+    tt(R("GM"), R("GG"), R("MH", 0, 2), MUL)
+    ts(R("GJ"), R("GI"), 3, SHR, 0xE0, AND)
+    ga = 4 * ((rank + 2) % 4 if rank < N // 2 else rank)
+    total_of(R("GA", ga, ga + 1), R("GM"))
+    to_all(R("GA", ga, ga + 1), lambda r: R("GA", ga, ga + 1), "ag")
+    for c in range(2):
+        ts(R("HU", c, c + 1), R("GJ", c, c + 1), R("KC", c, c + 1), ADD)
+    mine = [(a, b) for a, b in ((0, HS * rank), (HS * rank + HS, N * HS)) if a < b]
+    for s, sem in (("", "azc"), ("s", "azs")):
+        arrives([R("HW" + s, a, b) for a, b in mine], sem, part)
+    pick("WIN", HS * rank, "HW", 0, N * HS, "HU", 0, 2)
     for s, sem in (("", "awc"), ("s", "aws")):
-        to_each(lambda r: R("WIN2" + s, hc + 16 * r, hc + 16 * r + HS), lambda r: R("WIN2" + s, HS * rank, HS * rank + HS), sem)
-    list_slots(2, K + 128)
-    tt(R("AB"), R("FO"), R("CW8"), MAX)
-    ts(R("LAB2"), R("AB"), 0.0, ADD)
-    list_own(2)
-    list_numbers(2)
+        to_all(R("WIN" + s, HS * rank, HS * rank + HS), lambda r: R("WIN" + s, HS * rank, HS * rank + HS), sem)
+
+    act(R("PF", 1, 2), R("PF", 0, 1), AF.Copy, scale=2.0 ** -17)
+    act(R("PF", 0, 1), R("PF", 0, 1), AF.Copy, scale=2.0 ** -8)
+    plus("s", R("V384"), R("IRB", 0, 64), 384)
+    plus("s", R("V192"), R("IRB", 0, 64), 192)
+    plus("s", R("FR"), R("IRB"), 64)
+    scatter(R("ROW"), R("OU"), R("VR"))
+    dma("y", R("LST", 0, 16), R("ROW", 0, 256, 0, 8))
+    tt(R("OF8"), R("OFF", 0, 8), R("M8"), MUL)
+    ts(R("O2", p1=64), R("D16", 0, 4, 0, 64), 0.0, ADD)
+    total_of(R("OFC"), R("OF8"))
+    ts(R("M16"), R("N16"), Q16, EQL)
+    ts(R("WD"), R("OFC"), 2.0 ** -10, MUL, R("PF", 1, 2), ADD)
+    ts(R("RST"), R("N16"), 0.0, GT)
     quant("WQ", 0, 128, "TW", 0)
+    arrives([R("GA", 4 * c, 4 * c + 1) for c in range(N) if 4 * c != ga], "ag", whole)
+    for c in range(N):
+        if c % 4 == 3:
+            ts(R("GB", 32 * c, 32 * c + 32), R("ONE", 0, 32), R("GA", 4 * c, 4 * c + 1), MUL)
+        else:
+            act(R("GB", 32 * c, 32 * c + 32), R("ONE", 0, 32), AF.Copy, scale=R("GA", 4 * c, 4 * c + 1))
+    tt(R("GT8"), R("GA", 0, 32, step=4), R("M4"), MUL)
+    for k in range(2):
+        total_of(R("GC", k, k + 1), R("GT8", 4 * k, 4 * k + 4))
+    turn(R("GR"), R("GB"))
+    ts(R("MD"), R("GR", 0, 128), R("GC", 0, 1), LT, -0.5, ADD)
+    tt(R("G8"), R("GR", 128 + 8 * rank, 136 + 8 * rank), R("M8B"), MUL)
+    ts(R("ML"), R("GR", 128, 256), R("GC", 1, 2), GE, -0.5, ADD)
+    total_of(R("G1"), R("G8"))
+    ts(R("PLU", 0, 16), R("LST", 0, 16), 0.0, ADD)
+    ts(R("G1I"), R("G1"), 0.0, ADD)
+    ts(R("G1J"), R("G1I"), 5, SHR, 0x38, AND)
+    ts(R("H2U", 0, 1), R("G1J"), R("CC", 4, 5), ADD)
+
     for s, sem in (("", "awc"), ("s", "aws")):
-        arrives([R("WIN2" + s, a, b) for a, b in others], sem, part)
-    renew(2, K + 128 + 2 * P)
+        arrives([R("WIN" + s, a, b) for a, b in mine], sem, whole)
+    dmaq("y", "FW", 128, "WIN", 192, K)
+    dmaq("y", "AW", K, "WIN", 192, K)
+    dmaq("y", "XW", P, "WIN", K, 128)
+    for b in range(4):
+        mm("pD", b, "EC", 128 * b, "WIN", 0, 128, False, True)
+    mm("pA", 0, "UQ", 192, "WIN", K, 128)
+    mm("pB", 0, "WIN", K, "UQ", 192, 128)
+    for b in range(4):
+        copy("sv"[b % 2], R("HT", 256 + b, 512, step=4), R("pD", 512 * b, 512 * b + 64))
+    quant("FW", 0, 128, "HT", 0)
+    mm("pE", 0, "UQ", 0, "FW", 0, 128)
+    mm("pC", 0, "UQ", 0, "WIN", 128, 128)
+    act(R("RD"), R("pA", 0, 128), AF.Abs)
+    act(R("OWN", 0, 1), R("pB", 0, 1), AF.Abs)
+    mm("pB", 0, "WIN", 128, "UQ", 0, 128)
+    act(R("D2"), R("RD"), AF.Sign, bias=R("OWN", 0, 1), scale=-1.0)
+    tt(R("SM64"), R("MO"), R("pE", 64, 128), MUL)
+    for a in range(2):
+        total_of(R("SC", 4 * rank + a, 4 * rank + a + 1), R("SM64", 32 * a, 32 * a + 32), True)
+
+    def new_to_hubs(s, sem):
+        to_each(lambda r: R("FW" + s, K + 8 * r, K + 8 * r + 8), lambda r: R("HW2" + s, 8 * rank, 8 * rank + 8), sem)
+    new_to_hubs("", "anc")
+    to_all(R("SC", 4 * rank, 4 * rank + 2), lambda r: R("SC", 4 * rank, 4 * rank + 2), "asc")
+    new_to_hubs("s", "ans")
+    dmaq("y", "HW2", 8 * rank, "FW", K + 8 * rank, 8)
+    dma("y", None, R("GR", 128, 192, 0, 1), outap=T.lw[0:1, :])
+    dma("y", None, R("GR", 64, 128, 0, 1), outap=T.sw[0:1, :])
+
+    def first_of(what, between=None):
+        ts(R("XB"), R("NK"), R("CNT"), ADD, what, ADD)
+        turn(R("YB"), R("XB"))
+        for c in range(4):
+            total_of(R("PA", c, c + 1), R("YB", 32 * c, 32 * c + 32), True, MIN)
+        for q in range(4):
+            copy("vs"[q % 2], R("PB", p0=32 * q, p1=32 * q + 32), R("PA", p0=other(q), p1=other(q) + 32))
+        if between:
+            between()
+        tt(R("PC"), R("PA"), R("PB"), MIN)
+        for p in (0, 64):
+            copy("vs"[p // 64], R("PD", p0=p, p1=p + 64), R("PC", p0=64 - p, p1=128 - p))
+        tt(R("RES"), R("PC"), R("PD"), MIN)
+
+    tt(R("B2T"), R("D2"), R("MD"), LT)
+    total_of(R("CNT"), R("B2T"))
+    act(R("RL", 64, 128), R("pC", 64, 128), AF.Abs)
+    act(R("OWN", 1, 2, 64, 128), R("pB", 0, 1, 64, 128), AF.Abs)
+    first_of(R("WD"))
+    ts(R("RI"), R("RES"), 2.0 ** 17, MUL)
+    ts(R("RJ"), R("RI"), 127, AND)
+    ts(R("RK"), R("RI"), 7, SHR)
+    ts(R("BU"), R("RJ"), 0.0, ADD)
+    ts(R("O2", p0=64), R("RK", p0=64), 0.0, ADD)
+    pick("B2", 0, "WIN", K, 128, "BU", 0, 4)
+    for b in range(4):
+        mm("pD", b, "EC", 128 * b, "B2", 0, 128, True, False)
+
+    arrives([R("SC", 4 * r, 4 * r + 2) for r in peers], "asc", whole)
+    for a in range(2):
+        total_of(R("S2", a, a + 1), R("SC", a, 32, step=4))
+    act(R("SB", 0, 32), R("ONE", 0, 32), AF.Copy, scale=R("S2", 0, 1))
+    ts(R("SB", 32, 64), R("ONE", 0, 32), R("S2", 1, 2), MUL)
+    for a in range(2):
+        copy("s", R("OWN", 1, 2, 32 * a, 32 * a + 32), R("S2", a, a + 1, 32 * a, 32 * a + 32))
+    turn(R("RL", 0, 64), R("SB"))
+    act(R("D2"), R("RL"), AF.Sign, bias=R("OWN", 1, 2), scale=-1.0)
+    scatter(R("ROW"), R("O2"), R("V384"))
+    dma("y", R("LST", 16, 32), R("ROW", 0, 256, 64, 72))
+    tt(R("B2T"), R("D2"), R("ML"), GT)
+    gather(R("NUM", 0, 64), R("GR", 0, 128), R("BU"))
+    dma("y", None, R("NUM", 0, 64, 0, 1), outap=T.sw[1:2, :])
+    total_of(R("CNT"), R("B2T"))
+    for s, sem in (("", "anc"), ("s", "ans")):
+        arrives([R("HW2" + s, 8 * r, 8 * r + 8) for r in peers], sem, part)
+
+    def hand_on():
+        pick("H2O", 0, "HW2", 0, K, "H2U", 0, 1)
+        for s, sem in (("", "ahc"), ("s", "ahs")):
+            to_all(R("H2O" + s, 0, 8), lambda r: R("AW" + s, 8 * rank, 8 * rank + 8), sem)
+        dmaq("y", "AW", 8 * rank, "H2O", 0, 8)
+    first_of(R("PF", 0, 1), hand_on)
+    ts(R("LU"), R("RES"), 256.0, MUL)
+    pick("N2", 0, "NE", 0, 128, "LU", 0, 4)
+    for b in range(4):
+        mm("pD", b, "EC", 128 * b, "N2", 0, 128, False, True)
+    scatter(R("FR"), R("LU"), R("V192"))
+    tt(R("FM"), R("FR"), R("M16"), MUL)
+    scan(R("FS16"), R("RST"), R("FM"), MUL)
+    for b in range(4):
+        copy("sv"[b % 2], R("HT", 256 + b, 512, step=4), R("pD", 512 * b, 512 * b + 64))
+    ts(R("FU"), R("FS16", 15, 128, step=16), 0.0, ADD)
+    quant("FW", 192, 128, "HT", K)
+    gather(R("NUM", 64, 128), R("GR", 128, 256), R("LU"))
+    dma("y", None, R("NUM", 64, 128, 0, 1), outap=T.lw[1:2, :])
+    pick("LW", P, "FW", 0, 320, "FU", 0, 8)
 
     for h in range(2):
-        mm("pD", h, "WQ", 0, "LX3", 128 * h, 128)
-    dma("y", None, R("LX3", P, 2 * P), outap=T.oc[:, 4 * P:8 * P])
-    for k in range(4):
-        dma("y", None, R("LX3s", P, 2 * P, 32 * k, 32 * k + 4), outap=T.osc[4 * k:4 * k + 4, P:2 * P])
-    arrives([R("NL")], "anum", whole)
-    for t in range(2):
-        total_of(R("RES", t, t + 1), R("NL", t, 14, step=2))
-    tt(R("RES", 2, 4), R("RES", 0, 2), R("NUM"), ADD)
+        pick("LX3", 128 * h, "LW", 0, 384, "PLU", 8 * h, 8 * h + 8)
+        mm(("pA", "pB")[h], 0, "WQ", 0, "LX3", 128 * h, 128)
     dma("y", None, R("LX3", 0, P), outap=T.oc[:, 0:4 * P])
-    for h in range(2):
-        copy("sv"[h], R("YO", 128 * h, 128 * h + 128), R("pD", 512 * h, 512 * h + 128))
     for k in range(4):
         dma("y", None, R("LX3s", 0, P, 32 * k, 32 * k + 4), outap=T.osc[4 * k:4 * k + 4, 0:P])
-    dma("s", None, R("YO", 0, 128), outap=T.y[:, 0:128])
-    for t in range(2):
-        dma("s", None, R("RES", 2 + t, 3 + t, 0, 64), outap=T.lw[t:t + 1, :])
-        dma("s", None, R("RES", 2 + t, 3 + t, 64, 128), outap=T.sw[t:t + 1, :])
-    dma("y", None, R("YO", 128, 256), outap=T.y[:, 128:256])
+    ts(R("PLU", 16, 32), R("LST", 16, 32), 0.0, ADD)
+    for s, sem in (("", "ahc"), ("s", "ahs")):
+        arrives([R("AW" + s, 8 * r, 8 * r + 8) for r in peers], sem, whole)
+    pick("XW", 384, "AW", 0, 128, "LU", 0, 4)
+    for h in range(2):
+        copy("v", R("YO", 128 * h, 128 * h + 128), R(("pA", "pB")[h], 0, 128))
+    dma("y", None, R("YO"), outap=T.y[:, :])
+    pick("LX3", P, "XW", 0, 448, "PLU", 16, 32)
+    dma("y", None, R("LX3", P, 2 * P), outap=T.oc[:, 4 * P:8 * P])
+    for k in range(4):
+        dma("sy"[k % 2], None, R("LX3s", P, 2 * P, 32 * k, 32 * k + 4), outap=T.osc[4 * k:4 * k + 4, P:2 * P])
     for sem in total:
         if known["g"].get(sem, 0) < total[sem]:
             g.wait_ge(T.sem[sem], total[sem])

@@ -6,7 +6,7 @@ PEERS = N - 1
 HS = 4 * K // N
 
 SCRATCH, VIEW = {}, {}
-SEMAPHORES = ["qv", "qs", "qt", "qg", "ls", "aka", "akb", "ai", "azc", "azs", "ag", "awc", "aws", "asc", "anc", "ans", "ahc", "ahs"] + ["d%d" % i for i in range(48)]
+SEMAPHORES = ["qv", "qs", "qt", "qg", "ls", "aka", "akb", "ai", "azc", "azs", "awc", "aws", "asc", "anc", "ans", "ahc", "ahs"] + ["d%d" % i for i in range(48)]
 
 
 def _sb(name, w, d):
@@ -31,27 +31,29 @@ for _n, _w in (("TL", 1024), ("TX", 1024), ("TN", 1024), ("TW", 512), ("U4", 4),
                ("ZB", 128), ("CO", 512), ("WT", 1024), ("ET", 2048), ("EYE", 128), ("CT", 1024), ("OT", 512), ("HT", 768),
                ("MSK", 256), ("DS", 512), ("SEL", 192), ("IRB", 128), ("FR", 128)):
     _sb(_n, _w, "bfloat16")
-_pool("BB", "bfloat16", (("EQK", 256), ("EQL", 256), ("MM", 6 * 224), ("JB", 448), ("MD", 128), ("ML", 128), ("D2", 128), ("B2T", 128),
-                         ("FM", 128), ("FS16", 128), ("JS", 224), ("XOB", 2)))
-_pool("BC", "bfloat16", (("M16", 128), ("RST", 128), ("V192", 64)))
-_pool("FC", "float32", (("CC", 16), ("N16", 128), ("SGN", 32), ("ICT", 128), ("NK", 128), ("KC", 8), ("NKC", 8), ("D16", 16),
-                        ("N32", 64), ("M32", 64), ("M4", 8), ("M8", 8), ("M8B", 8), ("MH", 4), ("VR", 128), ("V384", 64), ("PF", 2),
-                        ("SM", 32), ("R32", 128)))
+_pool("BB", "bfloat16", (("EQK", 256), ("EQL", 256), ("MM", 6 * 224), ("JB", 448), ("MD", 128), ("D2", 128), ("B2T", 128), ("FM", 128),
+                         ("FS16", 128), ("JS", 224), ("XOB", 2), ("CN", 64), ("XB", 256), ("YB", 256), ("SB2", 256), ("WD", 1)))
+_pool("BC", "bfloat16", (("M16", 128), ("RST", 128), ("V192", 64), ("KB", 128), ("R32B", 256), ("PB", 1)))
+_pool("FC", "float32", (("CC", 16), ("N16", 128), ("FLO", 32), ("FHI", 32), ("INI", 3), ("R3D", 128), ("ICT", 128), ("KC", 8), ("NKC", 8),
+                        ("D16", 16), ("N32", 64), ("M32", 64), ("M4", 8), ("M8", 8), ("M8B", 8), ("MH", 8), ("VR", 128), ("V384", 128),
+                        ("SM", 48), ("R32", 128)))
 _pool("FD", "float32", (("AC", 4), ("RLA", 256), ("RXA", 256)))
-_pool("FB", "float32", (("PRD", 256), ("PRE", 256), ("OKC", 4), ("KR", 448), ("KW", 448), ("XC", 2), ("XO", 4), ("XR", 128), ("Y", 128), ("VV", 128),
-                        ("AB", 1024), ("FS", 8), ("XS", 16), ("G2", 2), ("GG", 2), ("GM", 2), ("A16", 16), ("H16", 16), ("PI16", 16), ("OFF", 16),
-                        ("GB", 256), ("GR", 256), ("GT8", 8), ("GC", 2), ("OF8", 8), ("OFC", 1), ("WD", 1), ("RD", 128), ("RL", 128), ("OWN", 2),
-                        ("CNT", 1), ("XB", 128), ("YB", 128), ("PA", 4), ("PB", 4), ("PC", 4), ("PD", 4), ("RES", 4), ("O4", 4), ("O5", 4),
-                        ("O32", 2), ("MO", 64), ("SM64", 64), ("S2", 2), ("SB", 64), ("G8", 8), ("G1", 1), ("NUM", 128)))
-for _n, _w in (("K1a", 1), ("K1b", 1), ("KLa", 7), ("KLb", 7), ("IL", 32), ("GA", 32), ("SC", 32), ("ROW", 384), ("LST", 32), ("YO", 256)):
+_pool("FB", "float32", (("PRD", 257), ("PRE", 257), ("OKC", 4), ("KR", 448), ("KW", 448), ("XC", 2), ("XO", 4), ("XR", 128), ("Y", 128), ("VV", 128),
+                        ("AB", 1024), ("FS", 8), ("XS", 16), ("ILF", 64), ("I32", 32), ("I16", 16), ("GF", 8), ("GM", 8), ("G4", 4), ("GA", 8),
+                        ("A16", 16), ("H16", 16), ("PI16", 16), ("OFF", 16), ("GB", 256), ("GR", 256), ("GT8", 8), ("GC", 2), ("OF8", 8),
+                        ("OFC", 1), ("GOB", 32), ("GO", 32), ("FT", 64), ("FC2", 64), ("CA", 64), ("CF", 64), ("OW2", 1), ("O3", 4), ("VA", 64),
+                        ("RD", 128), ("RL", 128), ("OWN", 2), ("PC", 8), ("RES", 8), ("O4", 4), ("O5", 4), ("O32", 2), ("MO", 64),
+                        ("SM64", 64), ("S2", 2), ("SB", 64), ("G8", 8), ("G1", 1), ("NUM", 128)))
+for _n, _w in (("K1a", 1), ("K1b", 1), ("KLa", 7), ("KLb", 7), ("SC", 36), ("ROW", 384), ("LST", 32), ("YO", 256)):
     _sb(_n, _w, "float32")
 _pool("UB", "uint16", (("ZU", 16), ("HU", 2), ("NU", 8), ("OU", 8), ("BU", 4), ("O2", 4), ("LU", 4), ("FU", 8), ("H2U", 2), ("PLU", 32)))
+_sb("IL", 64, "uint16")
 _sb("PI", 1, "int32")
 _sb("II", 8, "int32")
-_pool("IB", "int32", (("GI", 2), ("GJ", 2), ("AI", 16), ("HI", 16), ("RI", 4), ("RJ", 4), ("RK", 4), ("G1I", 1), ("G1J", 1)))
+_pool("IB", "int32", (("GI", 2), ("GJ", 2), ("AI", 16), ("HI", 16), ("G1I", 1), ("G1J", 1)))
 for _n, _w in (("UQ", 320), ("LX1", 512), ("LX3", 512), ("NQ", 256), ("WQ", 128), ("COQ", 128), ("WTQ", 256), ("EC", 512), ("CQ", 256),
                ("OQ", 128), ("Z", 256), ("HW", 256), ("WIN", 256), ("NE", 128), ("B2", 128), ("N2", 128), ("FW", 320), ("HW2", 64),
-               ("H2O", 16), ("AW", 128), ("LW", 384), ("XW", 448)):
+               ("H2O", 16), ("LW", 384), ("XW", 512)):
     _codes(_n, _w)
 PSUM = {"pA": 1, "pB": 1, "pC": 1, "pD": 4, "pE": 1}
 for _n in PSUM:
@@ -61,6 +63,7 @@ for _n in PSUM:
 ADD, SUB, MUL, MAX, MIN = AluOpType.add, AluOpType.subtract, AluOpType.mult, AluOpType.max, AluOpType.min
 GT, GE, LT, LE, EQL = AluOpType.is_gt, AluOpType.is_ge, AluOpType.is_lt, AluOpType.is_le, AluOpType.is_equal
 AND, SHR = AluOpType.bitwise_and, AluOpType.arith_shift_right
+TINY, LESS = 2.0 ** -120, 1.0 - 2.0 ** -24
 
 
 def R(name, c0=0, c1=None, p0=0, p1=128, step=1):
@@ -158,6 +161,8 @@ def rank_program(g, core, T, topo):
 
     def tt(out, a, b, op):
         run("v", lambda: g.vector.tensor_tensor(A(out), A(a), A(b), op), [a, b], [out])
+        if a[3] != b[3]:
+            waits("v", [out], [])
 
     def ts(out, a, s1, op0, s2=None, op1=None):
         reads = [a] + [s for s in (s1, s2) if isinstance(s, tuple)]
@@ -168,8 +173,9 @@ def rank_program(g, core, T, topo):
         else:
             run("v", lambda: g.vector.tensor_scalar(A(out), A(a), v1, v2, op0, op1), reads, [out])
 
-    def scan(out, a, b, op0):
-        run("v", lambda: g.vector.tensor_tensor_scan(A(out), A(a), A(b), 0.0, op0, ADD), [a, b], [out])
+    def scan(out, a, b, op0, first=None):
+        run("v", lambda: g.vector.tensor_tensor_scan(A(out), A(a), A(b), A(first) if first else 0.0, op0, ADD),
+            [a, b] + ([first] if first else []), [out])
 
     def act(out, in_, f, bias=None, scale=None, acc=None):
         kw = {}
@@ -285,8 +291,13 @@ def rank_program(g, core, T, topo):
     choose(R("MSK", 0, 128), [[1, 128]], GT, -0.5, -1)
     iota(R("IRB"), [[1, 128]], 0, 0)
     for p in (0, 64):
-        fills(R("SGN", p0=p, p1=p + 64), -1.0 if p else 1.0)
-    for i, v in enumerate((1.0, 0.0, 1.0)):
+        fills(R("FLO", p0=p, p1=p + 64), 1.0 if p else LESS)
+        fills(R("FHI", p0=p, p1=p + 64), LESS if p else 1.0)
+        fills(R("INI", 0, 1, p, p + 64), -448.0 if p else 0.0)
+        fills(R("INI", 1, 2, p, p + 64), 4096.0 if p else -4096.0)
+    for pr in ("PRD", "PRE"):
+        fills(R(pr, 256, 257), TINY)
+    for i, v in enumerate((1.0, 0.0, -1.0)):
         fills(R("SEL", 64 * i, 64 * i + 64), v)
     memset(R("ONE"), 1.0)
     memset(R("UT", 512, 768), 0.0)
@@ -359,15 +370,18 @@ def rank_program(g, core, T, topo):
         to_all(R("K1" + n), lambda r: R("KL" + n, slot_at(r), slot_at(r) + 1), "ak" + n)
 
     iota(R("R32"), [[32, 4], [0, 32]], 0, 0)
+    iota(R("R3D"), [[-512, 2], [-32, 2], [0, 32]], 0, 0)
     iota(R("SM", 0, 8), [[16, 8]], 0, 0)
     iota(R("N16"), [[0, 8], [1, 16]], 0, 0)
     iota(R("ROW", 0, 256), [[1, 16], [16, 16]], 0, 0)
-    iota(R("NK"), [[-16, 4], [0, 2], [-1, 16]], 0, 0)
-    iota(R("SM", 8, 16), [[0, 2], [1, 4]], 0, 0)
+    iota(R("KB"), [[16, 4], [0, 2], [1, 16]], 0, 0)
+    iota(R("SM", 8, 12), [[-2, 2], [1, 2]], 2, 0)
+    iota(R("SM", 12, 16), [[1, 4]], 0, 0)
     iota(R("SM", 16, 24), [[-4, 2], [1, 4]], 4, 0)
     iota(R("N32"), [[0, 2], [1, 32]], 0, 0)
-    iota(R("PF", 0, 1), [[0, 1]], 0, 1)
-    iota(R("SM", 24, 28), [[0, 2], [16, 2]], 0, 0)
+    iota(R("SM", 32, 40), [[0, 4], [16, 2]], 0, 0)
+    iota(R("PB"), [[0, 1]], 0, 1)
+    iota(R("R32B"), [[0, 8], [1, 32]], 0, 0)
     for b in range(4):
         c = 512 * (b % 2) + 64 * (b // 2)
         ts(R("OT", b, 512, step=4), R("IRB"), R("pD", c, c + 1), EQL)
@@ -376,17 +390,19 @@ def rank_program(g, core, T, topo):
     for m in range(4):
         for q in range(4):
             s = 64 * (q // 2) + 32 * (m % 2)
-            act(R("OKC", m, m + 1, 32 * q, 32 * q + 32), R("K1" + "aabb"[m], 0, 1, s, s + 32), AF.Copy, scale=-1.0 if q > 1 else 1.0)
+            copy("s", R("OKC", m, m + 1, 32 * q, 32 * q + 32), R("K1" + "aabb"[m], 0, 1, s, s + 32))
     for m in range(2):
         mm("pB", 0, "WTQ", 128 * m, "OQ", 0, 128, m == 0, m == 1)
     quant("NQ", 0, P, "TN", 0)
     for b in (2, 3):
         memset(R("ET", 512 * b, 512 * b + 512), 0.0)
-    act(R("ICT"), R("R32"), AF.Identity, bias=R("CC", 3, 4))
-    act(R("KC"), R("SM", 0, 8), AF.Identity, bias=Q16)
-    act(R("NKC"), R("KC"), AF.Copy, scale=-4096.0)
     for b in range(4):
         copy("s", R("ET", 512 * b + b, 512 * b + 512, step=4), R("EYE"))
+    act(R("INI", 2, 3), R("CC", 3, 4), AF.Copy, scale=-1.0)
+    act(R("ICT", p1=64), R("R32", p1=64), AF.Identity, bias=R("CC", 3, 4, 0, 64))
+    act(R("ICT", p0=64), R("R3D", p0=64), AF.Identity, bias=R("INI", 2, 3, 64))
+    act(R("KC"), R("SM", 0, 8), AF.Identity, bias=Q16)
+    act(R("NKC"), R("KC"), AF.Copy, scale=R("INI", 1, 2))
     memset(R("HT", 0, 256), 0.0)
     memset(R("HT", 512, 768), 0.0)
     quant("EC", 0, 512, "ET", 0)
@@ -407,17 +423,14 @@ def rank_program(g, core, T, topo):
     def spread(t, on_s):
         for s in range(PEERS):
             o, kc = R("KR", 224 * t + 32 * s, 224 * t + 32 * s + 32), R("KL" + "ab"[t], s, s + 1)
+            f = R("FLO" if s < rank else "FHI")
             if s in on_s:
-                act(o, R("SGN"), AF.Copy, scale=kc)
+                act(o, f, AF.Copy, scale=kc)
             else:
-                ts(o, R("SGN"), kc, MUL)
+                ts(o, f, kc, MUL)
 
     def against(u, t, m):
-        own, a = R("OKC", m, m + 1), 224 * t
-        if rank:
-            ts(R("MM", 224 * u, 224 * u + 32 * rank), R("KW", a, a + 32 * rank), own, LE)
-        if rank < PEERS:
-            ts(R("MM", 224 * u + 32 * rank, 224 * u + 224), R("KW", a + 32 * rank, a + 224), own, LT)
+        ts(R("MM", 224 * u, 224 * u + 224), R("KW", 224 * t, 224 * t + 224), R("OKC", m, m + 1), LT)
 
     def other(q):
         return 32 * (q ^ 1)
@@ -425,9 +438,10 @@ def rank_program(g, core, T, topo):
     spread(0, (1, 3, 5))
     turn(R("KW", 0, 224), R("KR", 0, 224))
     spread(1, range(PEERS))
-    for m in (2, 3):
-        against(m, 0, m)
-        act(R("JS"), R("MM", 224 * m, 224 * m + 224), AF.Copy, acc=R("XC", m - 2, m - 1))
+    against(2, 0, 2)
+    act(R("MM", 672, 896), R("KW", 0, 224), AF.Sign, bias=R("OKC", 3, 4), scale=-1.0)
+    act(R("JS"), R("MM", 672, 896), AF.Relu, acc=R("XC", 1, 2))
+    act(R("JS"), R("MM", 448, 672), AF.Copy, acc=R("XC", 0, 1))
     for m in (0, 1):
         against(m, 0, m)
     for q in range(4):
@@ -436,7 +450,7 @@ def rank_program(g, core, T, topo):
     for m in (0, 1):
         against(4 + m, 1, m)
     for m in (0, 1):
-        scan(R("JB", 224 * m, 224 * m + 224), R("MM", 224 * m, 224 * m + 224), R("MM", 224 * (4 + m), 224 * (5 + m)), ADD)
+        scan(R("JB", 224 * m, 224 * m + 224), R("MM", 224 * m, 224 * m + 224), R("MM", 224 * (4 + m), 224 * (5 + m)), ADD, R("INI", 0, 1))
     for q in range(4):
         copy("vs"[q % 2], R("XOB", 0, 2, 32 * q, 32 * q + 32), R("JB", 223, 448, other(q), other(q) + 32, 224))
         if q % 2:
@@ -446,18 +460,21 @@ def rank_program(g, core, T, topo):
         ts(R("XR", 32 * m, 32 * m + 32), R("ICT", 32 * m, 32 * m + 32), R("JB", 224 * m + 223, 224 * m + 224), ADD, R("XOB", m, m + 1), ADD)
     turn(R("Y"), R("XR"))
     tt(R("VV"), R("Y"), R("pB", 0, 128), ADD)
-    for c in range(7, -1, -1):
-        a = R("AB", 128 * c, 128 * c + 16 * c + 16)
-        act(a, R("VV", 0, 16 * c + 16), AF.Abs, bias=R("NKC", c, c + 1), scale=4096.0)
-        total_of(R("FS", c, c + 1), a, op=MIN)
+    for c in (7, 6, 5, 4, 3, 2):
+        act(R("AB", 128 * c, 144 * c + 16), R("VV", 0, 16 * c + 16), AF.Abs, bias=R("NKC", c, c + 1), scale=4096.0)
+    for c in (0, 1):
+        ts(R("AB", 128 * c, 144 * c + 16), R("VV", 0, 16 * c + 16), 4096.0, MUL, R("NKC", c, c + 1), ADD)
+    for c in (0, 1, 7, 6, 5, 4, 3, 2):
+        total_of(R("FS", c, c + 1), R("AB", 128 * c, 144 * c + 16), True, MIN)
+    own = R("IL", 8 * rank, 8 * rank + 8)
+    ts(own, R("FS"), float(base - 1), ADD)
+    to_all(own, lambda r: own, "ai")
     for q, d, s in (("v", 0, 64), ("s", 0, 0), ("v", 64, 0), ("s", 64, 64)):
         plus(q, R("XS", 8 - s // 8, 16 - s // 8, d, d + 64), R("FS", 0, 8, s, s + 64), base - 1 + 4 * s)
-    to_each(lambda r: R("XS", 2 * r, 2 * r + 2), lambda r: R("IL", 4 * rank, 4 * rank + 2), "ai")
     ts(R("ZU"), R("XS"), float(base + 2 * P - 1), MIN, float(-base), ADD)
     pick("Z", 0, "LX1", 0, 2 * P, "ZU", 0, 16)
     for s, sem in (("", "azc"), ("s", "azs")):
         to_each(lambda r: R("Z" + s, HS * r, HS * r + HS), lambda r: R("HW" + s, HS * rank, HS * rank + HS), sem)
-    copy("s", R("IL", 4 * rank, 4 * rank + 2), R("XS", 2 * rank, 2 * rank + 2))
     pick("HW", HS * rank, "LX1", 0, 2 * P, "ZU", 2 * rank, 2 * rank + 2)
 
     ts(R("NU"), R("XS", 8, 16), float(base + P - 1), MIN, float(-base), ADD)
@@ -469,11 +486,11 @@ def rank_program(g, core, T, topo):
     ts(R("HI"), R("AI"), 4, SHR)
     ts(R("A16"), R("AI"), 16.0, MUL)
     ts(R("H16"), R("HI"), -255.0, MUL)
-    ts(R("MH"), R("SM", 24, 28), R("CC", 6, 7), EQL)
+    ts(R("MH"), R("SM", 32, 40), R("CC", 6, 7), EQL)
     tt(R("PI16"), R("A16"), R("H16"), ADD)
     ts(R("O4"), R("XS", 8, 12), float(base + P), LT)
     tt(R("OFF"), R("PI16"), R("D16"), MIN)
-    tt(R("O5"), R("O4"), R("MH"), MUL)
+    tt(R("O5"), R("O4"), R("MH", 0, 4), MUL)
     for p in (0, 64):
         ts(R("OU", p0=p, p1=p + 64), R("OFF", 8 - p // 8, 16 - p // 8, p, p + 64), 0.0, ADD)
     tt(R("O32"), R("O5", 0, 4, step=2), R("O5", 1, 4, step=2), ADD)
@@ -485,18 +502,24 @@ def rank_program(g, core, T, topo):
     for a in (0, 64):
         plus("s", R("VR", a, a + 64, 64), R("IRB", 64 - a, 128 - a, 64), 256)
 
-    arrives([R("IL", 4 * r, 4 * r + 2) for r in peers], "ai", part)
-    for c in range(2):
-        total_of(R("G2", c, c + 1), R("IL", c, 32, step=4), op=MIN)
-    plus("s", R("GG"), R("G2"), -P if rank < N // 2 else 0)
-    ts(R("GI"), R("G2"), float(-P if rank < N // 2 else 0), ADD)
-    tt(R("GM"), R("GG"), R("MH", 0, 2), MUL)
+    arrives([R("IL", 8 * r, 8 * r + 8) for r in peers], "ai", whole)
+    ts(R("ILF"), R("IL"), 0.0, ADD)
+    tt(R("I32"), R("ILF", 0, 32), R("ILF", 32, 64), MIN)
+    tt(R("I16"), R("I32", 0, 16), R("I32", 16, 32), MIN)
+    tt(R("GF"), R("I16", 0, 8), R("I16", 8, 16), MIN)
+    hp, hc = 64 if rank < N // 2 else 0, 2 * (rank % 4)
+    for p in (0, 64):
+        ts(R("GI", p0=p, p1=p + 64), R("GF", hc, hc + 2, hp, hp + 64), 0.0, ADD)
+    tt(R("GM"), R("GF"), R("MH"), MUL)
     ts(R("GJ"), R("GI"), 3, SHR, 0xE0, AND)
-    ga = 4 * ((rank + 2) % 4 if rank < N // 2 else rank)
-    total_of(R("GA", ga, ga + 1), R("GM"))
-    to_all(R("GA", ga, ga + 1), lambda r: R("GA", ga, ga + 1), "ag")
+    tt(R("G4"), R("GM", 0, 8, step=2), R("GM", 1, 8, step=2), ADD)
     for c in range(2):
         ts(R("HU", c, c + 1), R("GJ", c, c + 1), R("KC", c, c + 1), ADD)
+    for d, s in ((0, 64), (0, 0), (64, 0), (64, 64)):
+        copy("s", R("GA", 4 - s // 16, 8 - s // 16, d, d + 64), R("G4", 0, 4, s, s + 64))
+    for c in range(N):
+        b = (c + 2) % 4 if c < 4 else c
+        act(R("GB", 32 * b, 32 * b + 32), R("ONE", 0, 32), AF.Copy, scale=R("GA", c, c + 1))
     mine = [(a, b) for a, b in ((0, HS * rank), (HS * rank + HS, N * HS)) if a < b]
     for s, sem in (("", "azc"), ("s", "azs")):
         arrives([R("HW" + s, a, b) for a, b in mine], sem, part)
@@ -504,44 +527,42 @@ def rank_program(g, core, T, topo):
     for s, sem in (("", "awc"), ("s", "aws")):
         to_all(R("WIN" + s, HS * rank, HS * rank + HS), lambda r: R("WIN" + s, HS * rank, HS * rank + HS), sem)
 
-    act(R("PF", 1, 2), R("PF", 0, 1), AF.Copy, scale=2.0 ** -17)
-    act(R("PF", 0, 1), R("PF", 0, 1), AF.Copy, scale=2.0 ** -8)
-    plus("s", R("V384"), R("IRB", 0, 64), 384)
+    for a in (0, 64):
+        plus("s", R("V384", a, a + 64), R("IRB", 64 - a, 128 - a), 384)
     plus("s", R("V192"), R("IRB", 0, 64), 192)
     plus("s", R("FR"), R("IRB"), 64)
     scatter(R("ROW"), R("OU"), R("VR"))
     dma("y", R("LST", 0, 16), R("ROW", 0, 256, 0, 8))
-    tt(R("OF8"), R("OFF", 0, 8), R("M8"), MUL)
+    tt(R("OF8"), R("PI16", 0, 8), R("M8"), MUL)
     ts(R("O2", p1=64), R("D16", 0, 4, 0, 64), 0.0, ADD)
     total_of(R("OFC"), R("OF8"))
     ts(R("M16"), R("N16"), Q16, EQL)
-    ts(R("WD"), R("OFC"), 2.0 ** -10, MUL, R("PF", 1, 2), ADD)
+    ts(R("WD"), R("OFC"), 0.0, ADD)
+    ts(R("R32B"), R("R32B"), 0.0, GT)
+    memset(R("SC", 32, 36), TINY)
     ts(R("RST"), R("N16"), 0.0, GT)
+    tt(R("GT8"), R("GA"), R("M4"), MUL)
     quant("WQ", 0, 128, "TW", 0)
-    arrives([R("GA", 4 * c, 4 * c + 1) for c in range(N) if 4 * c != ga], "ag", whole)
-    for c in range(N):
-        if c % 4 == 3:
-            ts(R("GB", 32 * c, 32 * c + 32), R("ONE", 0, 32), R("GA", 4 * c, 4 * c + 1), MUL)
-        else:
-            act(R("GB", 32 * c, 32 * c + 32), R("ONE", 0, 32), AF.Copy, scale=R("GA", 4 * c, 4 * c + 1))
-    tt(R("GT8"), R("GA", 0, 32, step=4), R("M4"), MUL)
     for k in range(2):
         total_of(R("GC", k, k + 1), R("GT8", 4 * k, 4 * k + 4))
+    act(R("GOB"), R("ONE", 0, 32), AF.Copy, scale=R("GC", 1, 2))
     turn(R("GR"), R("GB"))
+    turn(R("GO"), R("GOB"))
     ts(R("MD"), R("GR", 0, 128), R("GC", 0, 1), LT, -0.5, ADD)
     tt(R("G8"), R("GR", 128 + 8 * rank, 136 + 8 * rank), R("M8B"), MUL)
-    ts(R("ML"), R("GR", 128, 256), R("GC", 1, 2), GE, -0.5, ADD)
+    ts(R("FC2"), R("GR", 192, 256), R("GC", 1, 2), GE, LESS, MAX)
     total_of(R("G1"), R("G8"))
-    ts(R("PLU", 0, 16), R("LST", 0, 16), 0.0, ADD)
+    for a in range(2):
+        ts(R("FT", 32 * a, 32 * a + 32), R("GO"), R("GA", 4 + a, 5 + a), LE, LESS, MAX)
     ts(R("G1I"), R("G1"), 0.0, ADD)
+    ts(R("PLU", 0, 16), R("LST", 0, 16), 0.0, ADD)
     ts(R("G1J"), R("G1I"), 5, SHR, 0x38, AND)
     ts(R("H2U", 0, 1), R("G1J"), R("CC", 4, 5), ADD)
 
     for s, sem in (("", "awc"), ("s", "aws")):
         arrives([R("WIN" + s, a, b) for a, b in mine], sem, whole)
     dmaq("y", "FW", 128, "WIN", 192, K)
-    dmaq("y", "AW", K, "WIN", 192, K)
-    dmaq("y", "XW", P, "WIN", K, 128)
+    dmaq("y", "XW", P, "WIN", K, 192)
     for b in range(4):
         mm("pD", b, "EC", 128 * b, "WIN", 0, 128, False, True)
     mm("pA", 0, "UQ", 192, "WIN", K, 128)
@@ -558,77 +579,69 @@ def rank_program(g, core, T, topo):
     tt(R("SM64"), R("MO"), R("pE", 64, 128), MUL)
     for a in range(2):
         total_of(R("SC", 4 * rank + a, 4 * rank + a + 1), R("SM64", 32 * a, 32 * a + 32), True)
-
-    def new_to_hubs(s, sem):
-        to_each(lambda r: R("FW" + s, K + 8 * r, K + 8 * r + 8), lambda r: R("HW2" + s, 8 * rank, 8 * rank + 8), sem)
-    new_to_hubs("", "anc")
     to_all(R("SC", 4 * rank, 4 * rank + 2), lambda r: R("SC", 4 * rank, 4 * rank + 2), "asc")
-    new_to_hubs("s", "ans")
+    for s, sem in (("", "anc"), ("s", "ans")):
+        to_each(lambda r: R("FW" + s, K + 8 * r, K + 8 * r + 8), lambda r: R("HW2" + s, 8 * rank, 8 * rank + 8), sem)
     dmaq("y", "HW2", 8 * rank, "FW", K + 8 * rank, 8)
     dma("y", None, R("GR", 128, 192, 0, 1), outap=T.lw[0:1, :])
     dma("y", None, R("GR", 64, 128, 0, 1), outap=T.sw[0:1, :])
 
-    def first_of(what, between=None):
-        ts(R("XB"), R("NK"), R("CNT"), ADD, what, ADD)
-        turn(R("YB"), R("XB"))
-        for c in range(4):
-            total_of(R("PA", c, c + 1), R("YB", 32 * c, 32 * c + 32), True, MIN)
+    def first_of(lst, whats, between):
+        n = len(whats)
+        scan(R("CN"), R("B2T", 0, 64), R("B2T", 64, 128), ADD)
+        for i, what in enumerate(whats):
+            ts(R("XB", 128 * i, 128 * i + 128), R("KB"), R("CN", 63, 64), EQL, what, MUL)
+        turn(R("YB", 0, 128 * n), R("XB", 0, 128 * n))
+        scan(R("SB2", 0, 128 * n), R("R32B", 0, 128 * n), R("YB", 0, 128 * n), MUL)
+        between()
+        tt(R("PC", 0, 4 * n, 0, 64), R("SB2", 31, 128 * n, 0, 64, 32), R("SB2", 31, 128 * n, 64, 128, 32), ADD)
+        tt(R("RES", 0, 4 * n, 0, 32), R("PC", 0, 4 * n, 0, 32), R("PC", 0, 4 * n, 32, 64), ADD)
         for q in range(4):
-            copy("vs"[q % 2], R("PB", p0=32 * q, p1=32 * q + 32), R("PA", p0=other(q), p1=other(q) + 32))
-        if between:
-            between()
-        tt(R("PC"), R("PA"), R("PB"), MIN)
-        for p in (0, 64):
-            copy("vs"[p // 64], R("PD", p0=p, p1=p + 64), R("PC", p0=64 - p, p1=128 - p))
-        tt(R("RES"), R("PC"), R("PD"), MIN)
+            ts(R(lst, p0=32 * q, p1=32 * q + 32), R("RES", 0, 4, 0, 32), 0.0, ADD)
 
     tt(R("B2T"), R("D2"), R("MD"), LT)
-    total_of(R("CNT"), R("B2T"))
-    act(R("RL", 64, 128), R("pC", 64, 128), AF.Abs)
-    act(R("OWN", 1, 2, 64, 128), R("pB", 0, 1, 64, 128), AF.Abs)
-    first_of(R("WD"))
-    ts(R("RI"), R("RES"), 2.0 ** 17, MUL)
-    ts(R("RJ"), R("RI"), 127, AND)
-    ts(R("RK"), R("RI"), 7, SHR)
-    ts(R("BU"), R("RJ"), 0.0, ADD)
-    ts(R("O2", p0=64), R("RK", p0=64), 0.0, ADD)
+    act(R("CA"), R("pC", 64, 128), AF.Abs)
+    act(R("OW2", p0=64), R("pB", 0, 1, 64, 128), AF.Abs)
+    plus("s", R("CF"), R("CA"), TINY)
+    plus("s", R("OWN", 1, 2, 64, 128), R("OW2", p0=64), TINY)
+    first_of("BU", [R("PB"), R("WD")], lambda: tt(R("RL", 64, 128), R("CF"), R("FC2"), MUL))
+    tt(R("O3", p1=32), R("RES", 4, 8, 0, 32), R("D16", 0, 4, 0, 32), MIN)
     pick("B2", 0, "WIN", K, 128, "BU", 0, 4)
     for b in range(4):
         mm("pD", b, "EC", 128 * b, "B2", 0, 128, True, False)
 
     arrives([R("SC", 4 * r, 4 * r + 2) for r in peers], "asc", whole)
     for a in range(2):
-        total_of(R("S2", a, a + 1), R("SC", a, 32, step=4))
-    act(R("SB", 0, 32), R("ONE", 0, 32), AF.Copy, scale=R("S2", 0, 1))
-    ts(R("SB", 32, 64), R("ONE", 0, 32), R("S2", 1, 2), MUL)
+        total_of(R("S2", a, a + 1), R("SC", a, 36, step=4))
     for a in range(2):
+        ts(R("SB", 32 * a, 32 * a + 32), R("FT", 32 * a, 32 * a + 32), R("S2", a, a + 1), MUL)
         copy("s", R("OWN", 1, 2, 32 * a, 32 * a + 32), R("S2", a, a + 1, 32 * a, 32 * a + 32))
     turn(R("RL", 0, 64), R("SB"))
-    act(R("D2"), R("RL"), AF.Sign, bias=R("OWN", 1, 2), scale=-1.0)
-    scatter(R("ROW"), R("O2"), R("V384"))
-    dma("y", R("LST", 16, 32), R("ROW", 0, 256, 64, 72))
-    tt(R("B2T"), R("D2"), R("ML"), GT)
+    ts(R("O2", p0=64, p1=96), R("O3", p1=32), 0.0, ADD)
+    ts(R("B2T"), R("RL"), R("OWN", 1, 2), LT)
+    ts(R("O2", p0=96), R("O3", p1=32), 0.0, ADD)
     gather(R("NUM", 0, 64), R("GR", 0, 128), R("BU"))
     dma("y", None, R("NUM", 0, 64, 0, 1), outap=T.sw[1:2, :])
-    total_of(R("CNT"), R("B2T"))
     for s, sem in (("", "anc"), ("s", "ans")):
         arrives([R("HW2" + s, 8 * r, 8 * r + 8) for r in peers], sem, part)
 
     def hand_on():
         pick("H2O", 0, "HW2", 0, K, "H2U", 0, 1)
         for s, sem in (("", "ahc"), ("s", "ahs")):
-            to_all(R("H2O" + s, 0, 8), lambda r: R("AW" + s, 8 * rank, 8 * rank + 8), sem)
-        dmaq("y", "AW", 8 * rank, "H2O", 0, 8)
-    first_of(R("PF", 0, 1), hand_on)
-    ts(R("LU"), R("RES"), 256.0, MUL)
+            to_all(R("H2O" + s, 0, 8), lambda r: R("XW" + s, 448 + 8 * rank, 456 + 8 * rank), sem)
+        dmaq("y", "XW", 448 + 8 * rank, "H2O", 0, 8)
+    first_of("LU", [R("PB")], hand_on)
     pick("N2", 0, "NE", 0, 128, "LU", 0, 4)
     for b in range(4):
         mm("pD", b, "EC", 128 * b, "N2", 0, 128, False, True)
+    gather(R("VA"), R("V384"), R("LU"))
     scatter(R("FR"), R("LU"), R("V192"))
+    scatter(R("ROW"), R("O2"), R("VA"))
+    dma("y", R("LST", 16, 32), R("ROW", 0, 256, 64, 72))
     tt(R("FM"), R("FR"), R("M16"), MUL)
     scan(R("FS16"), R("RST"), R("FM"), MUL)
     for b in range(4):
-        copy("sv"[b % 2], R("HT", 256 + b, 512, step=4), R("pD", 512 * b, 512 * b + 64))
+        copy("sssv"[b], R("HT", 256 + b, 512, step=4), R("pD", 512 * b, 512 * b + 64))
     ts(R("FU"), R("FS16", 15, 128, step=16), 0.0, ADD)
     quant("FW", 192, 128, "HT", K)
     gather(R("NUM", 64, 128), R("GR", 128, 256), R("LU"))
@@ -643,13 +656,12 @@ def rank_program(g, core, T, topo):
         dma("y", None, R("LX3s", 0, P, 32 * k, 32 * k + 4), outap=T.osc[4 * k:4 * k + 4, 0:P])
     ts(R("PLU", 16, 32), R("LST", 16, 32), 0.0, ADD)
     for s, sem in (("", "ahc"), ("s", "ahs")):
-        arrives([R("AW" + s, 8 * r, 8 * r + 8) for r in peers], sem, whole)
-    pick("XW", 384, "AW", 0, 128, "LU", 0, 4)
-    for h in range(2):
-        copy("v", R("YO", 128 * h, 128 * h + 128), R(("pA", "pB")[h], 0, 128))
-    dma("y", None, R("YO"), outap=T.y[:, :])
-    pick("LX3", P, "XW", 0, 448, "PLU", 16, 32)
+        arrives([R("XW" + s, 448 + 8 * r, 456 + 8 * r) for r in peers], sem, whole)
+    copy("s", R("YO", 0, 128), R("pA", 0, 128))
+    pick("LX3", P, "XW", 0, 512, "PLU", 16, 32)
     dma("y", None, R("LX3", P, 2 * P), outap=T.oc[:, 4 * P:8 * P])
+    copy("v", R("YO", 128, 256), R("pB", 0, 128))
+    dma("y", None, R("YO"), outap=T.y[:, :])
     for k in range(4):
         dma("sy"[k % 2], None, R("LX3s", P, 2 * P, 32 * k, 32 * k + 4), outap=T.osc[4 * k:4 * k + 4, P:2 * P])
     for sem in total:

@@ -32,15 +32,15 @@ for _n, _w in (("TL", 1024), ("TX", 1024), ("TN", 1024), ("TW", 512), ("U4", 4),
                ("MSK", 256), ("DS", 512), ("SEL", 192), ("IRB", 128), ("FR", 128)):
     _sb(_n, _w, "bfloat16")
 _pool("BB", "bfloat16", (("EQK", 256), ("EQL", 256), ("MM", 6 * 224), ("JB", 448), ("MD", 128), ("D2", 128), ("B2T", 128), ("FM", 128),
-                         ("FS16", 128), ("JS", 224), ("XOB", 2), ("CN", 64), ("XB", 256), ("YB", 256), ("SB2", 256), ("WD", 1)))
+                         ("FS16", 128), ("JS", 448), ("XOB", 2), ("CN", 64), ("XB", 256), ("YB", 256), ("SB2", 256), ("WD", 1)))
 _pool("BC", "bfloat16", (("M16", 128), ("RST", 128), ("V192", 64), ("KB", 128), ("R32B", 256), ("PB", 1)))
 _pool("FC", "float32", (("CC", 16), ("N16", 128), ("FLO", 32), ("FHI", 32), ("INI", 3), ("R3D", 128), ("ICT", 128), ("KC", 8), ("NKC", 8),
                         ("D16", 16), ("N32", 64), ("M32", 64), ("M4", 8), ("M8", 8), ("M8B", 8), ("MH", 8), ("VR", 128), ("V384", 128),
                         ("SM", 48), ("R32", 128)))
 _pool("FD", "float32", (("AC", 4), ("RLA", 256), ("RXA", 256)))
 _pool("FB", "float32", (("PRD", 257), ("PRE", 257), ("OKC", 4), ("KR", 448), ("KW", 448), ("XC", 2), ("XO", 4), ("XR", 128), ("Y", 128), ("VV", 128),
-                        ("AB", 1024), ("FS", 8), ("XS", 16), ("ILF", 64), ("I32", 32), ("I16", 16), ("GF", 8), ("GM", 8), ("G4", 4), ("GA", 8),
-                        ("A16", 16), ("H16", 16), ("PI16", 16), ("OFF", 16), ("GB", 256), ("GR", 256), ("GT8", 8), ("GC", 2), ("OF8", 8),
+                        ("AB", 1024), ("FS", 8), ("XS", 16), ("ILF", 64), ("I32", 32), ("I16", 16), ("GF", 8), ("G2", 2), ("GM", 8), ("G4", 4),
+                        ("GA", 8), ("A16", 16), ("H16", 16), ("PI16", 16), ("OFF", 16), ("GB", 256), ("GR", 256), ("GT8", 8), ("GC", 2), ("OF8", 8),
                         ("OFC", 1), ("GOB", 32), ("GO", 32), ("FT", 64), ("FC2", 64), ("CA", 64), ("CF", 64), ("OW2", 1), ("O3", 4), ("VA", 64),
                         ("RD", 128), ("RL", 128), ("OWN", 2), ("PC", 8), ("RES", 8), ("O4", 4), ("O5", 4), ("O32", 2), ("MO", 64),
                         ("SM64", 64), ("S2", 2), ("SB", 64), ("G8", 8), ("G1", 1), ("NUM", 128)))
@@ -254,6 +254,10 @@ def rank_program(g, core, T, topo):
     part = 1
     while 2 * part * PEERS <= len(shared):
         part *= 2
+    far = [r for r in peers if topo.die(T.cores[r]) != topo.die(core)]
+    near = [r for r in peers if r not in far]
+    spare = shared[0::2] + shared[1::2]
+    lanes = {r: spare[part * i:part * i + part] for i, r in enumerate(far + near)}
 
     def slot_at(r):
         return rank if rank < r else rank - 1
@@ -268,8 +272,8 @@ def rank_program(g, core, T, topo):
     def to_each(src, place, sem):
         waits("g", [src(r) for r in peers], [])
         calls = []
-        for i, r in enumerate(peers):
-            calls.append(RemoteDMATransfer(dst_ids=[dst(r)], dma_engine_mask=bits(shared[part * i:part * i + part]), remote_sem=T.sem[sem],
+        for r in peers:
+            calls.append(RemoteDMATransfer(dst_ids=[dst(r)], dma_engine_mask=bits(lanes[r]), remote_sem=T.sem[sem],
                                            srcs=[S8(src(r))], dsts=[S8(place(r))], alu_op=0))
         g.remote_dma_fused(calls, local_sem=T.sem.ls)
         total["ls"] = total.get("ls", 0) + part * PEERS
@@ -290,6 +294,7 @@ def rank_program(g, core, T, topo):
     choose(R("MSK", 128, 256), [[1, 128]], GT, 0.5, -1)
     choose(R("MSK", 0, 128), [[1, 128]], GT, -0.5, -1)
     iota(R("IRB"), [[1, 128]], 0, 0)
+    iota(R("ET", 1024, 2048), [[0, 1024]], 0, 0)
     for p in (0, 64):
         fills(R("FLO", p0=p, p1=p + 64), 1.0 if p else LESS)
         fills(R("FHI", p0=p, p1=p + 64), LESS if p else 1.0)
@@ -303,10 +308,10 @@ def rank_program(g, core, T, topo):
     memset(R("UT", 512, 768), 0.0)
     for i, (op, v) in enumerate(((AND, 15), (SHR, 4), (AND, 63), (AND, 31), (AND, 7), (SHR, 5), (AND, 16))):
         ts(R("II", i, i + 1), R("PI"), v, op)
-    memset(R("CO"), 0.0)
-    for c in (0, 1, 258, 259):
-        memset(R("CO", c, c // 256 * 256 + 256, step=4), 1.0)
     copy("v", R("CC", 0, 7), R("II", 0, 7))
+    memset(R("EYE"), 0.5)
+    for b in range(4):
+        act(R("CO", b, 512, step=4), R("SEL", 64 * (b // 2), 64 * (b // 2) + 128), AF.Abs)
     Q16, TGT = R("CC", 0, 1), R("CC", 2, 3)
     for t in range(4):
         if t < 2:
@@ -321,7 +326,6 @@ def rank_program(g, core, T, topo):
     act(R("CC", 11, 12), TGT, AF.Identity, bias=64.0)
     quant("COQ", 0, 128, "CO", 0)
     quant("LX1", 0, P, "TL", 0)
-    memset(R("EYE"), 0.5)
     choose(R("EYE"), [[-1, 128]], EQL, 0.0, 1)
     iota(R("ET", 0, 1024), [[0, 1024]], 0, 0)
     waits("y", [R("TL")], [])
@@ -394,10 +398,6 @@ def rank_program(g, core, T, topo):
     for m in range(2):
         mm("pB", 0, "WTQ", 128 * m, "OQ", 0, 128, m == 0, m == 1)
     quant("NQ", 0, P, "TN", 0)
-    for b in (2, 3):
-        memset(R("ET", 512 * b, 512 * b + 512), 0.0)
-    for b in range(4):
-        copy("s", R("ET", 512 * b + b, 512 * b + 512, step=4), R("EYE"))
     act(R("INI", 2, 3), R("CC", 3, 4), AF.Copy, scale=-1.0)
     act(R("ICT", p1=64), R("R32", p1=64), AF.Identity, bias=R("CC", 3, 4, 0, 64))
     act(R("ICT", p0=64), R("R3D", p0=64), AF.Identity, bias=R("INI", 2, 3, 64))
@@ -405,7 +405,6 @@ def rank_program(g, core, T, topo):
     act(R("NKC"), R("KC"), AF.Copy, scale=R("INI", 1, 2))
     memset(R("HT", 0, 256), 0.0)
     memset(R("HT", 512, 768), 0.0)
-    quant("EC", 0, 512, "ET", 0)
     for c in (0, 8):
         act(R("D16", c, c + 8), R("KC"), AF.Identity, bias=float(P))
     for c in (256, 320):
@@ -413,7 +412,7 @@ def rank_program(g, core, T, topo):
 
     arrives([R("KLa")], "aka", whole)
     arrives([R("KLb")], "akb", whole)
-    waits("y", [R("KLb")], [])
+    waits("y", [R("KLa"), R("KLb")], [])
     dmaq("y", "LW", 0, "LX1", 0, P)
     dmaq("y", "XW", 0, "LX1", P, P)
     for w in ("B2", "N2"):
@@ -438,10 +437,10 @@ def rank_program(g, core, T, topo):
     spread(0, (1, 3, 5))
     turn(R("KW", 0, 224), R("KR", 0, 224))
     spread(1, range(PEERS))
-    against(2, 0, 2)
-    act(R("MM", 672, 896), R("KW", 0, 224), AF.Sign, bias=R("OKC", 3, 4), scale=-1.0)
-    act(R("JS"), R("MM", 672, 896), AF.Relu, acc=R("XC", 1, 2))
-    act(R("JS"), R("MM", 448, 672), AF.Copy, acc=R("XC", 0, 1))
+    for m in (2, 3):
+        act(R("MM", 224 * m, 224 * m + 224), R("KW", 0, 224), AF.Sign, bias=R("OKC", m, m + 1), scale=-1.0)
+    for m in (2, 3):
+        act(R("JS", 224 * (m - 2), 224 * (m - 1)), R("MM", 224 * m, 224 * m + 224), AF.Relu, acc=R("XC", m - 2, m - 1))
     for m in (0, 1):
         against(m, 0, m)
     for q in range(4):
@@ -473,7 +472,7 @@ def rank_program(g, core, T, topo):
         plus(q, R("XS", 8 - s // 8, 16 - s // 8, d, d + 64), R("FS", 0, 8, s, s + 64), base - 1 + 4 * s)
     ts(R("ZU"), R("XS"), float(base + 2 * P - 1), MIN, float(-base), ADD)
     pick("Z", 0, "LX1", 0, 2 * P, "ZU", 0, 16)
-    for s, sem in (("", "azc"), ("s", "azs")):
+    for s, sem in (("s", "azs"), ("", "azc")):
         to_each(lambda r: R("Z" + s, HS * r, HS * r + HS), lambda r: R("HW" + s, HS * rank, HS * rank + HS), sem)
     pick("HW", HS * rank, "LX1", 0, 2 * P, "ZU", 2 * rank, 2 * rank + 2)
 
@@ -482,82 +481,77 @@ def rank_program(g, core, T, topo):
         ts(R("AI", c, c + 8), R("XS", c, c + 8), float(-a), ADD, 3839.0, MIN)
     pick("NE", 0, "NQ", 0, P, "NU", 0, 8)
     for b in range(4):
-        mm("pD", b, "EC", 128 * b, "NE", 0, 128, True, False)
+        copy("s", R("ET", 512 * b + b, 512 * b + 512, step=4), R("EYE"))
     ts(R("HI"), R("AI"), 4, SHR)
     ts(R("A16"), R("AI"), 16.0, MUL)
     ts(R("H16"), R("HI"), -255.0, MUL)
     ts(R("MH"), R("SM", 32, 40), R("CC", 6, 7), EQL)
     tt(R("PI16"), R("A16"), R("H16"), ADD)
-    ts(R("O4"), R("XS", 8, 12), float(base + P), LT)
     tt(R("OFF"), R("PI16"), R("D16"), MIN)
-    tt(R("O5"), R("O4"), R("MH", 0, 4), MUL)
-    for p in (0, 64):
-        ts(R("OU", p0=p, p1=p + 64), R("OFF", 8 - p // 8, 16 - p // 8, p, p + 64), 0.0, ADD)
-    tt(R("O32"), R("O5", 0, 4, step=2), R("O5", 1, 4, step=2), ADD)
-    for n, src, c in (("M32", R("N32"), 3), ("M8", R("SM", 16, 24), 1), ("M4", R("SM", 8, 16), 5), ("M8B", R("N16", 0, 8), 4)):
-        ts(R(n), src, R("CC", c, c + 1), EQL)
-    for a in range(2):
-        act(R("MO", 32 * a, 32 * a + 32), R("M32", 32 * a, 32 * a + 32), AF.Copy, scale=R("O32", a, a + 1))
     plus("s", R("VR", p1=64), R("IRB", p1=64), 256)
     for a in (0, 64):
         plus("s", R("VR", a, a + 64, 64), R("IRB", 64 - a, 128 - a, 64), 256)
 
     arrives([R("IL", 8 * r, 8 * r + 8) for r in peers], "ai", whole)
-    ts(R("ILF"), R("IL"), 0.0, ADD)
-    tt(R("I32"), R("ILF", 0, 32), R("ILF", 32, 64), MIN)
-    tt(R("I16"), R("I32", 0, 16), R("I32", 16, 32), MIN)
-    tt(R("GF"), R("I16", 0, 8), R("I16", 8, 16), MIN)
     hp, hc = 64 if rank < N // 2 else 0, 2 * (rank % 4)
+    ts(R("ILF"), R("IL"), 0.0, ADD)
+    ts(R("O4"), R("XS", 8, 12), float(base + P), LT)
+    for c in range(2):
+        total_of(R("G2", c, c + 1, hp, hp + 64), R("ILF", hc + c, 64, hp, hp + 64, 8), op=MIN)
+    tt(R("I32"), R("ILF", 0, 32), R("ILF", 32, 64), MIN)
     for p in (0, 64):
-        ts(R("GI", p0=p, p1=p + 64), R("GF", hc, hc + 2, hp, hp + 64), 0.0, ADD)
-    tt(R("GM"), R("GF"), R("MH"), MUL)
+        ts(R("GI", p0=p, p1=p + 64), R("G2", p0=hp, p1=hp + 64), 0.0, ADD)
+    tt(R("I16"), R("I32", 0, 16), R("I32", 16, 32), MIN)
     ts(R("GJ"), R("GI"), 3, SHR, 0xE0, AND)
-    tt(R("G4"), R("GM", 0, 8, step=2), R("GM", 1, 8, step=2), ADD)
+    tt(R("GF"), R("I16", 0, 8), R("I16", 8, 16), MIN)
     for c in range(2):
         ts(R("HU", c, c + 1), R("GJ", c, c + 1), R("KC", c, c + 1), ADD)
+    tt(R("GM"), R("GF"), R("MH"), MUL)
+    tt(R("O5"), R("O4"), R("MH", 0, 4), MUL)
+    tt(R("G4"), R("GM", 0, 8, step=2), R("GM", 1, 8, step=2), ADD)
+    for p in (0, 64):
+        ts(R("OU", p0=p, p1=p + 64), R("OFF", 8 - p // 8, 16 - p // 8, p, p + 64), 0.0, ADD)
+    tt(R("O32"), R("O5", 0, 4, step=2), R("O5", 1, 4, step=2), ADD)
+    for n, src, c in (("M32", R("N32"), 3), ("M8", R("SM", 16, 24), 1), ("M4", R("SM", 8, 16), 5), ("M8B", R("N16", 0, 8), 4), ("M16", R("N16"), 0)):
+        ts(R(n), src, R("CC", c, c + 1), EQL)
+    ts(R("RST"), R("N16"), 0.0, GT)
+    ts(R("R32B"), R("R32B"), 0.0, GT)
+    mine = [(a, b) for a, b in ((0, HS * rank), (HS * rank + HS, N * HS)) if a < b]
+    for s, sem in (("", "azc"), ("s", "azs")):
+        arrives([R("HW" + s, a, b) for a, b in mine], sem, part)
+    pick("WIN", HS * rank, "HW", 0, N * HS, "HU", 0, 2)
+    for s, sem in (("s", "aws"), ("", "awc")):
+        to_all(R("WIN" + s, HS * rank, HS * rank + HS), lambda r: R("WIN" + s, HS * rank, HS * rank + HS), sem)
+
     for d, s in ((0, 64), (0, 0), (64, 0), (64, 64)):
         copy("s", R("GA", 4 - s // 16, 8 - s // 16, d, d + 64), R("G4", 0, 4, s, s + 64))
     for c in range(N):
         b = (c + 2) % 4 if c < 4 else c
         act(R("GB", 32 * b, 32 * b + 32), R("ONE", 0, 32), AF.Copy, scale=R("GA", c, c + 1))
-    mine = [(a, b) for a, b in ((0, HS * rank), (HS * rank + HS, N * HS)) if a < b]
-    for s, sem in (("", "azc"), ("s", "azs")):
-        arrives([R("HW" + s, a, b) for a, b in mine], sem, part)
-    pick("WIN", HS * rank, "HW", 0, N * HS, "HU", 0, 2)
-    for s, sem in (("", "awc"), ("s", "aws")):
-        to_all(R("WIN" + s, HS * rank, HS * rank + HS), lambda r: R("WIN" + s, HS * rank, HS * rank + HS), sem)
-
     for a in (0, 64):
         plus("s", R("V384", a, a + 64), R("IRB", 64 - a, 128 - a), 384)
+    for a in range(2):
+        act(R("MO", 32 * a, 32 * a + 32), R("M32", 32 * a, 32 * a + 32), AF.Copy, scale=R("O32", a, a + 1))
     plus("s", R("V192"), R("IRB", 0, 64), 192)
     plus("s", R("FR"), R("IRB"), 64)
+    quant("EC", 0, 512, "ET", 0)
+    for b in range(4):
+        mm("pD", b, "EC", 128 * b, "NE", 0, 128, True, False)
     scatter(R("ROW"), R("OU"), R("VR"))
     dma("y", R("LST", 0, 16), R("ROW", 0, 256, 0, 8))
-    tt(R("OF8"), R("PI16", 0, 8), R("M8"), MUL)
-    ts(R("O2", p1=64), R("D16", 0, 4, 0, 64), 0.0, ADD)
-    total_of(R("OFC"), R("OF8"))
-    ts(R("M16"), R("N16"), Q16, EQL)
-    ts(R("WD"), R("OFC"), 0.0, ADD)
-    ts(R("R32B"), R("R32B"), 0.0, GT)
-    memset(R("SC", 32, 36), TINY)
-    ts(R("RST"), R("N16"), 0.0, GT)
     tt(R("GT8"), R("GA"), R("M4"), MUL)
-    quant("WQ", 0, 128, "TW", 0)
+    tt(R("OF8"), R("PI16", 0, 8), R("M8"), MUL)
     for k in range(2):
         total_of(R("GC", k, k + 1), R("GT8", 4 * k, 4 * k + 4))
+    total_of(R("OFC"), R("OF8"))
     act(R("GOB"), R("ONE", 0, 32), AF.Copy, scale=R("GC", 1, 2))
     turn(R("GR"), R("GB"))
-    turn(R("GO"), R("GOB"))
+    ts(R("WD"), R("OFC"), 0.0, ADD)
     ts(R("MD"), R("GR", 0, 128), R("GC", 0, 1), LT, -0.5, ADD)
-    tt(R("G8"), R("GR", 128 + 8 * rank, 136 + 8 * rank), R("M8B"), MUL)
-    ts(R("FC2"), R("GR", 192, 256), R("GC", 1, 2), GE, LESS, MAX)
-    total_of(R("G1"), R("G8"))
-    for a in range(2):
-        ts(R("FT", 32 * a, 32 * a + 32), R("GO"), R("GA", 4 + a, 5 + a), LE, LESS, MAX)
-    ts(R("G1I"), R("G1"), 0.0, ADD)
-    ts(R("PLU", 0, 16), R("LST", 0, 16), 0.0, ADD)
-    ts(R("G1J"), R("G1I"), 5, SHR, 0x38, AND)
-    ts(R("H2U", 0, 1), R("G1J"), R("CC", 4, 5), ADD)
+    turn(R("GO"), R("GOB"))
+    memset(R("SC", 32, 36), TINY)
+    ts(R("O2", p1=64), R("D16", 0, 4, 0, 64), 0.0, ADD)
+    quant("WQ", 0, 128, "TW", 0)
 
     for s, sem in (("", "awc"), ("s", "aws")):
         arrives([R("WIN" + s, a, b) for a, b in mine], sem, whole)
@@ -567,9 +561,19 @@ def rank_program(g, core, T, topo):
         mm("pD", b, "EC", 128 * b, "WIN", 0, 128, False, True)
     mm("pA", 0, "UQ", 192, "WIN", K, 128)
     mm("pB", 0, "WIN", K, "UQ", 192, 128)
+    tt(R("G8"), R("GR", 128 + 8 * rank, 136 + 8 * rank), R("M8B"), MUL)
+    ts(R("FC2"), R("GR", 192, 256), R("GC", 1, 2), GE, LESS, MAX)
+    total_of(R("G1"), R("G8"))
     for b in range(4):
         copy("sv"[b % 2], R("HT", 256 + b, 512, step=4), R("pD", 512 * b, 512 * b + 64))
+        if b == 1:
+            ts(R("G1I"), R("G1"), 0.0, ADD)
+            ts(R("PLU", 0, 16), R("LST", 0, 16), 0.0, ADD)
+            ts(R("G1J"), R("G1I"), 5, SHR, 0x38, AND)
     quant("FW", 0, 128, "HT", 0)
+    ts(R("H2U", 0, 1), R("G1J"), R("CC", 4, 5), ADD)
+    for a in range(2):
+        ts(R("FT", 32 * a, 32 * a + 32), R("GO"), R("GA", 4 + a, 5 + a), LE, LESS, MAX)
     mm("pE", 0, "UQ", 0, "FW", 0, 128)
     mm("pC", 0, "UQ", 0, "WIN", 128, 128)
     act(R("RD"), R("pA", 0, 128), AF.Abs)
@@ -658,10 +662,11 @@ def rank_program(g, core, T, topo):
     for s, sem in (("", "ahc"), ("s", "ahs")):
         arrives([R("XW" + s, 448 + 8 * r, 456 + 8 * r) for r in peers], sem, whole)
     copy("s", R("YO", 0, 128), R("pA", 0, 128))
+    dma("s", None, R("YO", 0, 128), outap=T.y[:, 0:128])
     pick("LX3", P, "XW", 0, 512, "PLU", 16, 32)
     dma("y", None, R("LX3", P, 2 * P), outap=T.oc[:, 4 * P:8 * P])
     copy("v", R("YO", 128, 256), R("pB", 0, 128))
-    dma("y", None, R("YO"), outap=T.y[:, :])
+    dma("y", None, R("YO", 128, 256), outap=T.y[:, 128:256])
     for k in range(4):
         dma("sy"[k % 2], None, R("LX3s", P, 2 * P, 32 * k, 32 * k + 4), outap=T.osc[4 * k:4 * k + 4, P:2 * P])
     for sem in total:

@@ -28,22 +28,22 @@ def _pool(name, d, parts):
 
 
 for _n, _w in (("TL", 1024), ("TX", 1024), ("TN", 1024), ("TW", 512), ("U4", 4), ("Z4", 4), ("UT", 1280), ("ONE", 128),
-               ("ZB", 128), ("CO", 512), ("WT", 1024), ("ET", 2048), ("EYE", 128), ("CT", 1024), ("OT", 512), ("HT", 768),
-               ("MSK", 256), ("DS", 512), ("SEL", 192), ("IRB", 128), ("FR", 128)):
+               ("ZB", 128), ("CO", 512), ("WT", 1024), ("ET", 1056), ("EYE", 128), ("CT", 1024), ("OT", 512), ("HT", 512),
+               ("MSK", 256), ("DS", 768), ("SEL", 192), ("IRB", 128), ("FR", 128)):
     _sb(_n, _w, "bfloat16")
 _pool("BB", "bfloat16", (("EQK", 256), ("EQL", 256), ("MM", 6 * 224), ("JB", 448), ("MD", 128), ("D2", 128), ("B2T", 128), ("FM", 128),
                          ("FS16", 128), ("JS", 448), ("XOB", 2), ("CN", 64), ("XB", 256), ("YB", 256), ("SB2", 256), ("WD", 1)))
-_pool("BC", "bfloat16", (("M16", 128), ("RST", 128), ("V192", 64), ("KB", 128), ("R32B", 256), ("PB", 1)))
-_pool("FC", "float32", (("CC", 16), ("N16", 128), ("FLO", 32), ("FHI", 32), ("INI", 3), ("R3D", 128), ("ICT", 128), ("KC", 8), ("NKC", 8),
+_pool("BC", "bfloat16", (("M16", 128), ("RST", 128), ("V128", 64), ("KB", 128), ("R32B", 256), ("PB", 1)))
+_pool("FC", "float32", (("CC", 16), ("N16", 128), ("FLO", 32), ("FHI", 32), ("INI", 3), ("ICT", 128), ("KC", 8), ("NKC", 8),
                         ("D16", 16), ("N32", 64), ("M32", 64), ("M4", 8), ("M8", 8), ("M8B", 8), ("MH", 8), ("VR", 128), ("V384", 128),
-                        ("SM", 48), ("R32", 128)))
+                        ("SM", 48)))
 _pool("FD", "float32", (("AC", 4), ("RLA", 256), ("RXA", 256)))
 _pool("FB", "float32", (("PRD", 257), ("PRE", 257), ("OKC", 4), ("KR", 448), ("KW", 448), ("XC", 2), ("XO", 4), ("XR", 128), ("Y", 128), ("VV", 128),
                         ("AB", 1024), ("FS", 8), ("XS", 16), ("ILF", 64), ("I32", 32), ("I16", 16), ("GF", 8), ("G2", 2), ("GM", 8), ("G4", 4),
                         ("GA", 8), ("A16", 16), ("H16", 16), ("PI16", 16), ("OFF", 16), ("GB", 256), ("GR", 256), ("GT8", 8), ("GC", 2), ("OF8", 8),
-                        ("OFC", 1), ("GOB", 32), ("GO", 32), ("FT", 64), ("FC2", 64), ("CA", 64), ("CF", 64), ("OW2", 1), ("O3", 4), ("VA", 64),
-                        ("RD", 128), ("RL", 128), ("OWN", 2), ("PC", 8), ("RES", 8), ("O4", 4), ("O5", 4), ("O32", 2), ("MO", 64),
-                        ("SM64", 64), ("S2", 2), ("SB", 64), ("G8", 8), ("G1", 1), ("NUM", 128)))
+                        ("OFC", 1), ("JF", 64), ("SG", 128), ("GOB", 32), ("GO", 32), ("FT", 64), ("FC2", 64), ("CA", 64), ("CF", 64), ("OW2", 1),
+                        ("O3", 4), ("VA", 64), ("RD", 128), ("RL", 128), ("OWN", 2), ("PC", 8), ("RES", 8), ("RED", 8), ("O4", 4), ("O5", 4),
+                        ("O32", 2), ("MO", 64), ("SM64", 64), ("S2", 2), ("SB", 64), ("G8", 8), ("G1", 1), ("NUM", 128)))
 for _n, _w in (("K1a", 1), ("K1b", 1), ("KLa", 7), ("KLb", 7), ("SC", 36), ("ROW", 384), ("LST", 32), ("YO", 256)):
     _sb(_n, _w, "float32")
 _pool("UB", "uint16", (("ZU", 16), ("HU", 2), ("NU", 8), ("OU", 8), ("BU", 4), ("O2", 4), ("LU", 4), ("FU", 8), ("H2U", 2), ("PLU", 32)))
@@ -51,8 +51,8 @@ _sb("IL", 64, "uint16")
 _sb("PI", 1, "int32")
 _sb("II", 8, "int32")
 _pool("IB", "int32", (("GI", 2), ("GJ", 2), ("AI", 16), ("HI", 16), ("G1I", 1), ("G1J", 1)))
-for _n, _w in (("UQ", 320), ("LX1", 512), ("LX3", 512), ("NQ", 256), ("WQ", 128), ("COQ", 128), ("WTQ", 256), ("EC", 512), ("CQ", 256),
-               ("OQ", 128), ("Z", 256), ("HW", 256), ("WIN", 256), ("NE", 128), ("B2", 128), ("N2", 128), ("FW", 320), ("HW2", 64),
+for _n, _w in (("UQ", 320), ("LX1", 512), ("LX3", 512), ("NQ", 256), ("COQ", 128), ("WTQ", 256), ("EC", 512), ("CQ", 256),
+               ("OQ", 128), ("Z", 256), ("HW", 256), ("WIN", 256), ("NE", 128), ("BN", 256), ("FW", 256), ("HW2", 64),
                ("H2O", 16), ("LW", 384), ("XW", 512)):
     _codes(_n, _w)
 PSUM = {"pA": 1, "pB": 1, "pC": 1, "pD": 4, "pE": 1}
@@ -204,8 +204,8 @@ def rank_program(g, core, T, topo):
         kw = {"apply_absolute_value": True} if sizes else {}
         run("v", lambda: g.vector.tensor_reduce(A(out), A(in_), AxisListType.X, op, **kw), [in_], [out])
 
-    def quant(out, c, n, tile, e):
-        o, s, i = R(out, c, c + n), R(out + "s", c, c + n), R(tile, 4 * e, 4 * e + 4 * n)
+    def quant(out, c, n, tile, e, shift=0):
+        o, s, i = R(out, c, c + n), R(out + "s", c, c + n), R(tile, 4 * e + shift, 4 * e + shift + 4 * n)
         run("v", lambda: g.vector.quantize_mx(A(o), A(s), A(i)), [i], [o, s])
 
     def mm(ps, b, w, c, x, d, n, start=True, stop=True):
@@ -217,9 +217,12 @@ def rank_program(g, core, T, topo):
         o, i, l = R(out, c, c + 16 * (f - e)), R(win, a, a + width), R(lst, e, f)
         run("v", lambda: g.vector.tensor_copy(A(o).bitcast(dt.uint32), A(i).bitcast(dt.uint32).indirect(A(l))), [i, l], [o])
 
-    def pick_scales(out, c, win, a, width, lst, e, f):
+    def pick_scales(out, c, win, a, width, lst, e, f, q="s"):
         o, i, l = R(out + "s", c, c + 16 * (f - e)), R(win + "s", a, a + width), R(lst, e, f)
-        run("s", lambda: g.scalar.activation(A(o), A(i).indirect(A(l)), AF.Copy), [i, l], [o])
+        if q == "s":
+            run("s", lambda: g.scalar.activation(A(o), A(i).indirect(A(l)), AF.Copy), [i, l], [o])
+        else:
+            run("v", lambda: g.vector.tensor_copy(A(o), A(i).indirect(A(l))), [i, l], [o])
 
     def pick(*a):
         pick_codes(*a)
@@ -248,9 +251,9 @@ def rank_program(g, core, T, topo):
         return DstId(rid=a[0], pnc=a[1])
 
     shared = [e for e in topo.engines(core, T.cores[peers[0]]) if all(e in topo.engines(core, T.cores[r]) for r in peers)]
-    whole = 1
-    while 2 * whole <= len(shared):
-        whole *= 2
+    side = 1
+    while 4 * side <= len(shared):
+        side *= 2
     part = 1
     while 2 * part * PEERS <= len(shared):
         part *= 2
@@ -258,16 +261,18 @@ def rank_program(g, core, T, topo):
     near = [r for r in peers if r not in far]
     spare = shared[0::2] + shared[1::2]
     lanes = {r: spare[part * i:part * i + part] for i, r in enumerate(far + near)}
+    wide = ("awc",)
 
     def slot_at(r):
         return rank if rank < r else rank - 1
 
     def to_all(src, place, sem):
         waits("g", [src], [])
-        t = RemoteDMATransfer(dst_ids=[dst(r) for r in peers], dma_engine_mask=bits(shared[:whole]), remote_sem=T.sem[sem],
-                              srcs=[S8(src)], dsts=[S8(place(r)) for r in peers], alu_op=0)
-        g.remote_dma_fused([t], local_sem=T.sem.ls)
-        total["ls"] = total.get("ls", 0) + whole
+        ways = ((far, spare[:side]), (near, spare[side:2 * side])) if sem in wide else ((peers, spare[:2 * side]),)
+        calls = [RemoteDMATransfer(dst_ids=[dst(r) for r in to], dma_engine_mask=bits(es), remote_sem=T.sem[sem],
+                                   srcs=[S8(src)], dsts=[S8(place(r)) for r in to], alu_op=0) for to, es in ways]
+        g.remote_dma_fused(calls, local_sem=T.sem.ls)
+        total["ls"] = total.get("ls", 0) + 2 * side
 
     def to_each(src, place, sem):
         waits("g", [src(r) for r in peers], [])
@@ -278,7 +283,8 @@ def rank_program(g, core, T, topo):
         g.remote_dma_fused(calls, local_sem=T.sem.ls)
         total["ls"] = total.get("ls", 0) + part * PEERS
 
-    def arrives(regions, sem, per):
+    def arrives(regions, sem, per=None):
+        per = per or (side if sem in wide else 2 * side)
         total[sem] = PEERS * per
         note("remote", [], regions, sem, PEERS * per)
 
@@ -286,7 +292,8 @@ def rank_program(g, core, T, topo):
     dma("y", R("U4"), None, inap=T.u[:, 0:4])
     dma("s", R("Z4"), None, inap=T.z[:, 0:4])
     dma("y", R("TX"), None, inap=T.dm[:, :])
-    dma("y", R("TL"), None, inap=T.lv[:, :])
+    for h in range(2):
+        dma("y", R("TL", 512 * h, 512 * h + 512), None, inap=T.lv[:, 512 * h:512 * h + 512])
     iota(R("PI"), [[0, 1]], 0, 1)
     memset(R("ZB"), 0.0)
     memset(R("MSK", 0, 128), 0.5)
@@ -294,14 +301,9 @@ def rank_program(g, core, T, topo):
     choose(R("MSK", 128, 256), [[1, 128]], GT, 0.5, -1)
     choose(R("MSK", 0, 128), [[1, 128]], GT, -0.5, -1)
     iota(R("IRB"), [[1, 128]], 0, 0)
-    iota(R("ET", 1024, 2048), [[0, 1024]], 0, 0)
     for p in (0, 64):
-        fills(R("FLO", p0=p, p1=p + 64), 1.0 if p else LESS)
-        fills(R("FHI", p0=p, p1=p + 64), LESS if p else 1.0)
         fills(R("INI", 0, 1, p, p + 64), -448.0 if p else 0.0)
         fills(R("INI", 1, 2, p, p + 64), 4096.0 if p else -4096.0)
-    for pr in ("PRD", "PRE"):
-        fills(R(pr, 256, 257), TINY)
     for i, v in enumerate((1.0, 0.0, -1.0)):
         fills(R("SEL", 64 * i, 64 * i + 64), v)
     memset(R("ONE"), 1.0)
@@ -310,8 +312,9 @@ def rank_program(g, core, T, topo):
         ts(R("II", i, i + 1), R("PI"), v, op)
     copy("v", R("CC", 0, 7), R("II", 0, 7))
     memset(R("EYE"), 0.5)
-    for b in range(4):
-        act(R("CO", b, 512, step=4), R("SEL", 64 * (b // 2), 64 * (b // 2) + 128), AF.Abs)
+    for p in (0, 64):
+        memset(R("FLO", p0=p, p1=p + 64), 1.0 if p else LESS)
+        memset(R("FHI", p0=p, p1=p + 64), LESS if p else 1.0)
     Q16, TGT = R("CC", 0, 1), R("CC", 2, 3)
     for t in range(4):
         if t < 2:
@@ -319,45 +322,85 @@ def rank_program(g, core, T, topo):
         else:
             ts(R("UT", 768 + t, 1280, step=4), R("ONE"), R("Z4", t, t + 1), MUL)
         ts(R("UT", t, 512, step=4), R("ONE"), R("U4", t, t + 1), MUL)
+    for b in range(4):
+        act(R("CO", b, 512, step=4), R("SEL", 64 * (b // 2), 64 * (b // 2) + 128), AF.Abs)
     quant("UQ", 0, 320, "UT", 0)
     quant("LX1", P, P, "TX", 0)
     for o, i, m, a in ((8, 0, 1.0, 1.0), (9, 1, 16.0, 0.0), (10, 1, 16.0, 128.0)):
         act(R("CC", o, o + 1), R("CC", i, i + 1), AF.Identity, bias=a / 4096, scale=m / 4096)
     act(R("CC", 11, 12), TGT, AF.Identity, bias=64.0)
     quant("COQ", 0, 128, "CO", 0)
-    quant("LX1", 0, P, "TL", 0)
+    for pr in ("PRD", "PRE"):
+        memset(R(pr, 256, 257), TINY)
+    quant("LX1", 0, 128, "TL", 0)
     choose(R("EYE"), [[-1, 128]], EQL, 0.0, 1)
-    iota(R("ET", 0, 1024), [[0, 1024]], 0, 0)
+    iota(R("SM", 0, 8), [[16, 8]], 0, 0)
+    iota(R("N16"), [[0, 8], [1, 16]], 0, 0)
+    iota(R("SM", 8, 12), [[-2, 2], [1, 2]], 2, 0)
+    iota(R("SM", 12, 16), [[1, 4]], 0, 0)
+    iota(R("SM", 16, 24), [[-4, 2], [1, 4]], 4, 0)
+    iota(R("N32"), [[0, 2], [1, 32]], 0, 0)
+    iota(R("SM", 32, 40), [[0, 4], [16, 2]], 0, 0)
+    iota(R("HT", 256, 512), [[0, 256]], 0, 0)
+    iota(R("PB"), [[0, 1]], 0, 1)
+    iota(R("KB"), [[16, 4], [0, 2], [1, 16]], 0, 0)
     waits("y", [R("TL")], [])
     dma("y", R("TN"), None, inap=T.nz[:, :])
 
-    def compare(typ):
-        bk, d0, m0 = (2, 256, 128) if typ == "X" else (0, 0, 0)
-        lo, le, on = (LT, LE, GT) if typ == "X" else (GT, GE, LT)
-        row = "R%sA" % typ
-        ts(R("CT", 512 + bk, 1024, step=4), R(row, 128, 256), R("AC", bk, bk + 1), le)
-        ts(R("CT", bk + 1, 512, step=4), R(row, 0, 128), R("AC", bk + 1, bk + 2), lo)
-        for h in range(2):
-            tt(R("CT", 513 * h + bk, 512 * h + 512, step=4), R("DS", d0 + 128 * h, d0 + 128 * h + 128), R("MSK", m0, m0 + 128), on)
+    kinds = {"X": (2, 256, 128, LE, GT, (("pE", 0), ("pC", 0))), "L": (0, 0, 0, GE, LT, (("pD", 0), ("pD", 1)))}
 
-    for typ in "XL":
-        c0, bk, row, d0 = (P, 2, "pB", 256) if typ == "X" else (0, 0, "pA", 0)
-        qc = 192 if typ == "X" else 0
-        at = (("pE", 0), ("pC", 0)) if typ == "X" else (("pD", 0), ("pD", 1))
-        mm(row, 0, "UQ", qc, "LX1", c0, P)
-        for h in range(2):
-            mm(at[h][0], at[h][1], "LX1", c0 + 128 * h, "UQ", qc, 128)
-        act(R("R%sA" % typ), R(row, 0, P), AF.Abs)
-        for h in range(2):
-            total_of(R("AC", bk + h, bk + h + 1), R(at[h][0], 512 * at[h][1], 512 * at[h][1] + 1), True)
-        for h in range(2):
-            act(R("DS", d0 + 128 * h, d0 + 128 * h + 128), R("R%sA" % typ, 128 * h, 128 * h + 128), AF.Sign,
-                bias=R("AC", bk + h, bk + h + 1), scale=-1.0)
-        compare(typ)
+    def half(h):
+        mm("pD", 2 + h, "UQ", 0, "LX1", 128 * h, 128)
+        mm("pD", h, "LX1", 128 * h, "UQ", 0, 128)
+
+    def column(typ, h):
+        bk, d0, m0, le, on, at = kinds[typ]
+        total_of(R("AC", bk + h, bk + h + 1), R(at[h][0], 512 * at[h][1], 512 * at[h][1] + 1), True)
+        act(R("DS", d0 + 128 * h, d0 + 128 * h + 128), R("R%sA" % typ, 128 * h, 128 * h + 128), AF.Sign, bias=R("AC", bk + h, bk + h + 1), scale=-1.0)
+
+    def across(typ):
+        bk, d0, m0, le, on, at = kinds[typ]
+        ts(R("CT", 512 + bk, 1024, step=4), R("R%sA" % typ, 128, 256), R("AC", bk, bk + 1), le)
+
+    def back(typ, step):
+        bk, d0, m0, le, on, at = kinds[typ]
+        ds = R("DS", 512 + m0, 640 + m0)
+        if step == 0:
+            act(ds, R("R%sA" % typ, 0, 128), AF.Sign, bias=R("AC", bk + 1, bk + 2), scale=-1.0)
+        else:
+            act(R("CT", bk + 1, 512, step=4), ds, AF.Relu, scale=1.0 if typ == "X" else -1.0)
+
+    def within(typ, h):
+        bk, d0, m0, le, on, at = kinds[typ]
+        tt(R("CT", 513 * h + bk, 512 * h + 512, step=4), R("DS", d0 + 128 * h, d0 + 128 * h + 128), R("MSK", m0, m0 + 128), on)
+
+    mm("pB", 0, "UQ", 192, "LX1", P, P)
+    for h in range(2):
+        mm(("pE", "pC")[h], 0, "LX1", P + 128 * h, "UQ", 192, 128)
+    act(R("RXA"), R("pB", 0, P), AF.Abs)
+    column("X", 0)
+    column("X", 1)
+    across("X")
+    half(0)
+    quant("LX1", 128, 128, "TL", 128)
+    half(1)
+    back("X", 0)
+    within("X", 0)
+    act(R("RLA", 0, 128), R("pD", 1024, 1152), AF.Abs)
+    back("X", 1)
+    column("L", 0)
+    act(R("RLA", 128, 256), R("pD", 1536, 1664), AF.Abs)
+    within("X", 1)
+    column("L", 1)
+    within("L", 0)
+    back("L", 0)
+    across("L")
+    back("L", 1)
+    within("L", 1)
     mm("pC", 0, "UQ", 64, "LX1", 0, P, True, False)
     mm("pC", 0, "UQ", 128, "LX1", P, P, False, True)
-    quant("CQ", 0, P, "CT", 0)
-    for h in range(2):
+    for h in (1, 0):
+        quant("CQ", 128 * h, 128, "CT", 128 * h)
         mm(("pE", "pA")[h], 0, "COQ", 0, "CQ", 128 * h, 128)
     for h in range(2):
         mm("pD", h, "CQ", 128 * h, "COQ", 0, 128)
@@ -365,62 +408,44 @@ def rank_program(g, core, T, topo):
         for b in range(4):
             s0, dc = 0 if b < 2 else 64, 8 + m * (1 + b % 2)
             act(R("WT", 512 * m + b, 512 * m + 512, step=4), R("SEL", s0, s0 + 128), AF.Copy, scale=R("CC", dc, dc + 1))
+    act(R("INI", 2, 3), R("CC", 3, 4), AF.Copy, scale=-1.0)
+    for m in range(4):
+        act(R("ICT", 32 * m, 32 * m + 32, 0, 64), R("ONE", 0, 32, 0, 64), AF.Identity, bias=32.0 * m, scale=R("CC", 3, 4, 0, 64))
+        act(R("ICT", 32 * m, 32 * m + 32, 64), R("ONE", 0, 32, 64), AF.Identity, bias=-32.0 * m - 448.0 * (m // 2), scale=R("INI", 2, 3, 64))
     for n, e, pr, tg in (("a", "EQK", "PRD", TGT), ("b", "EQL", "PRE", R("CC", 11, 12))):
-        for h in range(2):
+        for h in (1, 0):
             ts(R(e, 128 * h, 128 * h + 128), R(("pE", "pA")[h], 0, 128), tg, EQL)
-        for h in range(2):
+        for h in (1, 0):
             tt(R(pr, 128 * h, 128 * h + 128), R(e, 128 * h, 128 * h + 128), R("pC", 128 * h, 128 * h + 128), MUL)
         total_of(R("K1" + n), R(pr), True)
         to_all(R("K1" + n), lambda r: R("KL" + n, slot_at(r), slot_at(r) + 1), "ak" + n)
 
-    iota(R("R32"), [[32, 4], [0, 32]], 0, 0)
-    iota(R("R3D"), [[-512, 2], [-32, 2], [0, 32]], 0, 0)
-    iota(R("SM", 0, 8), [[16, 8]], 0, 0)
-    iota(R("N16"), [[0, 8], [1, 16]], 0, 0)
+    iota(R("ET"), [[0, 1056]], 0, 0)
     iota(R("ROW", 0, 256), [[1, 16], [16, 16]], 0, 0)
-    iota(R("KB"), [[16, 4], [0, 2], [1, 16]], 0, 0)
-    iota(R("SM", 8, 12), [[-2, 2], [1, 2]], 2, 0)
-    iota(R("SM", 12, 16), [[1, 4]], 0, 0)
-    iota(R("SM", 16, 24), [[-4, 2], [1, 4]], 4, 0)
-    iota(R("N32"), [[0, 2], [1, 32]], 0, 0)
-    iota(R("SM", 32, 40), [[0, 4], [16, 2]], 0, 0)
-    iota(R("PB"), [[0, 1]], 0, 1)
     iota(R("R32B"), [[0, 8], [1, 32]], 0, 0)
     for b in range(4):
         c = 512 * (b % 2) + 64 * (b // 2)
         ts(R("OT", b, 512, step=4), R("IRB"), R("pD", c, c + 1), EQL)
+    ts(R("MH"), R("SM", 32, 40), R("CC", 6, 7), EQL)
     quant("OQ", 0, 128, "OT", 0)
     quant("WTQ", 0, 256, "WT", 0)
+    quant("NQ", 0, P, "TN", 0)
     for m in range(4):
         for q in range(4):
             s = 64 * (q // 2) + 32 * (m % 2)
             copy("s", R("OKC", m, m + 1, 32 * q, 32 * q + 32), R("K1" + "aabb"[m], 0, 1, s, s + 32))
     for m in range(2):
         mm("pB", 0, "WTQ", 128 * m, "OQ", 0, 128, m == 0, m == 1)
-    quant("NQ", 0, P, "TN", 0)
-    act(R("INI", 2, 3), R("CC", 3, 4), AF.Copy, scale=-1.0)
-    act(R("ICT", p1=64), R("R32", p1=64), AF.Identity, bias=R("CC", 3, 4, 0, 64))
-    act(R("ICT", p0=64), R("R3D", p0=64), AF.Identity, bias=R("INI", 2, 3, 64))
-    act(R("KC"), R("SM", 0, 8), AF.Identity, bias=Q16)
-    act(R("NKC"), R("KC"), AF.Copy, scale=R("INI", 1, 2))
-    memset(R("HT", 0, 256), 0.0)
-    memset(R("HT", 512, 768), 0.0)
-    for c in (0, 8):
-        act(R("D16", c, c + 8), R("KC"), AF.Identity, bias=float(P))
-    for c in (256, 320):
-        fills(R("ROW", c, c + 64), 0.0)
 
-    arrives([R("KLa")], "aka", whole)
-    arrives([R("KLb")], "akb", whole)
+    arrives([R("KLa")], "aka")
+    arrives([R("KLb")], "akb")
     waits("y", [R("KLa"), R("KLb")], [])
     dmaq("y", "LW", 0, "LX1", 0, P)
     dmaq("y", "XW", 0, "LX1", P, P)
-    for w in ("B2", "N2"):
-        dmaq("y", w, K, "LX1", 0, K)
     dma("y", R("TW"), None, inap=T.w[:, :])
 
-    def spread(t, on_s):
-        for s in range(PEERS):
+    def spread(t, who, on_s):
+        for s in who:
             o, kc = R("KR", 224 * t + 32 * s, 224 * t + 32 * s + 32), R("KL" + "ab"[t], s, s + 1)
             f = R("FLO" if s < rank else "FHI")
             if s in on_s:
@@ -434,22 +459,26 @@ def rank_program(g, core, T, topo):
     def other(q):
         return 32 * (q ^ 1)
 
-    spread(0, (1, 3, 5))
+    spread(0, range(PEERS), (1, 3, 5))
     turn(R("KW", 0, 224), R("KR", 0, 224))
-    spread(1, range(PEERS))
+    spread(1, range(5), range(5))
     for m in (2, 3):
         act(R("MM", 224 * m, 224 * m + 224), R("KW", 0, 224), AF.Sign, bias=R("OKC", m, m + 1), scale=-1.0)
     for m in (2, 3):
         act(R("JS", 224 * (m - 2), 224 * (m - 1)), R("MM", 224 * m, 224 * m + 224), AF.Relu, acc=R("XC", m - 2, m - 1))
+    ts(R("M32"), R("N32"), R("CC", 3, 4), EQL)
     for m in (0, 1):
         against(m, 0, m)
+    spread(1, (5, 6), ())
     for q in range(4):
         copy("s", R("XO", 2, 4, 32 * q, 32 * q + 32), R("XC", 0, 2, other(q), other(q) + 32))
     turn(R("KW", 224, 448), R("KR", 224, 448))
+    ts(R("M8"), R("SM", 16, 24), R("CC", 1, 2), EQL)
     for m in (0, 1):
         against(4 + m, 1, m)
     for m in (0, 1):
         scan(R("JB", 224 * m, 224 * m + 224), R("MM", 224 * m, 224 * m + 224), R("MM", 224 * (4 + m), 224 * (5 + m)), ADD, R("INI", 0, 1))
+    ts(R("M4"), R("SM", 8, 16), R("CC", 5, 6), EQL)
     for q in range(4):
         copy("vs"[q % 2], R("XOB", 0, 2, 32 * q, 32 * q + 32), R("JB", 223, 448, other(q), other(q) + 32, 224))
         if q % 2:
@@ -457,6 +486,9 @@ def rank_program(g, core, T, topo):
             ts(R("XR", 32 * m, 32 * m + 32), R("ICT", 32 * m, 32 * m + 32), R("XC", m - 2, m - 1), ADD, R("XO", m, m + 1), ADD)
     for m in (0, 1):
         ts(R("XR", 32 * m, 32 * m + 32), R("ICT", 32 * m, 32 * m + 32), R("JB", 224 * m + 223, 224 * m + 224), ADD, R("XOB", m, m + 1), ADD)
+    act(R("KC"), R("SM", 0, 8), AF.Identity, bias=Q16)
+    act(R("NKC"), R("KC"), AF.Copy, scale=R("INI", 1, 2))
+    ts(R("M8B"), R("N16", 0, 8), R("CC", 4, 5), EQL)
     turn(R("Y"), R("XR"))
     tt(R("VV"), R("Y"), R("pB", 0, 128), ADD)
     for c in (7, 6, 5, 4, 3, 2):
@@ -471,31 +503,40 @@ def rank_program(g, core, T, topo):
     for q, d, s in (("v", 0, 64), ("s", 0, 0), ("v", 64, 0), ("s", 64, 64)):
         plus(q, R("XS", 8 - s // 8, 16 - s // 8, d, d + 64), R("FS", 0, 8, s, s + 64), base - 1 + 4 * s)
     ts(R("ZU"), R("XS"), float(base + 2 * P - 1), MIN, float(-base), ADD)
-    pick("Z", 0, "LX1", 0, 2 * P, "ZU", 0, 16)
+    ts(R("NU"), R("XS", 8, 16), float(base + P - 1), MIN, float(-base), ADD)
+    for h in range(2):
+        pick_scales("Z", 128 * h, "LX1", 0, 2 * P, "ZU", 8 * h, 8 * h + 8, "vs"[h])
+    for h in range(2):
+        pick_codes("Z", 128 * h, "LX1", 0, 2 * P, "ZU", 8 * h, 8 * h + 8)
     for s, sem in (("s", "azs"), ("", "azc")):
         to_each(lambda r: R("Z" + s, HS * r, HS * r + HS), lambda r: R("HW" + s, HS * rank, HS * rank + HS), sem)
     pick("HW", HS * rank, "LX1", 0, 2 * P, "ZU", 2 * rank, 2 * rank + 2)
 
-    ts(R("NU"), R("XS", 8, 16), float(base + P - 1), MIN, float(-base), ADD)
     for c, a in ((0, base + P), (8, base)):
         ts(R("AI", c, c + 8), R("XS", c, c + 8), float(-a), ADD, 3839.0, MIN)
-    pick("NE", 0, "NQ", 0, P, "NU", 0, 8)
-    for b in range(4):
-        copy("s", R("ET", 512 * b + b, 512 * b + 512, step=4), R("EYE"))
+    for c in (0, 8):
+        act(R("D16", c, c + 8), R("KC"), AF.Identity, bias=float(P))
+    ts(R("O4"), R("XS", 8, 12), float(base + P), LT)
     ts(R("HI"), R("AI"), 4, SHR)
-    ts(R("A16"), R("AI"), 16.0, MUL)
-    ts(R("H16"), R("HI"), -255.0, MUL)
-    ts(R("MH"), R("SM", 32, 40), R("CC", 6, 7), EQL)
-    tt(R("PI16"), R("A16"), R("H16"), ADD)
-    tt(R("OFF"), R("PI16"), R("D16"), MIN)
+    for c in (256, 320):
+        fills(R("ROW", c, c + 64), 0.0)
+    for b in range(2):
+        copy("s", R("ET", 528 * b + 2 + b, 528 * b + 514, step=4), R("EYE"))
     plus("s", R("VR", p1=64), R("IRB", p1=64), 256)
     for a in (0, 64):
         plus("s", R("VR", a, a + 64, 64), R("IRB", 64 - a, 128 - a, 64), 256)
+    fills(R("SC", 32, 36), TINY)
+    act(R("RST"), R("N16"), AF.Sign)
+    for a in (0, 64):
+        plus("s", R("V384", a, a + 64), R("IRB", 64 - a, 128 - a), 384)
+    plus("s", R("V128"), R("IRB", 0, 64), 128)
+    copy("s", R("FR"), R("IRB"))
+    act(R("R32B"), R("R32B"), AF.Sign)
 
-    arrives([R("IL", 8 * r, 8 * r + 8) for r in peers], "ai", whole)
+    arrives([R("IL", 8 * r, 8 * r + 8) for r in peers], "ai")
     hp, hc = 64 if rank < N // 2 else 0, 2 * (rank % 4)
     ts(R("ILF"), R("IL"), 0.0, ADD)
-    ts(R("O4"), R("XS", 8, 12), float(base + P), LT)
+    ts(R("A16"), R("AI"), 16.0, MUL)
     for c in range(2):
         total_of(R("G2", c, c + 1, hp, hp + 64), R("ILF", hc + c, 64, hp, hp + 64, 8), op=MIN)
     tt(R("I32"), R("ILF", 0, 32), R("ILF", 32, 64), MIN)
@@ -507,15 +548,9 @@ def rank_program(g, core, T, topo):
     for c in range(2):
         ts(R("HU", c, c + 1), R("GJ", c, c + 1), R("KC", c, c + 1), ADD)
     tt(R("GM"), R("GF"), R("MH"), MUL)
-    tt(R("O5"), R("O4"), R("MH", 0, 4), MUL)
+    ts(R("H16"), R("HI"), -255.0, MUL)
     tt(R("G4"), R("GM", 0, 8, step=2), R("GM", 1, 8, step=2), ADD)
-    for p in (0, 64):
-        ts(R("OU", p0=p, p1=p + 64), R("OFF", 8 - p // 8, 16 - p // 8, p, p + 64), 0.0, ADD)
-    tt(R("O32"), R("O5", 0, 4, step=2), R("O5", 1, 4, step=2), ADD)
-    for n, src, c in (("M32", R("N32"), 3), ("M8", R("SM", 16, 24), 1), ("M4", R("SM", 8, 16), 5), ("M8B", R("N16", 0, 8), 4), ("M16", R("N16"), 0)):
-        ts(R(n), src, R("CC", c, c + 1), EQL)
-    ts(R("RST"), R("N16"), 0.0, GT)
-    ts(R("R32B"), R("R32B"), 0.0, GT)
+    tt(R("O5"), R("O4"), R("MH", 0, 4), MUL)
     mine = [(a, b) for a, b in ((0, HS * rank), (HS * rank + HS, N * HS)) if a < b]
     for s, sem in (("", "azc"), ("s", "azs")):
         arrives([R("HW" + s, a, b) for a, b in mine], sem, part)
@@ -523,152 +558,170 @@ def rank_program(g, core, T, topo):
     for s, sem in (("s", "aws"), ("", "awc")):
         to_all(R("WIN" + s, HS * rank, HS * rank + HS), lambda r: R("WIN" + s, HS * rank, HS * rank + HS), sem)
 
+    tt(R("PI16"), R("A16"), R("H16"), ADD)
+    pick("NE", 0, "NQ", 0, P, "NU", 0, 8)
+    tt(R("OFF"), R("PI16"), R("D16"), MIN)
+    tt(R("O32"), R("O5", 0, 4, step=2), R("O5", 1, 4, step=2), ADD)
+    for p in (0, 64):
+        ts(R("OU", p0=p, p1=p + 64), R("OFF", 8 - p // 8, 16 - p // 8, p, p + 64), 0.0, ADD)
     for d, s in ((0, 64), (0, 0), (64, 0), (64, 64)):
         copy("s", R("GA", 4 - s // 16, 8 - s // 16, d, d + 64), R("G4", 0, 4, s, s + 64))
     for c in range(N):
         b = (c + 2) % 4 if c < 4 else c
         act(R("GB", 32 * b, 32 * b + 32), R("ONE", 0, 32), AF.Copy, scale=R("GA", c, c + 1))
-    for a in (0, 64):
-        plus("s", R("V384", a, a + 64), R("IRB", 64 - a, 128 - a), 384)
-    for a in range(2):
-        act(R("MO", 32 * a, 32 * a + 32), R("M32", 32 * a, 32 * a + 32), AF.Copy, scale=R("O32", a, a + 1))
-    plus("s", R("V192"), R("IRB", 0, 64), 192)
-    plus("s", R("FR"), R("IRB"), 64)
-    quant("EC", 0, 512, "ET", 0)
-    for b in range(4):
-        mm("pD", b, "EC", 128 * b, "NE", 0, 128, True, False)
-    scatter(R("ROW"), R("OU"), R("VR"))
-    dma("y", R("LST", 0, 16), R("ROW", 0, 256, 0, 8))
     tt(R("GT8"), R("GA"), R("M4"), MUL)
     tt(R("OF8"), R("PI16", 0, 8), R("M8"), MUL)
     for k in range(2):
-        total_of(R("GC", k, k + 1), R("GT8", 4 * k, 4 * k + 4))
-    total_of(R("OFC"), R("OF8"))
+        act(R("JF", 4 * k, 4 * k + 4), R("GT8", 4 * k, 4 * k + 4), AF.Copy, acc=R("GC", k, k + 1))
     act(R("GOB"), R("ONE", 0, 32), AF.Copy, scale=R("GC", 1, 2))
-    turn(R("GR"), R("GB"))
-    ts(R("WD"), R("OFC"), 0.0, ADD)
-    ts(R("MD"), R("GR", 0, 128), R("GC", 0, 1), LT, -0.5, ADD)
+    for b in range(4):
+        if b == 3:
+            turn(R("GR"), R("GB"))
+        quant("EC", 128 * b, 128, "ET", 132 * (b % 2), 2 - b // 2 * 2)
+        mm("pD", b, "EC", 128 * b, "NE", 0, 128, True, False)
+    act(R("JF", 8, 16), R("OF8"), AF.Copy, acc=R("OFC"))
+    act(R("SG"), R("GR", 0, 128), AF.Sign, bias=R("GC", 0, 1), scale=-1.0)
+    copy("s", R("WD"), R("OFC"))
+    act(R("MD"), R("SG"), AF.Copy, scale=0.5)
+    for a in range(2):
+        act(R("MO", 32 * a, 32 * a + 32), R("M32", 32 * a, 32 * a + 32), AF.Copy, scale=R("O32", a, a + 1))
     turn(R("GO"), R("GOB"))
-    memset(R("SC", 32, 36), TINY)
-    ts(R("O2", p1=64), R("D16", 0, 4, 0, 64), 0.0, ADD)
-    quant("WQ", 0, 128, "TW", 0)
+    tt(R("G8"), R("GR", 128 + 8 * rank, 136 + 8 * rank), R("M8B"), MUL)
+    act(R("JF", 16, 24), R("G8"), AF.Copy, acc=R("G1"))
+    scatter(R("ROW"), R("OU"), R("VR"))
 
     for s, sem in (("", "awc"), ("s", "aws")):
-        arrives([R("WIN" + s, a, b) for a, b in mine], sem, whole)
-    dmaq("y", "FW", 128, "WIN", 192, K)
+        arrives([R("WIN" + s, a, b) for a, b in mine], sem)
     dmaq("y", "XW", P, "WIN", K, 192)
+    dma("y", R("LST", 0, 16), R("ROW", 0, 256, 0, 8))
     for b in range(4):
         mm("pD", b, "EC", 128 * b, "WIN", 0, 128, False, True)
     mm("pA", 0, "UQ", 192, "WIN", K, 128)
     mm("pB", 0, "WIN", K, "UQ", 192, 128)
-    tt(R("G8"), R("GR", 128 + 8 * rank, 136 + 8 * rank), R("M8B"), MUL)
     ts(R("FC2"), R("GR", 192, 256), R("GC", 1, 2), GE, LESS, MAX)
-    total_of(R("G1"), R("G8"))
+    ts(R("G1I"), R("G1"), 0.0, ADD)
+    ts(R("M16"), R("N16"), Q16, EQL)
     for b in range(4):
-        copy("sv"[b % 2], R("HT", 256 + b, 512, step=4), R("pD", 512 * b, 512 * b + 64))
+        copy("sv"[b % 2], R("HT", b, 256, step=4), R("pD", 512 * b, 512 * b + 64))
         if b == 1:
-            ts(R("G1I"), R("G1"), 0.0, ADD)
-            ts(R("PLU", 0, 16), R("LST", 0, 16), 0.0, ADD)
             ts(R("G1J"), R("G1I"), 5, SHR, 0x38, AND)
+            ts(R("FT", 0, 32), R("GO"), R("GA", 4, 5), LE, LESS, MAX)
     quant("FW", 0, 128, "HT", 0)
     ts(R("H2U", 0, 1), R("G1J"), R("CC", 4, 5), ADD)
-    for a in range(2):
-        ts(R("FT", 32 * a, 32 * a + 32), R("GO"), R("GA", 4 + a, 5 + a), LE, LESS, MAX)
+    ts(R("FT", 32, 64), R("GO"), R("GA", 5, 6), LE, LESS, MAX)
+    quant("BN", 128, 128, "TW", 0)
     mm("pE", 0, "UQ", 0, "FW", 0, 128)
     mm("pC", 0, "UQ", 0, "WIN", 128, 128)
     act(R("RD"), R("pA", 0, 128), AF.Abs)
     act(R("OWN", 0, 1), R("pB", 0, 1), AF.Abs)
     mm("pB", 0, "WIN", 128, "UQ", 0, 128)
     act(R("D2"), R("RD"), AF.Sign, bias=R("OWN", 0, 1), scale=-1.0)
-    tt(R("SM64"), R("MO"), R("pE", 64, 128), MUL)
-    for a in range(2):
-        total_of(R("SC", 4 * rank + a, 4 * rank + a + 1), R("SM64", 32 * a, 32 * a + 32), True)
+    tt(R("SM64"), R("MO"), R("pE", 0, 64), MUL)
+    act(R("JF", 32, 64), R("SM64", 32, 64), AF.Abs, acc=R("SC", 4 * rank + 1, 4 * rank + 2))
+    total_of(R("SC", 4 * rank, 4 * rank + 1), R("SM64", 0, 32), True)
     to_all(R("SC", 4 * rank, 4 * rank + 2), lambda r: R("SC", 4 * rank, 4 * rank + 2), "asc")
     for s, sem in (("", "anc"), ("s", "ans")):
-        to_each(lambda r: R("FW" + s, K + 8 * r, K + 8 * r + 8), lambda r: R("HW2" + s, 8 * rank, 8 * rank + 8), sem)
-    dmaq("y", "HW2", 8 * rank, "FW", K + 8 * rank, 8)
-    dma("y", None, R("GR", 128, 192, 0, 1), outap=T.lw[0:1, :])
-    dma("y", None, R("GR", 64, 128, 0, 1), outap=T.sw[0:1, :])
+        to_each(lambda r: R("FW" + s, 8 * r, 8 * r + 8), lambda r: R("HW2" + s, 8 * rank, 8 * rank + 8), sem)
+    dmaq("y", "HW2", 8 * rank, "FW", 8 * rank, 8)
 
-    def first_of(lst, whats, between):
+    def first_of(res, whats, fill):
         n = len(whats)
         scan(R("CN"), R("B2T", 0, 64), R("B2T", 64, 128), ADD)
+        fill[0]()
         for i, what in enumerate(whats):
             ts(R("XB", 128 * i, 128 * i + 128), R("KB"), R("CN", 63, 64), EQL, what, MUL)
+        fill[1]()
         turn(R("YB", 0, 128 * n), R("XB", 0, 128 * n))
+        fill[2]()
         scan(R("SB2", 0, 128 * n), R("R32B", 0, 128 * n), R("YB", 0, 128 * n), MUL)
-        between()
+        fill[3]()
         tt(R("PC", 0, 4 * n, 0, 64), R("SB2", 31, 128 * n, 0, 64, 32), R("SB2", 31, 128 * n, 64, 128, 32), ADD)
-        tt(R("RES", 0, 4 * n, 0, 32), R("PC", 0, 4 * n, 0, 32), R("PC", 0, 4 * n, 32, 64), ADD)
-        for q in range(4):
-            ts(R(lst, p0=32 * q, p1=32 * q + 32), R("RES", 0, 4, 0, 32), 0.0, ADD)
+        tt(R(res, 0, 4 * n, 0, 32), R("PC", 0, 4 * n, 0, 32), R("PC", 0, 4 * n, 32, 64), ADD)
+
+    def offsets(lst, res, q):
+        ts(R(lst, p0=32 * q, p1=32 * q + 32), R(res, 0, 4, 0, 32), 0.0, ADD)
+
+    def nothing():
+        return None
 
     tt(R("B2T"), R("D2"), R("MD"), LT)
+    ts(R("O2", p1=64), R("D16", 0, 4, 0, 64), 0.0, ADD)
     act(R("CA"), R("pC", 64, 128), AF.Abs)
     act(R("OW2", p0=64), R("pB", 0, 1, 64, 128), AF.Abs)
     plus("s", R("CF"), R("CA"), TINY)
     plus("s", R("OWN", 1, 2, 64, 128), R("OW2", p0=64), TINY)
-    first_of("BU", [R("PB"), R("WD")], lambda: tt(R("RL", 64, 128), R("CF"), R("FC2"), MUL))
-    tt(R("O3", p1=32), R("RES", 4, 8, 0, 32), R("D16", 0, 4, 0, 32), MIN)
-    pick("B2", 0, "WIN", K, 128, "BU", 0, 4)
-    for b in range(4):
-        mm("pD", b, "EC", 128 * b, "B2", 0, 128, True, False)
+    first_of("RED", [R("PB"), R("WD")], [nothing, nothing, nothing, lambda: tt(R("RL", 64, 128), R("CF"), R("FC2"), MUL)])
 
-    arrives([R("SC", 4 * r, 4 * r + 2) for r in peers], "asc", whole)
+    arrives([R("SC", 4 * r, 4 * r + 2) for r in peers], "asc")
+    offsets("BU", "RED", 0)
+    offsets("BU", "RED", 1)
     for a in range(2):
         total_of(R("S2", a, a + 1), R("SC", a, 36, step=4))
     for a in range(2):
         ts(R("SB", 32 * a, 32 * a + 32), R("FT", 32 * a, 32 * a + 32), R("S2", a, a + 1), MUL)
         copy("s", R("OWN", 1, 2, 32 * a, 32 * a + 32), R("S2", a, a + 1, 32 * a, 32 * a + 32))
+    offsets("BU", "RED", 2)
     turn(R("RL", 0, 64), R("SB"))
-    ts(R("O2", p0=64, p1=96), R("O3", p1=32), 0.0, ADD)
+    offsets("BU", "RED", 3)
     ts(R("B2T"), R("RL"), R("OWN", 1, 2), LT)
-    ts(R("O2", p0=96), R("O3", p1=32), 0.0, ADD)
+    tt(R("O3", p1=32), R("RED", 4, 8, 0, 32), R("D16", 0, 4, 0, 32), MIN)
+    pick_scales("BN", K, "WIN", K, 128, "BU", 0, 4)
     gather(R("NUM", 0, 64), R("GR", 0, 128), R("BU"))
     dma("y", None, R("NUM", 0, 64, 0, 1), outap=T.sw[1:2, :])
+    dmaq("y", "FW", K, "WIN", 192, K)
+    dma("y", None, R("GR", 128, 192, 0, 1), outap=T.lw[0:1, :])
+    dma("y", None, R("GR", 64, 128, 0, 1), outap=T.sw[0:1, :])
     for s, sem in (("", "anc"), ("s", "ans")):
         arrives([R("HW2" + s, 8 * r, 8 * r + 8) for r in peers], sem, part)
+
+    def unpack():
+        pick_codes("BN", K, "WIN", K, 128, "BU", 0, 4)
+        for b in range(4):
+            mm("pD", b, "EC", 128 * b, "BN", K, 128, True, False)
 
     def hand_on():
         pick("H2O", 0, "HW2", 0, K, "H2U", 0, 1)
         for s, sem in (("", "ahc"), ("s", "ahs")):
             to_all(R("H2O" + s, 0, 8), lambda r: R("XW" + s, 448 + 8 * rank, 456 + 8 * rank), sem)
         dmaq("y", "XW", 448 + 8 * rank, "H2O", 0, 8)
-    first_of("LU", [R("PB")], hand_on)
-    pick("N2", 0, "NE", 0, 128, "LU", 0, 4)
+    first_of("RES", [R("PB")], [unpack, lambda: ts(R("O2", p0=64, p1=96), R("O3", p1=32), 0.0, ADD),
+                                lambda: ts(R("O2", p0=96), R("O3", p1=32), 0.0, ADD), hand_on])
+    for q in range(4):
+        offsets("LU", "RES", q)
+
+    pick("BN", 0, "NE", 0, 128, "LU", 0, 4)
     for b in range(4):
-        mm("pD", b, "EC", 128 * b, "N2", 0, 128, False, True)
+        mm("pD", b, "EC", 128 * b, "BN", 0, 128, False, True)
     gather(R("VA"), R("V384"), R("LU"))
-    scatter(R("FR"), R("LU"), R("V192"))
+    scatter(R("FR"), R("LU"), R("V128"))
     scatter(R("ROW"), R("O2"), R("VA"))
     dma("y", R("LST", 16, 32), R("ROW", 0, 256, 64, 72))
     tt(R("FM"), R("FR"), R("M16"), MUL)
+    ts(R("PLU", 0, 16), R("LST", 0, 16), 0.0, ADD)
     scan(R("FS16"), R("RST"), R("FM"), MUL)
     for b in range(4):
-        copy("sssv"[b], R("HT", 256 + b, 512, step=4), R("pD", 512 * b, 512 * b + 64))
+        copy("sssv"[b], R("HT", b, 256, step=4), R("pD", 512 * b, 512 * b + 64))
     ts(R("FU"), R("FS16", 15, 128, step=16), 0.0, ADD)
-    quant("FW", 192, 128, "HT", K)
+    quant("FW", 128, 128, "HT", 0)
     gather(R("NUM", 64, 128), R("GR", 128, 256), R("LU"))
     dma("y", None, R("NUM", 64, 128, 0, 1), outap=T.lw[1:2, :])
-    pick("LW", P, "FW", 0, 320, "FU", 0, 8)
+    pick("LW", P, "FW", 0, 256, "FU", 0, 8)
 
     for h in range(2):
         pick("LX3", 128 * h, "LW", 0, 384, "PLU", 8 * h, 8 * h + 8)
-        mm(("pA", "pB")[h], 0, "WQ", 0, "LX3", 128 * h, 128)
-    dma("y", None, R("LX3", 0, P), outap=T.oc[:, 0:4 * P])
-    for k in range(4):
-        dma("y", None, R("LX3s", 0, P, 32 * k, 32 * k + 4), outap=T.osc[4 * k:4 * k + 4, 0:P])
+        mm(("pA", "pB")[h], 0, "BN", 128, "LX3", 128 * h, 128)
+        dma("y", None, R("LX3", 128 * h, 128 * h + 128), outap=T.oc[:, 512 * h:512 * h + 512])
     ts(R("PLU", 16, 32), R("LST", 16, 32), 0.0, ADD)
     for s, sem in (("", "ahc"), ("s", "ahs")):
-        arrives([R("XW" + s, 448 + 8 * r, 456 + 8 * r) for r in peers], sem, whole)
+        arrives([R("XW" + s, 448 + 8 * r, 456 + 8 * r) for r in peers], sem)
     copy("s", R("YO", 0, 128), R("pA", 0, 128))
-    dma("s", None, R("YO", 0, 128), outap=T.y[:, 0:128])
+    dma("y", None, R("YO", 0, 128), outap=T.y[:, 0:128])
     pick("LX3", P, "XW", 0, 512, "PLU", 16, 32)
     dma("y", None, R("LX3", P, 2 * P), outap=T.oc[:, 4 * P:8 * P])
     copy("v", R("YO", 128, 256), R("pB", 0, 128))
     dma("y", None, R("YO", 128, 256), outap=T.y[:, 128:256])
     for k in range(4):
-        dma("sy"[k % 2], None, R("LX3s", P, 2 * P, 32 * k, 32 * k + 4), outap=T.osc[4 * k:4 * k + 4, P:2 * P])
+        dma("sy"[k % 2], None, R("LX3s", 0, 2 * P, 32 * k, 32 * k + 4), outap=T.osc[4 * k:4 * k + 4, :])
     for sem in total:
         if known["g"].get(sem, 0) < total[sem]:
             g.wait_ge(T.sem[sem], total[sem])

from concourse.bass import DstId, RemoteDMATransfer
from concourse.mybir import dt, AluOpType, AxisListType, ActivationFunctionType as AF

N, P, K = 8, 256, 64
PEERS = N - 1
HS = 4 * K // N

SCRATCH, VIEW = {}, {}
SEMAPHORES = ["qv", "qs", "qt", "qg", "ls", "aka", "akb", "ai", "azc", "azs", "awc", "aws", "asc", "anc", "ans", "ahc", "ahs"] + ["d%d" % i for i in range(48)]


def _sb(name, w, d):
    SCRATCH[name] = ("sbuf", [128, w], d)
    VIEW[name] = (name, 0, w)


def _codes(name, w):
    _sb(name, w, "float8_e4m3fn_x4")
    _sb(name + "s", w, "uint8")


def _pool(name, d, parts):
    at = 0
    for n, w in parts:
        VIEW[n] = (name, at, w)
        at += (w + 15) // 16 * 16
    SCRATCH[name] = ("sbuf", [128, at], d)


for _n, _w in (("TL", 1024), ("TX", 1024), ("TN", 1024), ("TW", 512), ("U4", 4), ("Z4", 4), ("UT", 1280), ("ONE", 128),
               ("ZB", 128), ("CO", 512), ("WT", 1024), ("ET", 1056), ("EYE", 128), ("CT", 1024), ("OT", 512), ("HT", 512),
               ("MSK", 256), ("DS", 768), ("SEL", 192), ("IRB", 128), ("FR", 128)):
    _sb(_n, _w, "bfloat16")
_pool("BB", "bfloat16", (("EQK", 256), ("EQL", 256), ("MM", 6 * 224), ("JB", 448), ("MD", 128), ("D2", 128), ("B2T", 128), ("FM", 128),
                         ("FS16", 128), ("JS", 448), ("XOB", 2), ("CN", 64), ("XB", 256), ("YB", 256), ("SB2", 256), ("WD", 1)))
_pool("BC", "bfloat16", (("M16", 128), ("RST", 128), ("V128", 64), ("KB", 128), ("R32B", 256), ("PB", 1)))
_pool("FC", "float32", (("CC", 16), ("N16", 128), ("FLO", 32), ("FHI", 32), ("INI", 3), ("ICT", 128), ("KC", 8), ("NKC", 8),
                        ("D16", 16), ("N32", 64), ("M32", 64), ("M4", 8), ("M8", 8), ("M8B", 8), ("MH", 8), ("VR", 128), ("V384", 128),
                        ("SM", 48)))
_pool("FD", "float32", (("AC", 4), ("RLA", 256), ("RXA", 256)))
_pool("FB", "float32", (("PRD", 257), ("PRE", 257), ("OKC", 4), ("KR", 448), ("KW", 448), ("XC", 2), ("XO", 4), ("XR", 128), ("Y", 128), ("VV", 128),
                        ("AB", 1024), ("FS", 8), ("XS", 16), ("ILF", 64), ("I32", 32), ("I16", 16), ("GF", 8), ("G2", 2), ("GM", 8), ("G4", 4),
                        ("GA", 8), ("A16", 16), ("H16", 16), ("PI16", 16), ("OFF", 16), ("GB", 256), ("GR", 256), ("GT8", 8), ("GC", 2), ("OF8", 8),
                        ("OFC", 1), ("JF", 64), ("SG", 128), ("GOB", 32), ("GO", 32), ("FT", 64), ("FC2", 64), ("CA", 64), ("CF", 64), ("OW2", 1),
                        ("O3", 4), ("VA", 64), ("RD", 128), ("RL", 128), ("OWN", 2), ("PC", 8), ("RES", 8), ("RED", 8), ("O4", 4), ("O5", 4),
                        ("O32", 2), ("MO", 64), ("SM64", 64), ("S2", 2), ("SB", 64), ("G8", 8), ("G1", 1), ("NUM", 128)))
for _n, _w in (("K1a", 1), ("K1b", 1), ("KLa", 7), ("KLb", 7), ("SC", 36), ("ROW", 384), ("LST", 32), ("YO", 256)):
    _sb(_n, _w, "float32")
_pool("UB", "uint16", (("ZU", 16), ("HU", 2), ("NU", 8), ("OU", 8), ("BU", 4), ("O2", 4), ("LU", 4), ("FU", 8), ("H2U", 2), ("PLU", 32)))
_sb("IL", 64, "uint16")
_sb("PI", 1, "int32")
_sb("II", 8, "int32")
_pool("IB", "int32", (("GI", 2), ("GJ", 2), ("AI", 16), ("HI", 16), ("G1I", 1), ("G1J", 1)))
for _n, _w in (("UQ", 320), ("LX1", 512), ("LX3", 512), ("NQ", 256), ("COQ", 128), ("WTQ", 256), ("EC", 512), ("CQ", 256),
               ("OQ", 128), ("Z", 256), ("HW", 256), ("WIN", 256), ("NE", 128), ("BN", 256), ("FW", 256), ("HW2", 64),
               ("H2O", 16), ("LW", 384), ("XW", 512)):
    _codes(_n, _w)
PSUM = {"pA": 1, "pB": 1, "pC": 1, "pD": 4, "pE": 1}
for _n in PSUM:
    SCRATCH[_n] = ("psum", [128, 512 * PSUM[_n]], "float32")
    VIEW[_n] = (_n, 0, 512 * PSUM[_n])

ADD, SUB, MUL, MAX, MIN = AluOpType.add, AluOpType.subtract, AluOpType.mult, AluOpType.max, AluOpType.min
GT, GE, LT, LE, EQL = AluOpType.is_gt, AluOpType.is_ge, AluOpType.is_lt, AluOpType.is_le, AluOpType.is_equal
AND, SHR = AluOpType.bitwise_and, AluOpType.arith_shift_right
TINY, LESS = 2.0 ** -120, 1.0 - 2.0 ** -24


def R(name, c0=0, c1=None, p0=0, p1=128, step=1):
    buf, at, width = VIEW[name]
    return (buf, at + c0, at + (width if c1 is None else c1), p0, p1, step)


def overlap(a, b):
    if a[4] <= b[3] or b[4] <= a[3] or a[2] <= b[1] or b[2] <= a[1]:
        return False
    return not (a[5] == b[5] and a[5] > 1 and (a[1] - b[1]) % a[5])


def covers(a, b):
    return a[5] == 1 and a[1] <= b[1] and a[2] >= b[2] and a[3] <= b[3] and a[4] >= b[4]


def bank(r):
    return (r[0], r[1] // 512 * 512, (r[2] + 511) // 512 * 512, 0, 128, 1) if r[0] in PSUM else r


def rank_program(g, core, T, topo):
    rank = T.rank_of(core)
    if rank is None:
        return
    peers = [r for r in range(N) if r != rank]
    queues = {"v": g.vector, "s": g.scalar, "t": g.tensor, "g": g, "y": g.sync}
    hist, known, count, total = {}, {q: {} for q in queues}, {q: 0 for q in queues}, {}
    seq, ndma = [0], [0]

    def waits(q, reads, writes, adds=False):
        need = []
        for r in reads:
            b, ps = bank(r), r[0] in PSUM
            for kind, box, tok in hist.get(r[0], []):
                if overlap(b, box) and (kind == "w" or ps and tok[2] != q):
                    need.append(tok)
        for w in writes:
            b = bank(w)
            for kind, box, tok in hist.get(w[0], []):
                if overlap(b, box) and not (adds and tok[2] == q):
                    need.append(tok)
        for tok in sorted(need, key=lambda k: -k[3]):
            if known[q].get(tok[0], 0) < tok[1]:
                queues[q].wait_ge(T.sem[tok[0]], tok[1])
                known[q][tok[0]] = tok[1]
                for s, n in tok[4].items():
                    known[q][s] = max(known[q].get(s, 0), n)

    def note(q, reads, writes, sem, val):
        seq[0] += 1
        tok = (sem, val, q, seq[0], dict(known[q]) if q in known else {})
        for w in writes:
            b = bank(w)
            hist[w[0]] = [h for h in hist.get(w[0], []) if not covers(b, h[1])] + [("w", b, tok)]
        for r in reads:
            hist.setdefault(r[0], []).append(("r", bank(r), tok))

    def run(q, make, reads, writes, adds=False):
        waits(q, reads, writes, adds)
        count[q] += 1
        make().then_inc(T.sem["q" + q], 1)
        total["q" + q] = count[q]
        note(q, reads, writes, "q" + q, count[q])

    def A(r):
        t = T[r[0]]
        rows = slice(None) if (r[3], r[4]) == (0, 128) else slice(r[3], r[4])
        return t[rows, r[1]:r[2]] if r[5] == 1 else t[rows, r[1]:r[2]:r[5]]

    def S8(r):
        return A(r).bitcast(dt.uint8) if SCRATCH[r[0]][2] == "float8_e4m3fn_x4" else A(r)

    def dma(q, out, in_, outap=None, inap=None):
        reads, writes = [in_] if in_ else [], [out] if out else []
        waits(q, reads, writes)
        sem = "d%d" % ndma[0]
        ndma[0] += 1
        queues[q].dma_start(outap if outap is not None else S8(out), inap if inap is not None else S8(in_)).then_inc(T.sem[sem], 16)
        total[sem] = 16
        note(q, reads, writes, sem, 16)

    def dmaq(q, out, c, in_, d, n):
        dma(q, R(out, c, c + n), R(in_, d, d + n))
        dma(q, R(out + "s", c, c + n), R(in_ + "s", d, d + n))

    def memset(r, v):
        run("v", lambda: g.vector.memset(A(r), v), [], [r])

    def copy(q, out, in_):
        if q == "v":
            run("v", lambda: g.vector.tensor_copy(A(out), A(in_)), [in_], [out])
        else:
            run("s", lambda: g.scalar.activation(A(out), A(in_), AF.Copy), [in_], [out])

    def tt(out, a, b, op):
        run("v", lambda: g.vector.tensor_tensor(A(out), A(a), A(b), op), [a, b], [out])
        if a[3] != b[3]:
            waits("v", [out], [])

    def ts(out, a, s1, op0, s2=None, op1=None):
        reads = [a] + [s for s in (s1, s2) if isinstance(s, tuple)]
        v1 = A(s1) if isinstance(s1, tuple) else s1
        v2 = A(s2) if isinstance(s2, tuple) else s2
        if op1 is None:
            run("v", lambda: g.vector.tensor_scalar(A(out), A(a), v1, None, op0), reads, [out])
        else:
            run("v", lambda: g.vector.tensor_scalar(A(out), A(a), v1, v2, op0, op1), reads, [out])

    def scan(out, a, b, op0, first=None):
        run("v", lambda: g.vector.tensor_tensor_scan(A(out), A(a), A(b), A(first) if first else 0.0, op0, ADD),
            [a, b] + ([first] if first else []), [out])

    def act(out, in_, f, bias=None, scale=None, acc=None):
        kw = {}
        if bias is not None:
            kw["bias"] = A(bias) if isinstance(bias, tuple) else bias
        if scale is not None:
            kw["scale"] = A(scale) if isinstance(scale, tuple) else scale
        if acc is not None:
            kw["accum_out"] = A(acc)
        run("s", lambda: g.scalar.activation(A(out), A(in_), f, **kw), [in_] + [x for x in (bias, scale) if isinstance(x, tuple)],
            [out] + ([acc] if acc is not None else []))

    def fills(r, v):
        act(r, R("ZB", 0, r[2] - r[1], r[3], r[4]), AF.Identity, bias=float(v))

    def plus(q, out, in_, v):
        if q == "v":
            ts(out, in_, float(v), ADD)
        else:
            act(out, in_, AF.Identity, bias=float(v))

    def turn(out, in_):
        run("v", lambda: g.vector.transpose(A(out), A(in_)), [in_], [out])

    def total_of(out, in_, sizes=False, op=ADD):
        kw = {"apply_absolute_value": True} if sizes else {}
        run("v", lambda: g.vector.tensor_reduce(A(out), A(in_), AxisListType.X, op, **kw), [in_], [out])

    def quant(out, c, n, tile, e, shift=0):
        o, s, i = R(out, c, c + n), R(out + "s", c, c + n), R(tile, 4 * e + shift, 4 * e + shift + 4 * n)
        run("v", lambda: g.vector.quantize_mx(A(o), A(s), A(i)), [i], [o, s])

    def mm(ps, b, w, c, x, d, n, start=True, stop=True):
        o = R(ps, 512 * b, 512 * b + n)
        l, ls, r, rs = R(w, c, c + 128), R(w + "s", c, c + 128), R(x, d, d + n), R(x + "s", d, d + n)
        run("t", lambda: g.tensor.matmul_mx(A(o), A(l), A(ls), A(r), A(rs), start, stop), [l, ls, r, rs], [o], not start)

    def pick_codes(out, c, win, a, width, lst, e, f):
        o, i, l = R(out, c, c + 16 * (f - e)), R(win, a, a + width), R(lst, e, f)
        run("v", lambda: g.vector.tensor_copy(A(o).bitcast(dt.uint32), A(i).bitcast(dt.uint32).indirect(A(l))), [i, l], [o])

    def pick_scales(out, c, win, a, width, lst, e, f, q="s"):
        o, i, l = R(out + "s", c, c + 16 * (f - e)), R(win + "s", a, a + width), R(lst, e, f)
        if q == "s":
            run("s", lambda: g.scalar.activation(A(o), A(i).indirect(A(l)), AF.Copy), [i, l], [o])
        else:
            run("v", lambda: g.vector.tensor_copy(A(o), A(i).indirect(A(l))), [i, l], [o])

    def pick(*a):
        pick_codes(*a)
        pick_scales(*a)

    def scatter(win, off, vals):
        run("v", lambda: g.vector.tensor_copy(A(win).indirect(A(off)), A(vals)), [vals, off], [win])

    def gather(out, win, off):
        run("s", lambda: g.scalar.activation(A(out), A(win).indirect(A(off)), AF.Copy), [win, off], [out])

    def iota(out, pattern, base, cm):
        if SCRATCH[out[0]][2] == "int32":
            run("g", lambda: g.iota(A(out), pattern, base, cm), [], [out])
        else:
            run("g", lambda: g.iota(A(out), pattern, base, cm, allow_small_or_imprecise_dtypes=True), [], [out])

    def choose(r, pattern, op, fill, cm):
        run("g", lambda: g.affine_select(A(r), A(r), pattern, op, fill, 0, cm), [r], [r])

    def bits(es):
        return sum(1 << e for e in es)

    def dst(r):
        a = topo.addr(T.cores[r])
        return DstId(rid=a[0], pnc=a[1])

    shared = [e for e in topo.engines(core, T.cores[peers[0]]) if all(e in topo.engines(core, T.cores[r]) for r in peers)]
    side = 1
    while 4 * side <= len(shared):
        side *= 2
    part = 1
    while 2 * part * PEERS <= len(shared):
        part *= 2
    far = [r for r in peers if topo.die(T.cores[r]) != topo.die(core)]
    near = [r for r in peers if r not in far]
    spare = shared[0::2] + shared[1::2]
    lanes = {r: spare[part * i:part * i + part] for i, r in enumerate(far + near)}
    wide = ("awc",)

    def slot_at(r):
        return rank if rank < r else rank - 1

    def to_all(src, place, sem):
        waits("g", [src], [])
        ways = ((far, spare[:side]), (near, spare[side:2 * side])) if sem in wide else ((peers, spare[:2 * side]),)
        calls = [RemoteDMATransfer(dst_ids=[dst(r) for r in to], dma_engine_mask=bits(es), remote_sem=T.sem[sem],
                                   srcs=[S8(src)], dsts=[S8(place(r)) for r in to], alu_op=0) for to, es in ways]
        g.remote_dma_fused(calls, local_sem=T.sem.ls)
        total["ls"] = total.get("ls", 0) + 2 * side

    def to_each(src, place, sem):
        waits("g", [src(r) for r in peers], [])
        calls = []
        for r in peers:
            calls.append(RemoteDMATransfer(dst_ids=[dst(r)], dma_engine_mask=bits(lanes[r]), remote_sem=T.sem[sem],
                                           srcs=[S8(src(r))], dsts=[S8(place(r))], alu_op=0))
        g.remote_dma_fused(calls, local_sem=T.sem.ls)
        total["ls"] = total.get("ls", 0) + part * PEERS

    def arrives(regions, sem, per=None):
        per = per or (side if sem in wide else 2 * side)
        total[sem] = PEERS * per
        note("remote", [], regions, sem, PEERS * per)

    base = P * rank
    dma("y", R("U4"), None, inap=T.u[:, 0:4])
    dma("s", R("Z4"), None, inap=T.z[:, 0:4])
    dma("y", R("TX"), None, inap=T.dm[:, :])
    for h in range(2):
        dma("y", R("TL", 512 * h, 512 * h + 512), None, inap=T.lv[:, 512 * h:512 * h + 512])
    iota(R("PI"), [[0, 1]], 0, 1)
    memset(R("ZB"), 0.0)
    memset(R("MSK", 0, 128), 0.5)
    memset(R("MSK", 128, 256), -0.5)
    choose(R("MSK", 128, 256), [[1, 128]], GT, 0.5, -1)
    choose(R("MSK", 0, 128), [[1, 128]], GT, -0.5, -1)
    iota(R("IRB"), [[1, 128]], 0, 0)
    for p in (0, 64):
        fills(R("INI", 0, 1, p, p + 64), -448.0 if p else 0.0)
        fills(R("INI", 1, 2, p, p + 64), 4096.0 if p else -4096.0)
    for i, v in enumerate((1.0, 0.0, -1.0)):
        fills(R("SEL", 64 * i, 64 * i + 64), v)
    memset(R("ONE"), 1.0)
    memset(R("UT", 512, 768), 0.0)
    for i, (op, v) in enumerate(((AND, 15), (SHR, 4), (AND, 63), (AND, 31), (AND, 7), (SHR, 5), (AND, 16))):
        ts(R("II", i, i + 1), R("PI"), v, op)
    copy("v", R("CC", 0, 7), R("II", 0, 7))
    memset(R("EYE"), 0.5)
    for p in (0, 64):
        memset(R("FLO", p0=p, p1=p + 64), 1.0 if p else LESS)
        memset(R("FHI", p0=p, p1=p + 64), LESS if p else 1.0)
    Q16, TGT = R("CC", 0, 1), R("CC", 2, 3)
    for t in range(4):
        if t < 2:
            act(R("UT", 768 + t, 1280, step=4), R("ZB"), AF.Identity, bias=R("Z4", t, t + 1))
        else:
            ts(R("UT", 768 + t, 1280, step=4), R("ONE"), R("Z4", t, t + 1), MUL)
        ts(R("UT", t, 512, step=4), R("ONE"), R("U4", t, t + 1), MUL)
    for b in range(4):
        act(R("CO", b, 512, step=4), R("SEL", 64 * (b // 2), 64 * (b // 2) + 128), AF.Abs)
    quant("UQ", 0, 320, "UT", 0)
    quant("LX1", P, P, "TX", 0)
    for o, i, m, a in ((8, 0, 1.0, 1.0), (9, 1, 16.0, 0.0), (10, 1, 16.0, 128.0)):
        act(R("CC", o, o + 1), R("CC", i, i + 1), AF.Identity, bias=a / 4096, scale=m / 4096)
    act(R("CC", 11, 12), TGT, AF.Identity, bias=64.0)
    quant("COQ", 0, 128, "CO", 0)
    for pr in ("PRD", "PRE"):
        memset(R(pr, 256, 257), TINY)
    quant("LX1", 0, 128, "TL", 0)
    choose(R("EYE"), [[-1, 128]], EQL, 0.0, 1)
    iota(R("SM", 0, 8), [[16, 8]], 0, 0)
    iota(R("N16"), [[0, 8], [1, 16]], 0, 0)
    iota(R("SM", 8, 12), [[-2, 2], [1, 2]], 2, 0)
    iota(R("SM", 12, 16), [[1, 4]], 0, 0)
    iota(R("SM", 16, 24), [[-4, 2], [1, 4]], 4, 0)
    iota(R("N32"), [[0, 2], [1, 32]], 0, 0)
    iota(R("SM", 32, 40), [[0, 4], [16, 2]], 0, 0)
    iota(R("HT", 256, 512), [[0, 256]], 0, 0)
    iota(R("PB"), [[0, 1]], 0, 1)
    iota(R("KB"), [[16, 4], [0, 2], [1, 16]], 0, 0)
    waits("y", [R("TL")], [])
    dma("y", R("TN"), None, inap=T.nz[:, :])

    kinds = {"X": (2, 256, 128, LE, GT, (("pE", 0), ("pC", 0))), "L": (0, 0, 0, GE, LT, (("pD", 0), ("pD", 1)))}

    def half(h):
        mm("pD", 2 + h, "UQ", 0, "LX1", 128 * h, 128)
        mm("pD", h, "LX1", 128 * h, "UQ", 0, 128)

    def column(typ, h):
        bk, d0, m0, le, on, at = kinds[typ]
        total_of(R("AC", bk + h, bk + h + 1), R(at[h][0], 512 * at[h][1], 512 * at[h][1] + 1), True)
        act(R("DS", d0 + 128 * h, d0 + 128 * h + 128), R("R%sA" % typ, 128 * h, 128 * h + 128), AF.Sign, bias=R("AC", bk + h, bk + h + 1), scale=-1.0)

    def across(typ):
        bk, d0, m0, le, on, at = kinds[typ]
        ts(R("CT", 512 + bk, 1024, step=4), R("R%sA" % typ, 128, 256), R("AC", bk, bk + 1), le)

    def back(typ, step):
        bk, d0, m0, le, on, at = kinds[typ]
        ds = R("DS", 512 + m0, 640 + m0)
        if step == 0:
            act(ds, R("R%sA" % typ, 0, 128), AF.Sign, bias=R("AC", bk + 1, bk + 2), scale=-1.0)
        else:
            act(R("CT", bk + 1, 512, step=4), ds, AF.Relu, scale=1.0 if typ == "X" else -1.0)

    def within(typ, h):
        bk, d0, m0, le, on, at = kinds[typ]
        tt(R("CT", 513 * h + bk, 512 * h + 512, step=4), R("DS", d0 + 128 * h, d0 + 128 * h + 128), R("MSK", m0, m0 + 128), on)

    mm("pB", 0, "UQ", 192, "LX1", P, P)
    for h in range(2):
        mm(("pE", "pC")[h], 0, "LX1", P + 128 * h, "UQ", 192, 128)
    act(R("RXA"), R("pB", 0, P), AF.Abs)
    column("X", 0)
    column("X", 1)
    across("X")
    half(0)
    quant("LX1", 128, 128, "TL", 128)
    half(1)
    back("X", 0)
    within("X", 0)
    act(R("RLA", 0, 128), R("pD", 1024, 1152), AF.Abs)
    back("X", 1)
    column("L", 0)
    act(R("RLA", 128, 256), R("pD", 1536, 1664), AF.Abs)
    within("X", 1)
    column("L", 1)
    within("L", 0)
    back("L", 0)
    across("L")
    back("L", 1)
    within("L", 1)
    mm("pC", 0, "UQ", 64, "LX1", 0, P, True, False)
    mm("pC", 0, "UQ", 128, "LX1", P, P, False, True)
    for h in (1, 0):
        quant("CQ", 128 * h, 128, "CT", 128 * h)
        mm(("pE", "pA")[h], 0, "COQ", 0, "CQ", 128 * h, 128)
    for h in range(2):
        mm("pD", h, "CQ", 128 * h, "COQ", 0, 128)
    for m in range(2):
        for b in range(4):
            s0, dc = 0 if b < 2 else 64, 8 + m * (1 + b % 2)
            act(R("WT", 512 * m + b, 512 * m + 512, step=4), R("SEL", s0, s0 + 128), AF.Copy, scale=R("CC", dc, dc + 1))
    act(R("INI", 2, 3), R("CC", 3, 4), AF.Copy, scale=-1.0)
    for m in range(4):
        act(R("ICT", 32 * m, 32 * m + 32, 0, 64), R("ONE", 0, 32, 0, 64), AF.Identity, bias=32.0 * m, scale=R("CC", 3, 4, 0, 64))
        act(R("ICT", 32 * m, 32 * m + 32, 64), R("ONE", 0, 32, 64), AF.Identity, bias=-32.0 * m - 448.0 * (m // 2), scale=R("INI", 2, 3, 64))
    for n, e, pr, tg in (("a", "EQK", "PRD", TGT), ("b", "EQL", "PRE", R("CC", 11, 12))):
        for h in (1, 0):
            ts(R(e, 128 * h, 128 * h + 128), R(("pE", "pA")[h], 0, 128), tg, EQL)
        for h in (1, 0):
            tt(R(pr, 128 * h, 128 * h + 128), R(e, 128 * h, 128 * h + 128), R("pC", 128 * h, 128 * h + 128), MUL)
        total_of(R("K1" + n), R(pr), True)
        to_all(R("K1" + n), lambda r: R("KL" + n, slot_at(r), slot_at(r) + 1), "ak" + n)

    iota(R("ET"), [[0, 1056]], 0, 0)
    iota(R("ROW", 0, 256), [[1, 16], [16, 16]], 0, 0)
    iota(R("R32B"), [[0, 8], [1, 32]], 0, 0)
    for b in range(4):
        c = 512 * (b % 2) + 64 * (b // 2)
        ts(R("OT", b, 512, step=4), R("IRB"), R("pD", c, c + 1), EQL)
    ts(R("MH"), R("SM", 32, 40), R("CC", 6, 7), EQL)
    quant("OQ", 0, 128, "OT", 0)
    quant("WTQ", 0, 256, "WT", 0)
    quant("NQ", 0, P, "TN", 0)
    for m in range(4):
        for q in range(4):
            s = 64 * (q // 2) + 32 * (m % 2)
            copy("s", R("OKC", m, m + 1, 32 * q, 32 * q + 32), R("K1" + "aabb"[m], 0, 1, s, s + 32))
    for m in range(2):
        mm("pB", 0, "WTQ", 128 * m, "OQ", 0, 128, m == 0, m == 1)

    arrives([R("KLa")], "aka")
    arrives([R("KLb")], "akb")
    waits("y", [R("KLa"), R("KLb")], [])
    dmaq("y", "LW", 0, "LX1", 0, P)
    dmaq("y", "XW", 0, "LX1", P, P)
    dma("y", R("TW"), None, inap=T.w[:, :])

    def spread(t, who, on_s):
        for s in who:
            o, kc = R("KR", 224 * t + 32 * s, 224 * t + 32 * s + 32), R("KL" + "ab"[t], s, s + 1)
            f = R("FLO" if s < rank else "FHI")
            if s in on_s:
                act(o, f, AF.Copy, scale=kc)
            else:
                ts(o, f, kc, MUL)

    def against(u, t, m):
        ts(R("MM", 224 * u, 224 * u + 224), R("KW", 224 * t, 224 * t + 224), R("OKC", m, m + 1), LT)

    def other(q):
        return 32 * (q ^ 1)

    spread(0, range(PEERS), (1, 3, 5))
    turn(R("KW", 0, 224), R("KR", 0, 224))
    spread(1, range(5), range(5))
    for m in (2, 3):
        act(R("MM", 224 * m, 224 * m + 224), R("KW", 0, 224), AF.Sign, bias=R("OKC", m, m + 1), scale=-1.0)
    for m in (2, 3):
        act(R("JS", 224 * (m - 2), 224 * (m - 1)), R("MM", 224 * m, 224 * m + 224), AF.Relu, acc=R("XC", m - 2, m - 1))
    ts(R("M32"), R("N32"), R("CC", 3, 4), EQL)
    for m in (0, 1):
        against(m, 0, m)
    spread(1, (5, 6), ())
    for q in range(4):
        copy("s", R("XO", 2, 4, 32 * q, 32 * q + 32), R("XC", 0, 2, other(q), other(q) + 32))
    turn(R("KW", 224, 448), R("KR", 224, 448))
    ts(R("M8"), R("SM", 16, 24), R("CC", 1, 2), EQL)
    for m in (0, 1):
        against(4 + m, 1, m)
    for m in (0, 1):
        scan(R("JB", 224 * m, 224 * m + 224), R("MM", 224 * m, 224 * m + 224), R("MM", 224 * (4 + m), 224 * (5 + m)), ADD, R("INI", 0, 1))
    ts(R("M4"), R("SM", 8, 16), R("CC", 5, 6), EQL)
    for q in range(4):
        copy("vs"[q % 2], R("XOB", 0, 2, 32 * q, 32 * q + 32), R("JB", 223, 448, other(q), other(q) + 32, 224))
        if q % 2:
            m = 2 + q // 2
            ts(R("XR", 32 * m, 32 * m + 32), R("ICT", 32 * m, 32 * m + 32), R("XC", m - 2, m - 1), ADD, R("XO", m, m + 1), ADD)
    for m in (0, 1):
        ts(R("XR", 32 * m, 32 * m + 32), R("ICT", 32 * m, 32 * m + 32), R("JB", 224 * m + 223, 224 * m + 224), ADD, R("XOB", m, m + 1), ADD)
    act(R("KC"), R("SM", 0, 8), AF.Identity, bias=Q16)
    act(R("NKC"), R("KC"), AF.Copy, scale=R("INI", 1, 2))
    ts(R("M8B"), R("N16", 0, 8), R("CC", 4, 5), EQL)
    turn(R("Y"), R("XR"))
    tt(R("VV"), R("Y"), R("pB", 0, 128), ADD)
    for c in (7, 6, 5, 4, 3, 2):
        act(R("AB", 128 * c, 144 * c + 16), R("VV", 0, 16 * c + 16), AF.Abs, bias=R("NKC", c, c + 1), scale=4096.0)
    for c in (0, 1):
        ts(R("AB", 128 * c, 144 * c + 16), R("VV", 0, 16 * c + 16), 4096.0, MUL, R("NKC", c, c + 1), ADD)
    for c in (0, 1, 7, 6, 5, 4, 3, 2):
        total_of(R("FS", c, c + 1), R("AB", 128 * c, 144 * c + 16), True, MIN)
    own = R("IL", 8 * rank, 8 * rank + 8)
    ts(own, R("FS"), float(base - 1), ADD)
    to_all(own, lambda r: own, "ai")
    for q, d, s in (("v", 0, 64), ("s", 0, 0), ("v", 64, 0), ("s", 64, 64)):
        plus(q, R("XS", 8 - s // 8, 16 - s // 8, d, d + 64), R("FS", 0, 8, s, s + 64), base - 1 + 4 * s)
    ts(R("ZU"), R("XS"), float(base + 2 * P - 1), MIN, float(-base), ADD)
    ts(R("NU"), R("XS", 8, 16), float(base + P - 1), MIN, float(-base), ADD)
    for h in range(2):
        pick_scales("Z", 128 * h, "LX1", 0, 2 * P, "ZU", 8 * h, 8 * h + 8, "vs"[h])
    for h in range(2):
        pick_codes("Z", 128 * h, "LX1", 0, 2 * P, "ZU", 8 * h, 8 * h + 8)
    for s, sem in (("s", "azs"), ("", "azc")):
        to_each(lambda r: R("Z" + s, HS * r, HS * r + HS), lambda r: R("HW" + s, HS * rank, HS * rank + HS), sem)
    pick("HW", HS * rank, "LX1", 0, 2 * P, "ZU", 2 * rank, 2 * rank + 2)

    for c, a in ((0, base + P), (8, base)):
        ts(R("AI", c, c + 8), R("XS", c, c + 8), float(-a), ADD, 3839.0, MIN)
    for c in (0, 8):
        act(R("D16", c, c + 8), R("KC"), AF.Identity, bias=float(P))
    ts(R("O4"), R("XS", 8, 12), float(base + P), LT)
    ts(R("HI"), R("AI"), 4, SHR)
    for c in (256, 320):
        fills(R("ROW", c, c + 64), 0.0)
    for b in range(2):
        copy("s", R("ET", 528 * b + 2 + b, 528 * b + 514, step=4), R("EYE"))
    plus("s", R("VR", p1=64), R("IRB", p1=64), 256)
    for a in (0, 64):
        plus("s", R("VR", a, a + 64, 64), R("IRB", 64 - a, 128 - a, 64), 256)
    fills(R("SC", 32, 36), TINY)
    act(R("RST"), R("N16"), AF.Sign)
    for a in (0, 64):
        plus("s", R("V384", a, a + 64), R("IRB", 64 - a, 128 - a), 384)
    plus("s", R("V128"), R("IRB", 0, 64), 128)
    copy("s", R("FR"), R("IRB"))
    act(R("R32B"), R("R32B"), AF.Sign)

    arrives([R("IL", 8 * r, 8 * r + 8) for r in peers], "ai")
    hp, hc = 64 if rank < N // 2 else 0, 2 * (rank % 4)
    ts(R("ILF"), R("IL"), 0.0, ADD)
    ts(R("A16"), R("AI"), 16.0, MUL)
    for c in range(2):
        total_of(R("G2", c, c + 1, hp, hp + 64), R("ILF", hc + c, 64, hp, hp + 64, 8), op=MIN)
    tt(R("I32"), R("ILF", 0, 32), R("ILF", 32, 64), MIN)
    for p in (0, 64):
        ts(R("GI", p0=p, p1=p + 64), R("G2", p0=hp, p1=hp + 64), 0.0, ADD)
    tt(R("I16"), R("I32", 0, 16), R("I32", 16, 32), MIN)
    ts(R("GJ"), R("GI"), 3, SHR, 0xE0, AND)
    tt(R("GF"), R("I16", 0, 8), R("I16", 8, 16), MIN)
    for c in range(2):
        ts(R("HU", c, c + 1), R("GJ", c, c + 1), R("KC", c, c + 1), ADD)
    tt(R("GM"), R("GF"), R("MH"), MUL)
    ts(R("H16"), R("HI"), -255.0, MUL)
    tt(R("G4"), R("GM", 0, 8, step=2), R("GM", 1, 8, step=2), ADD)
    tt(R("O5"), R("O4"), R("MH", 0, 4), MUL)
    mine = [(a, b) for a, b in ((0, HS * rank), (HS * rank + HS, N * HS)) if a < b]
    for s, sem in (("", "azc"), ("s", "azs")):
        arrives([R("HW" + s, a, b) for a, b in mine], sem, part)
    pick("WIN", HS * rank, "HW", 0, N * HS, "HU", 0, 2)
    for s, sem in (("s", "aws"), ("", "awc")):
        to_all(R("WIN" + s, HS * rank, HS * rank + HS), lambda r: R("WIN" + s, HS * rank, HS * rank + HS), sem)

    tt(R("PI16"), R("A16"), R("H16"), ADD)
    pick("NE", 0, "NQ", 0, P, "NU", 0, 8)
    tt(R("OFF"), R("PI16"), R("D16"), MIN)
    tt(R("O32"), R("O5", 0, 4, step=2), R("O5", 1, 4, step=2), ADD)
    for p in (0, 64):
        ts(R("OU", p0=p, p1=p + 64), R("OFF", 8 - p // 8, 16 - p // 8, p, p + 64), 0.0, ADD)
    for d, s in ((0, 64), (0, 0), (64, 0), (64, 64)):
        copy("s", R("GA", 4 - s // 16, 8 - s // 16, d, d + 64), R("G4", 0, 4, s, s + 64))
    for c in range(N):
        b = (c + 2) % 4 if c < 4 else c
        act(R("GB", 32 * b, 32 * b + 32), R("ONE", 0, 32), AF.Copy, scale=R("GA", c, c + 1))
    tt(R("GT8"), R("GA"), R("M4"), MUL)
    tt(R("OF8"), R("PI16", 0, 8), R("M8"), MUL)
    for k in range(2):
        act(R("JF", 4 * k, 4 * k + 4), R("GT8", 4 * k, 4 * k + 4), AF.Copy, acc=R("GC", k, k + 1))
    act(R("GOB"), R("ONE", 0, 32), AF.Copy, scale=R("GC", 1, 2))
    for b in range(4):
        if b == 3:
            turn(R("GR"), R("GB"))
        quant("EC", 128 * b, 128, "ET", 132 * (b % 2), 2 - b // 2 * 2)
        mm("pD", b, "EC", 128 * b, "NE", 0, 128, True, False)
    act(R("JF", 8, 16), R("OF8"), AF.Copy, acc=R("OFC"))
    act(R("SG"), R("GR", 0, 128), AF.Sign, bias=R("GC", 0, 1), scale=-1.0)
    copy("s", R("WD"), R("OFC"))
    act(R("MD"), R("SG"), AF.Copy, scale=0.5)
    for a in range(2):
        act(R("MO", 32 * a, 32 * a + 32), R("M32", 32 * a, 32 * a + 32), AF.Copy, scale=R("O32", a, a + 1))
    turn(R("GO"), R("GOB"))
    tt(R("G8"), R("GR", 128 + 8 * rank, 136 + 8 * rank), R("M8B"), MUL)
    act(R("JF", 16, 24), R("G8"), AF.Copy, acc=R("G1"))
    scatter(R("ROW"), R("OU"), R("VR"))

    for s, sem in (("", "awc"), ("s", "aws")):
        arrives([R("WIN" + s, a, b) for a, b in mine], sem)
    dmaq("y", "XW", P, "WIN", K, 192)
    dma("y", R("LST", 0, 16), R("ROW", 0, 256, 0, 8))
    for b in range(4):
        mm("pD", b, "EC", 128 * b, "WIN", 0, 128, False, True)
    mm("pA", 0, "UQ", 192, "WIN", K, 128)
    mm("pB", 0, "WIN", K, "UQ", 192, 128)
    ts(R("FC2"), R("GR", 192, 256), R("GC", 1, 2), GE, LESS, MAX)
    ts(R("G1I"), R("G1"), 0.0, ADD)
    ts(R("M16"), R("N16"), Q16, EQL)
    for b in range(4):
        copy("sv"[b % 2], R("HT", b, 256, step=4), R("pD", 512 * b, 512 * b + 64))
        if b == 1:
            ts(R("G1J"), R("G1I"), 5, SHR, 0x38, AND)
            ts(R("FT", 0, 32), R("GO"), R("GA", 4, 5), LE, LESS, MAX)
    quant("FW", 0, 128, "HT", 0)
    ts(R("H2U", 0, 1), R("G1J"), R("CC", 4, 5), ADD)
    ts(R("FT", 32, 64), R("GO"), R("GA", 5, 6), LE, LESS, MAX)
    quant("BN", 128, 128, "TW", 0)
    mm("pE", 0, "UQ", 0, "FW", 0, 128)
    mm("pC", 0, "UQ", 0, "WIN", 128, 128)
    act(R("RD"), R("pA", 0, 128), AF.Abs)
    act(R("OWN", 0, 1), R("pB", 0, 1), AF.Abs)
    mm("pB", 0, "WIN", 128, "UQ", 0, 128)
    act(R("D2"), R("RD"), AF.Sign, bias=R("OWN", 0, 1), scale=-1.0)
    tt(R("SM64"), R("MO"), R("pE", 0, 64), MUL)
    act(R("JF", 32, 64), R("SM64", 32, 64), AF.Abs, acc=R("SC", 4 * rank + 1, 4 * rank + 2))
    total_of(R("SC", 4 * rank, 4 * rank + 1), R("SM64", 0, 32), True)
    to_all(R("SC", 4 * rank, 4 * rank + 2), lambda r: R("SC", 4 * rank, 4 * rank + 2), "asc")
    for s, sem in (("", "anc"), ("s", "ans")):
        to_each(lambda r: R("FW" + s, 8 * r, 8 * r + 8), lambda r: R("HW2" + s, 8 * rank, 8 * rank + 8), sem)
    dmaq("y", "HW2", 8 * rank, "FW", 8 * rank, 8)

    def first_of(res, whats, fill):
        n = len(whats)
        scan(R("CN"), R("B2T", 0, 64), R("B2T", 64, 128), ADD)
        fill[0]()
        for i, what in enumerate(whats):
            ts(R("XB", 128 * i, 128 * i + 128), R("KB"), R("CN", 63, 64), EQL, what, MUL)
        fill[1]()
        turn(R("YB", 0, 128 * n), R("XB", 0, 128 * n))
        fill[2]()
        scan(R("SB2", 0, 128 * n), R("R32B", 0, 128 * n), R("YB", 0, 128 * n), MUL)
        fill[3]()
        tt(R("PC", 0, 4 * n, 0, 64), R("SB2", 31, 128 * n, 0, 64, 32), R("SB2", 31, 128 * n, 64, 128, 32), ADD)
        tt(R(res, 0, 4 * n, 0, 32), R("PC", 0, 4 * n, 0, 32), R("PC", 0, 4 * n, 32, 64), ADD)

    def offsets(lst, res, q):
        ts(R(lst, p0=32 * q, p1=32 * q + 32), R(res, 0, 4, 0, 32), 0.0, ADD)

    def nothing():
        return None

    tt(R("B2T"), R("D2"), R("MD"), LT)
    ts(R("O2", p1=64), R("D16", 0, 4, 0, 64), 0.0, ADD)
    act(R("CA"), R("pC", 64, 128), AF.Abs)
    act(R("OW2", p0=64), R("pB", 0, 1, 64, 128), AF.Abs)
    plus("s", R("CF"), R("CA"), TINY)
    plus("s", R("OWN", 1, 2, 64, 128), R("OW2", p0=64), TINY)
    first_of("RED", [R("PB"), R("WD")], [nothing, nothing, nothing, lambda: tt(R("RL", 64, 128), R("CF"), R("FC2"), MUL)])

    arrives([R("SC", 4 * r, 4 * r + 2) for r in peers], "asc")
    offsets("BU", "RED", 0)
    offsets("BU", "RED", 1)
    for a in range(2):
        total_of(R("S2", a, a + 1), R("SC", a, 36, step=4))
    for a in range(2):
        ts(R("SB", 32 * a, 32 * a + 32), R("FT", 32 * a, 32 * a + 32), R("S2", a, a + 1), MUL)
        copy("s", R("OWN", 1, 2, 32 * a, 32 * a + 32), R("S2", a, a + 1, 32 * a, 32 * a + 32))
    offsets("BU", "RED", 2)
    turn(R("RL", 0, 64), R("SB"))
    offsets("BU", "RED", 3)
    ts(R("B2T"), R("RL"), R("OWN", 1, 2), LT)
    tt(R("O3", p1=32), R("RED", 4, 8, 0, 32), R("D16", 0, 4, 0, 32), MIN)
    pick_scales("BN", K, "WIN", K, 128, "BU", 0, 4)
    gather(R("NUM", 0, 64), R("GR", 0, 128), R("BU"))
    dma("y", None, R("NUM", 0, 64, 0, 1), outap=T.sw[1:2, :])
    dmaq("y", "FW", K, "WIN", 192, K)
    dma("y", None, R("GR", 128, 192, 0, 1), outap=T.lw[0:1, :])
    dma("y", None, R("GR", 64, 128, 0, 1), outap=T.sw[0:1, :])
    for s, sem in (("", "anc"), ("s", "ans")):
        arrives([R("HW2" + s, 8 * r, 8 * r + 8) for r in peers], sem, part)

    def unpack():
        pick_codes("BN", K, "WIN", K, 128, "BU", 0, 4)
        for b in range(4):
            mm("pD", b, "EC", 128 * b, "BN", K, 128, True, False)

    def hand_on():
        pick("H2O", 0, "HW2", 0, K, "H2U", 0, 1)
        for s, sem in (("", "ahc"), ("s", "ahs")):
            to_all(R("H2O" + s, 0, 8), lambda r: R("XW" + s, 448 + 8 * rank, 456 + 8 * rank), sem)
        dmaq("y", "XW", 448 + 8 * rank, "H2O", 0, 8)
    first_of("RES", [R("PB")], [unpack, lambda: ts(R("O2", p0=64, p1=96), R("O3", p1=32), 0.0, ADD),
                                lambda: ts(R("O2", p0=96), R("O3", p1=32), 0.0, ADD), hand_on])
    for q in range(4):
        offsets("LU", "RES", q)

    pick("BN", 0, "NE", 0, 128, "LU", 0, 4)
    for b in range(4):
        mm("pD", b, "EC", 128 * b, "BN", 0, 128, False, True)
    gather(R("VA"), R("V384"), R("LU"))
    scatter(R("FR"), R("LU"), R("V128"))
    scatter(R("ROW"), R("O2"), R("VA"))
    dma("y", R("LST", 16, 32), R("ROW", 0, 256, 64, 72))
    tt(R("FM"), R("FR"), R("M16"), MUL)
    ts(R("PLU", 0, 16), R("LST", 0, 16), 0.0, ADD)
    scan(R("FS16"), R("RST"), R("FM"), MUL)
    for b in range(4):
        copy("sssv"[b], R("HT", b, 256, step=4), R("pD", 512 * b, 512 * b + 64))
    ts(R("FU"), R("FS16", 15, 128, step=16), 0.0, ADD)
    quant("FW", 128, 128, "HT", 0)
    gather(R("NUM", 64, 128), R("GR", 128, 256), R("LU"))
    dma("y", None, R("NUM", 64, 128, 0, 1), outap=T.lw[1:2, :])
    pick("LW", P, "FW", 0, 256, "FU", 0, 8)

    for h in range(2):
        pick("LX3", 128 * h, "LW", 0, 384, "PLU", 8 * h, 8 * h + 8)
        mm(("pA", "pB")[h], 0, "BN", 128, "LX3", 128 * h, 128)
        dma("y", None, R("LX3", 128 * h, 128 * h + 128), outap=T.oc[:, 512 * h:512 * h + 512])
    ts(R("PLU", 16, 32), R("LST", 16, 32), 0.0, ADD)
    for s, sem in (("", "ahc"), ("s", "ahs")):
        arrives([R("XW" + s, 448 + 8 * r, 456 + 8 * r) for r in peers], sem)
    copy("s", R("YO", 0, 128), R("pA", 0, 128))
    dma("y", None, R("YO", 0, 128), outap=T.y[:, 0:128])
    pick("LX3", P, "XW", 0, 512, "PLU", 16, 32)
    dma("y", None, R("LX3", P, 2 * P), outap=T.oc[:, 4 * P:8 * P])
    copy("v", R("YO", 128, 256), R("pB", 0, 128))
    dma("y", None, R("YO", 128, 256), outap=T.y[:, 128:256])
    for k in range(4):
        dma("sy"[k % 2], None, R("LX3s", 0, 2 * P, 32 * k, 32 * k + 4), outap=T.osc[4 * k:4 * k + 4, :])
    for sem in total:
        if known["g"].get(sem, 0) < total[sem]:
            g.wait_ge(T.sem[sem], total[sem])
